import numpy as np
import ml_dtypes


def mxq(x, axis, fmt="e4m3"):
    dtype, down = {"e4m3": (ml_dtypes.float8_e4m3fn, 7), "e5m2": (ml_dtypes.float8_e5m2, 14)}[fmt]
    v = np.moveaxis(np.asarray(x, np.float32).astype(ml_dtypes.bfloat16).astype(np.float64), axis, -1)
    blocks = v.reshape(v.shape[:-1] + (-1, 32))
    amax = np.abs(blocks).max(-1, keepdims=True)
    byte = np.maximum(np.where(amax > 0, np.frexp(amax)[1] - 1 + 127, 0) - down, 1)
    scale = np.exp2(byte - 127.0)
    codes = (blocks / scale).astype(np.float32).astype(dtype).astype(np.float64)
    return np.moveaxis((codes * scale).reshape(v.shape), -1, axis)


WIDE = False


def mx_kscale(k):
    if not WIDE:
        return np.ones(k)
    levels = np.array([10, -10, 5, -5, 0])
    if k % 512:
        return np.exp2(np.random.permutation(np.resize(levels, k // 32))).repeat(32)
    a = np.empty((k // 512, 16))
    for p in range(k // 512):
        a[p, :8] = np.random.permutation(np.resize(levels, 8))
        for g in range(8):
            far = levels[np.abs(levels - a[p, g]) >= 10]
            a[p, g + 8] = far[np.random.randint(len(far))]
    return np.exp2(a.ravel()).repeat(32)


def f64(x):
    return np.asarray(x).astype(np.float64)


def striped(idx):
    return np.tile(idx.reshape(-1, 16).T, (8, 1)).astype(np.uint16)


def unstriped(offs):
    return offs[:16].T.reshape(-1).astype(np.int64)


E2M1 = np.array([0.0, 0.5, 1.0, 1.5, 2.0, 3.0, 4.0, 6.0, -0.0, -0.5, -1.0, -1.5, -2.0, -3.0, -4.0, -6.0])


def pack_weight(w, fmt):
    k, n = w.shape
    w = f64(np.asarray(w, np.float32).astype(ml_dtypes.bfloat16)).reshape(k // 32, 32, n)
    amax = np.abs(w).max(1)
    if fmt == "e4m3":
        byte = np.frexp(amax)[1] - 1 + 127 - 7
    else:
        mant, ex = np.frexp(amax / 6.0)
        byte = np.where(mant > 0.5, ex, ex - 1) + 127
    byte = np.clip(np.where(amax > 0, byte, 1), 1, 254)
    scaled = (w * np.exp2(127.0 - byte)[:, None, :]).reshape(k, n).astype(np.float32)
    by_word = np.ascontiguousarray(scaled.reshape(k // 512, 128, 4, n).transpose(0, 1, 3, 2))
    if fmt == "e4m3":
        words = by_word.astype(ml_dtypes.float8_e4m3fn).view(np.uint8)
    else:
        c = by_word.astype(ml_dtypes.float4_e2m1fn).view(np.uint8) & 0xF
        words = (c[..., 0::2] | (c[..., 1::2] << 4)).reshape(k // 512, 128, 2 * n)
    return np.ascontiguousarray(words), np.ascontiguousarray(byte.astype(np.uint8).reshape(k // 512, 16, n))


def unpack_weight(words, scales, fmt):
    g, _, n = scales.shape
    words = np.ascontiguousarray(words).reshape(g, 128, n, -1)
    if fmt == "e4m3":
        vals = words.view(ml_dtypes.float8_e4m3fn).astype(np.float64)
    else:
        nib = np.empty((g, 128, n, 4), np.uint8)
        nib[..., 0::2] = words & 0xF
        nib[..., 1::2] = words >> 4
        vals = E2M1[nib]
    vals = vals * np.repeat(np.exp2(scales.astype(np.float64) - 127.0), 8, axis=1)[..., None]
    return vals.transpose(0, 1, 3, 2).reshape(g * 512, n)


def gelu(v):
    return 0.5 * v * (1.0 + np.tanh(np.sqrt(2.0 / np.pi) * (v + 0.044715 * v**3)))


K, T, K2, T2, S, P, H, N = 1536, 4096, 1024, 2048, 1024, 1024, 512, 384

def setup_inputs():
    n = np.random.standard_normal
    s = mx_kscale(K)[:, None]
    s2 = mx_kscale(K2)[:, None]
    u = mx_kscale(H)[:, None]
    tab_words, tab_scales = pack_weight(n((K, T)) * s, "e4m3")
    wr_words, wr_scales = pack_weight(n((K, H)) / np.sqrt(K) / s, "e2m1")
    fd = np.random.uniform(0.0, np.pi, (1, N))
    dop = np.cos(fd * np.arange(H)[:, None]) * np.sqrt(2.0 / H)
    return {
        "tab_words": tab_words, "tab_scales": tab_scales,
        "offs": striped(np.random.permutation(T)[:P]),
        "xs": (np.round(16 * n((K2, S))) / 16 * s2).astype(np.float32),
        "base": (n((K2, T2)) * s2).astype(np.float32),
        "offs2": striped(np.random.permutation(T2)[:S]),
        "offs3": striped(np.random.permutation(T2)[:P]),
        "we": (n((K2, H)) / np.sqrt(K2) / s2 * u.T).astype(np.float32),
        "wr_words": wr_words, "wr_scales": wr_scales,
        "dop": (dop / u).astype(np.float32),
        "noise": np.random.uniform(0.5, 1.5, N).astype(np.float32),
    }

def reference(tab_words, tab_scales, offs, xs, base, offs2, offs3, we, wr_words, wr_scales, dop, noise):
    v = unpack_weight(tab_words, tab_scales, "e4m3")[:, unstriped(offs)]
    wr = unpack_weight(wr_words, wr_scales, "e2m1")
    page = f64(base).copy()
    page[:, unstriped(offs2)] = f64(xs)
    a = mxq(f64(we), 0, "e4m3").T @ mxq(page, 0, "e4m3")
    cells = a[:, unstriped(offs3)]
    b = wr.T @ v
    h = cells * b
    y = mxq(f64(dop), 0, "e4m3").T @ mxq(h, 0, "e4m3")
    return np.log(y * y + f64(noise)[:, None])

@@ -1,0 +1,288 @@
+from contextlib import ExitStack
+
+import concourse.mybir as mybir
+
+K, T, K2, T2, S, PJ, H, N = 1536, 4096, 1024, 2048, 1024, 1024, 512, 384
+FLOPS = 2 * (K2 * H * T2 + K * H * PJ + H * N * PJ)
+
+F32 = mybir.dt.float32
+BF16 = mybir.dt.bfloat16
+I32 = mybir.dt.int32
+U32 = mybir.dt.uint32
+U16 = mybir.dt.uint16
+U8 = mybir.dt.uint8
+FP8X4 = mybir.dt.float8_e4m3fn_x4
+FP4X4 = mybir.dt.float4_e2m1fn_x4
+MULT = mybir.AluOpType.mult
+ACT = mybir.ActivationFunctionType
+
+P = 128
+KB = 1024
+CH = 512
+NCH = T2 // CH
+QJ = 256
+NQ = PJ // QJ
+UJ = 128
+
+
+def tile_list_passive_radar_doppler_kernel(
+    tc, tab_words, tab_scales, offs, xs, base, offs2, offs3, we, wr_words, wr_scales, dop, noise, out
+):
+    nc = tc.nc
+    with ExitStack() as ctx:
+        lists = ctx.enter_context(tc.tile_pool(name="lists", bufs=1))
+        arena = ctx.enter_context(tc.tile_pool(name="arena", bufs=1))
+        keep = ctx.enter_context(tc.tile_pool(name="keep", bufs=1))
+        ring = ctx.enter_context(tc.tile_pool(name="ring", bufs=2))
+        psum = ctx.enter_context(tc.psum_pool(name="psum", bufs=1))
+
+        def placed(shape, dtype, name, at):
+            return arena.tile(shape, dtype, name=name, offset=at, align_bytes=64)
+
+        def kept(shape, dtype, name):
+            return keep.tile(shape, dtype, name=name, align_bytes=64)
+
+        page_at = [8 * KB * i for i in range(8)]
+        xs_at = [64 * KB + 4 * KB * i for i in range(6)] + [90 * KB, 94 * KB]
+
+        idx = lists.tile([P, PJ // 16], U16, name="idx")
+        idx2 = lists.tile([P, S // 16], U16, name="idx2")
+        idx3 = lists.tile([P, PJ // 16], U16, name="idx3")
+
+        tab_sc = kept([P, T], U8, "tab_sc")
+        wr_sc_raw = kept([P, 3 * H], U8, "wr_sc_raw")
+        v_sc = [kept([P, PJ], U8, "v_sc%d" % a) for a in range(3)]
+        nc.gpsimd.memset(tab_sc[:].bitcast(I32), 0)
+        nc.gpsimd.memset(wr_sc_raw[:].bitcast(I32), 0)
+        for a in (1, 2):
+            nc.gpsimd.memset(v_sc[a][:].bitcast(I32), 0)
+
+        base_v = base.rearrange("(a p i) t -> a i p t", a=2, i=4)
+        xs_v = xs.rearrange("(a p i) t -> a i p t", a=2, i=4)
+        page = [placed([P, T2], F32, "page%d" % i, page_at[i]) for i in range(8)]
+        xt = [placed([P, S], F32, "xs%d" % i, xs_at[i]) for i in range(8)]
+        we_raw = [kept([P, 4, H], F32, "we_raw%d" % a) for a in range(2)]
+        dop_raw = kept([P, 4, N], F32, "dop_raw")
+        noise_t = kept([P, 3], F32, "noise_t")
+        wr_raw = kept([P, 3 * 2 * H], U8, "wr_raw")
+        dop_v = dop.rearrange("(g t q) n -> t g q n", t=4, q=8)
+
+        nc.sync.dma_start(idx2[:], offs2)
+        for i in range(8):
+            nc.sync.dma_start(page[i][:], base_v[i // 4, i % 4])
+            if i == 0:
+                for hf in range(2):
+                    cols = slice(hf * S // 2, (hf + 1) * S // 2)
+                    nc.sync.dma_start(xt[i][:, cols], xs_v[0, 0][:, cols])
+            else:
+                nc.sync.dma_start(xt[i][:], xs_v[i // 4, i % 4])
+            if i in (1, 2):
+                a = i - 1
+                nc.sync.dma_start(we_raw[a][:], we[512 * a : 512 * (a + 1), :].rearrange("(p j) c -> p j c", j=4))
+            if i == 3:
+                for t in range(4):
+                    nc.sync.dma_start(dop_raw[:, t, :], dop_v[t])
+        nc.sync.dma_start(idx[:], offs)
+        nc.sync.dma_start(idx3[:], offs3)
+        nc.sync.dma_start(noise_t[:], noise.rearrange("(p c) -> p c", c=3))
+        nc.sync.dma_start(
+            wr_raw[:].bitcast(I32).rearrange("p (a n) -> p a n", a=3), wr_words.bitcast(I32).rearrange("a p n -> p a n")
+        )
+        for q in range(4):
+            nc.sync.dma_start(
+                wr_sc_raw[32 * q : 32 * q + 4, :].bitcast(I32).rearrange("p (a n) -> p a n", a=3),
+                wr_scales[:, 4 * q : 4 * q + 4, :].bitcast(I32).rearrange("a r n -> r a n"),
+            )
+        for q in range(4):
+            nc.sync.dma_start(
+                tab_sc[32 * q : 32 * q + 12, :].bitcast(I32), tab_scales[:, 4 * q : 4 * q + 4, :].bitcast(I32)
+            )
+
+        we_il = kept([P, 2 * 4 * H], BF16, "we_il")
+        dop_il = kept([P, 4 * N], BF16, "dop_il")
+        pg_sc = [kept([P, T2], U8, "pg_sc%d" % a) for a in range(2)]
+        pg_codes = [[None] * NCH, [None] * NCH]
+        tab = [None] * 3
+        v_w = [None] * 3
+
+        def scatter(i):
+            if i == 0:
+                for hf in range(2):
+                    nc.vector.tensor_copy(
+                        page[i][:].indirect(idx2[:, 32 * hf : 32 * (hf + 1)]), xt[i][:, hf * S // 2 : (hf + 1) * S // 2]
+                    )
+            else:
+                nc.vector.tensor_copy(page[i][:].indirect(idx2[:]), xt[i][:])
+
+        def round_chunk(i, c, pairs):
+            nc.scalar.copy(pairs[c][:, (i % 4) // 2, :, i % 2], page[i][:, c * CH : (c + 1) * CH])
+
+        def weave_chunk(c, pairs):
+            il = keep.tile([P, 4 * CH], BF16, name="il%d" % c, align_bytes=64)
+            nc.scalar.copy(
+                il[:].bitcast(F32).rearrange("p (c u) -> p c u", u=2),
+                pairs[c][:].rearrange("p u c e -> p u (c e)").bitcast(F32).rearrange("p u c -> p c u"),
+            )
+            return il
+
+        def quantize_chunk(a, c, il):
+            at = (xs_at[4] if a == 0 else 0) + 2 * KB * c
+            pg_codes[a][c] = placed([P, CH], U32, "pg_codes%d_%d" % (a, c), at)
+            nc.vector.quantize_mx(pg_codes[a][c][:].bitcast(FP8X4), pg_sc[a][:, c * CH : (c + 1) * CH], il[:])
+
+        def load_table(a):
+            tab[a] = placed([P, T], I32, "tab%d" % a, 16 * KB * a)
+            nc.sync.dma_start(tab[a][:], tab_words[a].rearrange("p t i -> p (t i)").bitcast(I32))
+
+        def gather_table(a):
+            v_w[a] = placed([P, PJ], U32, "v_w0", xs_at[7]) if a == 0 else kept([P, PJ], U32, "v_w%d" % a)
+            nc.vector.tensor_copy(v_w[a][:], tab[a][:].bitcast(U32).indirect(idx[:]))
+
+        ils = [None, None]
+        for a in range(2):
+            pairs = [keep.tile([P, 2, CH, 2], BF16, name="pairs%d" % c, align_bytes=64) for c in range(NCH)]
+            for i in range(4 * a, 4 * a + 4):
+                scatter(i)
+                if i == 5:
+                    for c in range(NCH):
+                        quantize_chunk(0, c, ils[0][c])
+                if i == 6:
+                    we_codes = placed([P, 2 * H], U32, "we_codes", 88 * KB)
+                    we_sc = kept([P, 2 * H], U8, "we_sc")
+                    nc.vector.quantize_mx(we_codes[:].bitcast(FP8X4), we_sc[:], we_il[:])
+                    dop_codes = placed([P, N], U32, "dop_codes", 92 * KB)
+                    dop_sc = kept([P, N], U8, "dop_sc")
+                    for lo, hi in ((0, 256), (256, 384)):
+                        nc.vector.quantize_mx(
+                            dop_codes[:, lo:hi].bitcast(FP8X4), dop_sc[:, lo:hi], dop_il[:, 4 * lo : 4 * hi]
+                        )
+                if i % 4 < 3:
+                    for c in range(NCH):
+                        round_chunk(i, c, pairs)
+                else:
+                    ils[a] = []
+                    for c in range(NCH):
+                        round_chunk(i, c, pairs)
+                        ils[a].append(weave_chunk(c, pairs))
+                if i in (1, 2):
+                    b = i - 1
+                    nc.scalar.copy(
+                        we_il[:, 4 * H * b : 4 * H * (b + 1)].rearrange("p (t g q j) -> p t g q j", t=4, g=16, q=8),
+                        we_raw[b][:].rearrange("p j (g t q) -> p t g q j", t=4, q=8),
+                    )
+                if i == 4:
+                    nc.scalar.copy(
+                        dop_il[:].rearrange("p (c m t) -> p c m t", c=3, t=4),
+                        dop_raw[:].rearrange("p t (m c) -> p c m t", c=3),
+                    )
+                if i in (1, 3, 5):
+                    load_table(i // 2)
+
+        wr_w = kept([P, 3 * 2 * H], U8, "wr_w")
+        wr_sc = kept([P, 3 * H], U8, "wr_sc")
+        nc.vector.tensor_copy(
+            wr_w[:].bitcast(I32).rearrange("p (a t g w) -> p a t g w", a=3, t=4, g=16),
+            wr_raw[:].bitcast(I32).rearrange("p (a g t w) -> p a t g w", a=3, t=4, g=16),
+        )
+        nc.vector.tensor_copy(
+            wr_sc[:].bitcast(I32).rearrange("p (a t g w) -> p a t g w", a=3, t=4, g=16),
+            wr_sc_raw[:].bitcast(I32).rearrange("p (a g t w) -> p a t g w", a=3, t=4, g=16),
+        )
+        nc.vector.tensor_copy(v_sc[0][:], tab_sc[:].indirect(idx[:]))
+        for a in (1, 2):
+            nc.sync.dma_start(v_sc[a][0:112, :].bitcast(I32), v_sc[0][4 * a : 4 * a + 112, :].bitcast(I32))
+        gather_table(0)
+        for c in range(NCH):
+            quantize_chunk(1, c, ils[1][c])
+        gather_table(1)
+        gather_table(2)
+
+        a_at = [xs_at[0], xs_at[2], page_at[6], page_at[7]]
+        a_sb = []
+        for t in range(4):
+            a_t = placed([P, T2], F32, "a%d" % t, a_at[t])
+            a_sb.append(a_t)
+            for c in range(NCH):
+                bank = psum.tile([P, CH], F32, name="bank%d" % ((NCH * t + c) % 8))
+                for a in range(2):
+                    wc = slice(H * a + P * t, H * a + P * (t + 1))
+                    nc.tensor.matmul_mx(
+                        bank[:],
+                        lhsT=we_codes[:, wc].bitcast(FP8X4),
+                        lhsT_scale=we_sc[:, wc],
+                        rhs=pg_codes[a][c][:].bitcast(FP8X4),
+                        rhs_scale=pg_sc[a][:, c * CH : (c + 1) * CH],
+                        start=(a == 0),
+                        stop=(a == 1),
+                    )
+                nc.scalar.copy(a_t[:, c * CH : (c + 1) * CH], bank[:])
+
+        b_ps = []
+        for u in range(PJ // UJ):
+            js = slice(u * UJ, (u + 1) * UJ)
+            bank = psum.tile([P, 4 * UJ], F32, name="bank%d" % u)
+            b_ps.append(bank)
+            for t in range(4):
+                for a in range(3):
+                    c0 = H * a + P * t
+                    nc.tensor.matmul_mx(
+                        bank[:, t * UJ : (t + 1) * UJ],
+                        lhsT=wr_w[:, 2 * c0 : 2 * (c0 + P)].bitcast(FP4X4),
+                        lhsT_scale=wr_sc[:, c0 : c0 + P],
+                        rhs=v_w[a][:, js].bitcast(FP8X4),
+                        rhs_scale=v_sc[a][:, js],
+                        start=(a == 0),
+                        stop=(a == 2),
+                    )
+
+        out_v = out.rearrange("(p c) j -> p c j", c=3)
+
+        def gather_cells(lo, hi):
+            cells = placed([P, 4, hi - lo], F32, "cells%d" % lo, 32 * KB)
+            for t in range(4):
+                nc.vector.tensor_copy(cells[:, t, :], a_sb[t][:].indirect(idx3[:, lo // 16 : hi // 16]))
+            return cells
+
+        def multiply(cells, first, lo, hi):
+            h_il = keep.tile([P, 4 * (hi - lo)], BF16, name="h_il%d" % lo, align_bytes=64)
+            for j in range(lo, hi, UJ):
+                nc.vector.tensor_tensor(
+                    h_il[:, 4 * (j - lo) : 4 * (j - lo + UJ)].rearrange("p (c i t) -> p c t i", i=4, t=4),
+                    cells[:, :, j - first : j - first + UJ].rearrange("p t (c i) -> p c t i", i=4),
+                    b_ps[j // UJ][:].rearrange("p (t c i) -> p c t i", t=4, i=4),
+                    MULT,
+                )
+            return h_il
+
+        def finish(h_il, lo, hi):
+            w = hi - lo
+            h_codes = keep.tile([P, w], U32, name="h_codes%d" % lo, align_bytes=64)
+            h_sc = keep.tile([P, w], U8, name="h_sc%d" % lo, align_bytes=64)
+            nc.vector.quantize_mx(h_codes[:].bitcast(FP8X4), h_sc[:], h_il[:])
+            sq = ring.tile([P, 3, w], F32, name="sq")
+            res = ring.tile([P, 3, w], F32, name="res")
+            groups = ((0, 1), (2,)) if w > UJ else ((0, 1, 2),)
+            for n, group in enumerate(groups):
+                bank = psum.tile([P, len(group) * w], F32, name="bank%d" % (lo // UJ + n))
+                for k, c in enumerate(group):
+                    nc.tensor.matmul_mx(
+                        bank[:, k * w : (k + 1) * w],
+                        lhsT=dop_codes[:, c * P : (c + 1) * P].bitcast(FP8X4),
+                        lhsT_scale=dop_sc[:, c * P : (c + 1) * P],
+                        rhs=h_codes[:].bitcast(FP8X4),
+                        rhs_scale=h_sc[:],
+                        start=True,
+                        stop=True,
+                    )
+                nc.scalar.activation(
+                    sq[:, group[0] : group[-1] + 1, :].rearrange("p c j -> p (c j)"), bank[:], ACT.Square
+                )
+                for c in group:
+                    nc.scalar.activation(res[:, c, :], sq[:, c, :], ACT.Ln, bias=noise_t[:, c : c + 1])
+            nc.sync.dma_start(out_v[:, :, lo:hi], res[:])
+
+        for first, last, pieces in ((0, 512, 2), (512, 768, 1), (768, 1024, 2)):
+            cells = gather_cells(first, last)
+            w = (last - first) // pieces
+            for lo in range(first, last, w):
+                finish(multiply(cells, first, lo, lo + w), lo, lo + w)

@@ -52,10 +52,15 @@ def tile_list_passive_radar_doppler_kernel(
         tab_sc = kept([P, T], U8, "tab_sc")
         wr_sc_raw = kept([P, 3 * H], U8, "wr_sc_raw")
         v_sc = [kept([P, PJ], U8, "v_sc%d" % a) for a in range(3)]
-        nc.gpsimd.memset(tab_sc[:].bitcast(I32), 0)
+        nc.vector.memset(tab_sc[0:80, :].bitcast(I32), 0)
+        v_sc_rows = kept([P, PJ], U8, "v_sc_rows")
         nc.gpsimd.memset(wr_sc_raw[:].bitcast(I32), 0)
-        for a in (1, 2):
+        for a in range(3):
             nc.gpsimd.memset(v_sc[a][:].bitcast(I32), 0)
+
+        warm = kept([P, 2], F32, "warm")
+        nc.vector.memset(warm[:, 0:1], 1.0)
+        nc.scalar.activation(warm[:, 1:2], warm[:, 0:1], ACT.Ln)
 
         base_v = base.rearrange("(a p i) t -> a i p t", a=2, i=4)
         xs_v = xs.rearrange("(a p i) t -> a i p t", a=2, i=4)
@@ -67,10 +72,12 @@ def tile_list_passive_radar_doppler_kernel(
         wr_raw = kept([P, 3 * 2 * H], U8, "wr_raw")
         dop_v = dop.rearrange("(g t q) n -> t g q n", t=4, q=8)
 
-        nc.sync.dma_start(idx2[:], offs2)
+        nc.scalar.dma_start(tab_sc[80:128, :].bitcast(I32), tab_scales.rearrange("a q t -> (a q) t").bitcast(I32))
+        nc.sync.dma_start(idx[:], offs)
         for i in range(8):
             nc.sync.dma_start(page[i][:], base_v[i // 4, i % 4])
             if i == 0:
+                nc.sync.dma_start(idx2[:], offs2)
                 for hf in range(2):
                     cols = slice(hf * S // 2, (hf + 1) * S // 2)
                     nc.sync.dma_start(xt[i][:, cols], xs_v[0, 0][:, cols])
@@ -82,7 +89,6 @@ def tile_list_passive_radar_doppler_kernel(
             if i == 3:
                 for t in range(4):
                     nc.sync.dma_start(dop_raw[:, t, :], dop_v[t])
-        nc.sync.dma_start(idx[:], offs)
         nc.sync.dma_start(idx3[:], offs3)
         nc.sync.dma_start(noise_t[:], noise.rearrange("(p c) -> p c", c=3))
         nc.sync.dma_start(
@@ -93,10 +99,13 @@ def tile_list_passive_radar_doppler_kernel(
                 wr_sc_raw[32 * q : 32 * q + 4, :].bitcast(I32).rearrange("p (a n) -> p a n", a=3),
                 wr_scales[:, 4 * q : 4 * q + 4, :].bitcast(I32).rearrange("a r n -> r a n"),
             )
-        for q in range(4):
-            nc.sync.dma_start(
-                tab_sc[32 * q : 32 * q + 12, :].bitcast(I32), tab_scales[:, 4 * q : 4 * q + 4, :].bitcast(I32)
-            )
+        nc.vector.tensor_copy(v_sc_rows[:], tab_sc[:].indirect(idx[:]))
+        for a in range(3):
+            for q in range(4):
+                row = 80 + 16 * a + 4 * q
+                nc.scalar.dma_start(
+                    v_sc[a][32 * q : 32 * q + 4, :].bitcast(I32), v_sc_rows[row : row + 4, :].bitcast(I32)
+                )
 
         we_il = kept([P, 2 * 4 * H], BF16, "we_il")
         dop_il = kept([P, 4 * N], BF16, "dop_il")
@@ -115,7 +124,8 @@ def tile_list_passive_radar_doppler_kernel(
                 nc.vector.tensor_copy(page[i][:].indirect(idx2[:]), xt[i][:])
 
         def round_chunk(i, c, pairs):
-            nc.scalar.copy(pairs[c][:, (i % 4) // 2, :, i % 2], page[i][:, c * CH : (c + 1) * CH])
+            dst = pairs[c][:, (i % 4) // 2, :, i % 2] if i < 4 else pairs[c][:, :, i % 4]
+            nc.scalar.copy(dst, page[i][:, c * CH : (c + 1) * CH])
 
         def weave_chunk(c, pairs):
             il = keep.tile([P, 4 * CH], BF16, name="il%d" % c, align_bytes=64)
@@ -128,7 +138,7 @@ def tile_list_passive_radar_doppler_kernel(
         def quantize_chunk(a, c, il):
             at = (xs_at[4] if a == 0 else 0) + 2 * KB * c
             pg_codes[a][c] = placed([P, CH], U32, "pg_codes%d_%d" % (a, c), at)
-            nc.vector.quantize_mx(pg_codes[a][c][:].bitcast(FP8X4), pg_sc[a][:, c * CH : (c + 1) * CH], il[:])
+            nc.vector.quantize_mx(pg_codes[a][c][:].bitcast(FP8X4), pg_sc[a][:, c * CH : (c + 1) * CH], il)
 
         def load_table(a):
             tab[a] = placed([P, T], I32, "tab%d" % a, 16 * KB * a)
@@ -140,7 +150,7 @@ def tile_list_passive_radar_doppler_kernel(
 
         ils = [None, None]
         for a in range(2):
-            pairs = [keep.tile([P, 2, CH, 2], BF16, name="pairs%d" % c, align_bytes=64) for c in range(NCH)]
+            pairs = [keep.tile([P, 2, CH, 2] if a == 0 else [P, CH, 4], BF16, name="pairs%d" % c, align_bytes=64) for c in range(NCH)]
             for i in range(4 * a, 4 * a + 4):
                 scatter(i)
                 if i == 5:
@@ -163,7 +173,7 @@ def tile_list_passive_radar_doppler_kernel(
                     ils[a] = []
                     for c in range(NCH):
                         round_chunk(i, c, pairs)
-                        ils[a].append(weave_chunk(c, pairs))
+                        ils[a].append(weave_chunk(c, pairs)[:] if a == 0 else pairs[c][:].rearrange("p c i -> p (c i)"))
                 if i in (1, 2):
                     b = i - 1
                     nc.scalar.copy(
@@ -188,9 +198,6 @@ def tile_list_passive_radar_doppler_kernel(
             wr_sc[:].bitcast(I32).rearrange("p (a t g w) -> p a t g w", a=3, t=4, g=16),
             wr_sc_raw[:].bitcast(I32).rearrange("p (a g t w) -> p a t g w", a=3, t=4, g=16),
         )
-        nc.vector.tensor_copy(v_sc[0][:], tab_sc[:].indirect(idx[:]))
-        for a in (1, 2):
-            nc.sync.dma_start(v_sc[a][0:112, :].bitcast(I32), v_sc[0][4 * a : 4 * a + 112, :].bitcast(I32))
         gather_table(0)
         for c in range(NCH):
             quantize_chunk(1, c, ils[1][c])
@@ -237,22 +244,16 @@ def tile_list_passive_radar_doppler_kernel(
 
         out_v = out.rearrange("(p c) j -> p c j", c=3)
 
-        def gather_cells(lo, hi):
-            cells = placed([P, 4, hi - lo], F32, "cells%d" % lo, 32 * KB)
-            for t in range(4):
-                nc.vector.tensor_copy(cells[:, t, :], a_sb[t][:].indirect(idx3[:, lo // 16 : hi // 16]))
-            return cells
+        def gather_cells(cells, t, lo, hi):
+            nc.vector.tensor_copy(cells[:, t, :], a_sb[t][:].indirect(idx3[:, lo // 16 : hi // 16]))
 
-        def multiply(cells, first, lo, hi):
-            h_il = keep.tile([P, 4 * (hi - lo)], BF16, name="h_il%d" % lo, align_bytes=64)
-            for j in range(lo, hi, UJ):
-                nc.vector.tensor_tensor(
-                    h_il[:, 4 * (j - lo) : 4 * (j - lo + UJ)].rearrange("p (c i t) -> p c t i", i=4, t=4),
-                    cells[:, :, j - first : j - first + UJ].rearrange("p t (c i) -> p c t i", i=4),
-                    b_ps[j // UJ][:].rearrange("p (t c i) -> p c t i", t=4, i=4),
-                    MULT,
-                )
-            return h_il
+        def multiply(cells, first, h_il, lo, j):
+            nc.vector.tensor_tensor(
+                h_il[:, 4 * (j - lo) : 4 * (j - lo + UJ)].rearrange("p (c i t) -> p c t i", i=4, t=4),
+                cells[:, :, j - first : j - first + UJ].rearrange("p t (c i) -> p c t i", i=4),
+                b_ps[j // UJ][:].rearrange("p (t c i) -> p c t i", t=4, i=4),
+                MULT,
+            )
 
         def finish(h_il, lo, hi):
             w = hi - lo
@@ -260,7 +261,7 @@ def tile_list_passive_radar_doppler_kernel(
             h_sc = keep.tile([P, w], U8, name="h_sc%d" % lo, align_bytes=64)
             nc.vector.quantize_mx(h_codes[:].bitcast(FP8X4), h_sc[:], h_il[:])
             sq = ring.tile([P, 3, w], F32, name="sq")
-            res = ring.tile([P, 3, w], F32, name="res")
+            res = placed([P, 3, w], F32, "res%d" % lo, 16 * KB + 12 * lo)
             groups = ((0, 1), (2,)) if w > UJ else ((0, 1, 2),)
             for n, group in enumerate(groups):
                 bank = psum.tile([P, len(group) * w], F32, name="bank%d" % (lo // UJ + n))
@@ -279,10 +280,26 @@ def tile_list_passive_radar_doppler_kernel(
                 )
                 for c in group:
                     nc.scalar.activation(res[:, c, :], sq[:, c, :], ACT.Ln, bias=noise_t[:, c : c + 1])
-            nc.sync.dma_start(out_v[:, :, lo:hi], res[:])
+            (nc.scalar if hi == PJ else nc.sync).dma_start(out_v[:, :, lo:hi], res[:])
 
-        for first, last, pieces in ((0, 512, 2), (512, 768, 1), (768, 1024, 2)):
-            cells = gather_cells(first, last)
-            w = (last - first) // pieces
-            for lo in range(first, last, w):
-                finish(multiply(cells, first, lo, lo + w), lo, lo + w)
+        SPLIT = 3 * QJ
+        pieces = [(0, QJ), (QJ, 2 * QJ), (2 * QJ, SPLIT), (SPLIT, SPLIT + UJ), (SPLIT + UJ, PJ)]
+        h_ils = [keep.tile([P, 4 * (hi - lo)], BF16, name="h_il%d" % lo, align_bytes=64) for lo, hi in pieces]
+        cells = placed([P, 4, SPLIT], F32, "cells_head", 32 * KB)
+        for t in range(4):
+            gather_cells(cells, t, 0, SPLIT)
+        for n in range(3):
+            lo, hi = pieces[n]
+            multiply(cells, 0, h_ils[n], lo, lo)
+            if n > 0:
+                finish(h_ils[n - 1], *pieces[n - 1])
+            multiply(cells, 0, h_ils[n], lo, lo + UJ)
+        cells = placed([P, 4, PJ - SPLIT], F32, "cells_tail", 32 * KB)
+        for t in range(4):
+            gather_cells(cells, t, SPLIT, PJ)
+            if t == 0:
+                finish(h_ils[2], *pieces[2])
+        for n in (3, 4):
+            lo, hi = pieces[n]
+            multiply(cells, SPLIT, h_ils[n], lo, lo)
+            finish(h_ils[n], lo, hi)

@@ -52,10 +52,9 @@ def tile_list_passive_radar_doppler_kernel(
         tab_sc = kept([P, T], U8, "tab_sc")
         wr_sc_raw = kept([P, 3 * H], U8, "wr_sc_raw")
         v_sc = [kept([P, PJ], U8, "v_sc%d" % a) for a in range(3)]
-        nc.vector.memset(tab_sc[0:80, :].bitcast(I32), 0)
-        v_sc_rows = kept([P, PJ], U8, "v_sc_rows")
+        nc.gpsimd.memset(tab_sc[:].bitcast(I32), 0)
         nc.gpsimd.memset(wr_sc_raw[:].bitcast(I32), 0)
-        for a in range(3):
+        for a in (1, 2):
             nc.gpsimd.memset(v_sc[a][:].bitcast(I32), 0)
 
         warm = kept([P, 2], F32, "warm")
@@ -72,8 +71,6 @@ def tile_list_passive_radar_doppler_kernel(
         wr_raw = kept([P, 3 * 2 * H], U8, "wr_raw")
         dop_v = dop.rearrange("(g t q) n -> t g q n", t=4, q=8)
 
-        nc.scalar.dma_start(tab_sc[80:128, :].bitcast(I32), tab_scales.rearrange("a q t -> (a q) t").bitcast(I32))
-        nc.sync.dma_start(idx[:], offs)
         for i in range(8):
             nc.sync.dma_start(page[i][:], base_v[i // 4, i % 4])
             if i == 0:
@@ -89,6 +86,7 @@ def tile_list_passive_radar_doppler_kernel(
             if i == 3:
                 for t in range(4):
                     nc.sync.dma_start(dop_raw[:, t, :], dop_v[t])
+        nc.sync.dma_start(idx[:], offs)
         nc.sync.dma_start(idx3[:], offs3)
         nc.sync.dma_start(noise_t[:], noise.rearrange("(p c) -> p c", c=3))
         nc.sync.dma_start(
@@ -99,13 +97,10 @@ def tile_list_passive_radar_doppler_kernel(
                 wr_sc_raw[32 * q : 32 * q + 4, :].bitcast(I32).rearrange("p (a n) -> p a n", a=3),
                 wr_scales[:, 4 * q : 4 * q + 4, :].bitcast(I32).rearrange("a r n -> r a n"),
             )
-        nc.vector.tensor_copy(v_sc_rows[:], tab_sc[:].indirect(idx[:]))
-        for a in range(3):
-            for q in range(4):
-                row = 80 + 16 * a + 4 * q
-                nc.scalar.dma_start(
-                    v_sc[a][32 * q : 32 * q + 4, :].bitcast(I32), v_sc_rows[row : row + 4, :].bitcast(I32)
-                )
+        for q in range(4):
+            nc.sync.dma_start(
+                tab_sc[32 * q : 32 * q + 12, :].bitcast(I32), tab_scales[:, 4 * q : 4 * q + 4, :].bitcast(I32)
+            )
 
         we_il = kept([P, 2 * 4 * H], BF16, "we_il")
         dop_il = kept([P, 4 * N], BF16, "dop_il")
@@ -124,8 +119,7 @@ def tile_list_passive_radar_doppler_kernel(
                 nc.vector.tensor_copy(page[i][:].indirect(idx2[:]), xt[i][:])
 
         def round_chunk(i, c, pairs):
-            dst = pairs[c][:, (i % 4) // 2, :, i % 2] if i < 4 else pairs[c][:, :, i % 4]
-            nc.scalar.copy(dst, page[i][:, c * CH : (c + 1) * CH])
+            nc.scalar.copy(pairs[c][:, (i % 4) // 2, :, i % 2], page[i][:, c * CH : (c + 1) * CH])
 
         def weave_chunk(c, pairs):
             il = keep.tile([P, 4 * CH], BF16, name="il%d" % c, align_bytes=64)
@@ -138,7 +132,7 @@ def tile_list_passive_radar_doppler_kernel(
         def quantize_chunk(a, c, il):
             at = (xs_at[4] if a == 0 else 0) + 2 * KB * c
             pg_codes[a][c] = placed([P, CH], U32, "pg_codes%d_%d" % (a, c), at)
-            nc.vector.quantize_mx(pg_codes[a][c][:].bitcast(FP8X4), pg_sc[a][:, c * CH : (c + 1) * CH], il)
+            nc.vector.quantize_mx(pg_codes[a][c][:].bitcast(FP8X4), pg_sc[a][:, c * CH : (c + 1) * CH], il[:])
 
         def load_table(a):
             tab[a] = placed([P, T], I32, "tab%d" % a, 16 * KB * a)
@@ -150,7 +144,7 @@ def tile_list_passive_radar_doppler_kernel(
 
         ils = [None, None]
         for a in range(2):
-            pairs = [keep.tile([P, 2, CH, 2] if a == 0 else [P, CH, 4], BF16, name="pairs%d" % c, align_bytes=64) for c in range(NCH)]
+            pairs = [keep.tile([P, 2, CH, 2], BF16, name="pairs%d" % c, align_bytes=64) for c in range(NCH)]
             for i in range(4 * a, 4 * a + 4):
                 scatter(i)
                 if i == 5:
@@ -173,7 +167,7 @@ def tile_list_passive_radar_doppler_kernel(
                     ils[a] = []
                     for c in range(NCH):
                         round_chunk(i, c, pairs)
-                        ils[a].append(weave_chunk(c, pairs)[:] if a == 0 else pairs[c][:].rearrange("p c i -> p (c i)"))
+                        ils[a].append(weave_chunk(c, pairs))
                 if i in (1, 2):
                     b = i - 1
                     nc.scalar.copy(
@@ -198,6 +192,9 @@ def tile_list_passive_radar_doppler_kernel(
             wr_sc[:].bitcast(I32).rearrange("p (a t g w) -> p a t g w", a=3, t=4, g=16),
             wr_sc_raw[:].bitcast(I32).rearrange("p (a g t w) -> p a t g w", a=3, t=4, g=16),
         )
+        nc.vector.tensor_copy(v_sc[0][:], tab_sc[:].indirect(idx[:]))
+        for a in (1, 2):
+            nc.sync.dma_start(v_sc[a][0:112, :].bitcast(I32), v_sc[0][4 * a : 4 * a + 112, :].bitcast(I32))
         gather_table(0)
         for c in range(NCH):
             quantize_chunk(1, c, ils[1][c])
@@ -249,9 +246,9 @@ def tile_list_passive_radar_doppler_kernel(
 
         def multiply(cells, first, h_il, lo, j):
             nc.vector.tensor_tensor(
-                h_il[:, 4 * (j - lo) : 4 * (j - lo + UJ)].rearrange("p (c i t) -> p c t i", i=4, t=4),
-                cells[:, :, j - first : j - first + UJ].rearrange("p t (c i) -> p c t i", i=4),
-                b_ps[j // UJ][:].rearrange("p (t c i) -> p c t i", t=4, i=4),
+                h_il[:, 4 * (j - lo) : 4 * (j - lo + UJ)].rearrange("p (c i t) -> p c t i", i=2, t=4),
+                cells[:, :, j - first : j - first + UJ].rearrange("p t (c i) -> p c t i", i=2),
+                b_ps[j // UJ][:].rearrange("p (t c i) -> p c t i", t=4, i=2),
                 MULT,
             )
 

@@ -2,8 +2,8 @@ from contextlib import ExitStack
 
 import concourse.mybir as mybir
 
-K, T, K2, T2, S, PJ, H, N = 1536, 4096, 1024, 2048, 1024, 1024, 512, 384
-FLOPS = 2 * (K2 * H * T2 + K * H * PJ + H * N * PJ)
+K, T, K2, T2, S, J, H, N = 1536, 4096, 1024, 2048, 1024, 1024, 512, 384
+FLOPS = 2 * (K2 * H * T2 + K * H * J + H * N * J)
 
 F32 = mybir.dt.float32
 BF16 = mybir.dt.bfloat16
@@ -13,16 +13,38 @@ U16 = mybir.dt.uint16
 U8 = mybir.dt.uint8
 FP8X4 = mybir.dt.float8_e4m3fn_x4
 FP4X4 = mybir.dt.float4_e2m1fn_x4
-MULT = mybir.AluOpType.mult
 ACT = mybir.ActivationFunctionType
 
 P = 128
+SLOTS = 4
+PASS = P * SLOTS
+M_PASSES = K2 // PASS
+K_PASSES = K // PASS
+PLANES = M_PASSES * SLOTS
+N_SLICES = N // P
+BANKS = 8
+CHUNK = 512
+CHUNKS = T2 // CHUNK
+UNIT = 128
+PER_COLUMN = 16
+SCALE_ROWS = 16
+SCALE_ROW0 = 48
+
+SPLIT = 6 * UNIT
+PIECES = [(0, 256), (256, 512), (512, SPLIT), (SPLIT, SPLIT + UNIT), (SPLIT + UNIT, J)]
+
 KB = 1024
-CH = 512
-NCH = T2 // CH
-QJ = 256
-NQ = PJ // QJ
-UJ = 128
+PAGE_AT = [8 * KB * i for i in range(PLANES)]
+XS_AT = [64 * KB + 4 * KB * i for i in range(PLANES)]
+TABLE_AT = [16 * KB * a for a in range(K_PASSES)]
+PAGE_CODES_FIRST_AT = XS_AT[-1] - 7 * KB
+DOP_CODES_AT = XS_AT[-1] + KB
+WE_CODES_AT = XS_AT[-1] + 3 * KB
+PAGE_CODES_SECOND_AT = TABLE_AT[0]
+PICKED_FIRST_AT = XS_AT[4]
+A_AT = [XS_AT[0], XS_AT[2], PAGE_AT[6], PAGE_AT[7]]
+CELLS_AT = TABLE_AT[2]
+RESULT_AT = TABLE_AT[1]
 
 
 def tile_list_passive_radar_doppler_kernel(
@@ -42,229 +64,230 @@ def tile_list_passive_radar_doppler_kernel(
         def kept(shape, dtype, name):
             return keep.tile(shape, dtype, name=name, align_bytes=64)
 
-        page_at = [8 * KB * i for i in range(8)]
-        xs_at = [64 * KB + 4 * KB * i for i in range(6)] + [90 * KB, 94 * KB]
+        def bank_tile(columns, bank):
+            return psum.tile([P, columns], F32, name="bank%d" % bank)
 
-        idx = lists.tile([P, PJ // 16], U16, name="idx")
-        idx2 = lists.tile([P, S // 16], U16, name="idx2")
-        idx3 = lists.tile([P, PJ // 16], U16, name="idx3")
+        idx = lists.tile([P, J // PER_COLUMN], U16, name="idx")
+        idx2 = lists.tile([P, S // PER_COLUMN], U16, name="idx2")
+        idx3 = lists.tile([P, J // PER_COLUMN], U16, name="idx3")
 
+        scale_end = SCALE_ROW0 + K_PASSES * SCALE_ROWS
         tab_sc = kept([P, T], U8, "tab_sc")
-        wr_sc_raw = kept([P, 3 * H], U8, "wr_sc_raw")
-        v_sc = [kept([P, PJ], U8, "v_sc%d" % a) for a in range(3)]
-        nc.gpsimd.memset(tab_sc[:].bitcast(I32), 0)
+        wr_sc_raw = kept([P, K_PASSES * H], U8, "wr_sc_raw")
+        v_sc = [kept([P, J], U8, "v_sc%d" % a) for a in range(K_PASSES)]
+        v_sc_rows = kept([P, J], U8, "v_sc_rows")
+        nc.vector.memset(tab_sc[0:SCALE_ROW0, :].bitcast(I32), 0)
+        nc.vector.memset(tab_sc[scale_end:P, :].bitcast(I32), 0)
         nc.gpsimd.memset(wr_sc_raw[:].bitcast(I32), 0)
-        for a in (1, 2):
+        for a in range(K_PASSES):
             nc.gpsimd.memset(v_sc[a][:].bitcast(I32), 0)
 
-        warm = kept([P, 2], F32, "warm")
-        nc.vector.memset(warm[:, 0:1], 1.0)
-        nc.scalar.activation(warm[:, 1:2], warm[:, 0:1], ACT.Ln)
+        sc_rows = tab_scales.rearrange("a q t -> (a q) t").bitcast(I32)
+        nc.sync.dma_start(idx[:], offs)
+        nc.sync.dma_start(tab_sc[SCALE_ROW0 : SCALE_ROW0 + SCALE_ROWS, :].bitcast(I32), sc_rows[0:SCALE_ROWS, :])
+        nc.sync.dma_start(tab_sc[SCALE_ROW0 + SCALE_ROWS : scale_end, :].bitcast(I32), sc_rows[SCALE_ROWS:, :])
+        nc.vector.tensor_copy(v_sc_rows[:], tab_sc[:].indirect(idx[:]))
 
-        base_v = base.rearrange("(a p i) t -> a i p t", a=2, i=4)
-        xs_v = xs.rearrange("(a p i) t -> a i p t", a=2, i=4)
-        page = [placed([P, T2], F32, "page%d" % i, page_at[i]) for i in range(8)]
-        xt = [placed([P, S], F32, "xs%d" % i, xs_at[i]) for i in range(8)]
-        we_raw = [kept([P, 4, H], F32, "we_raw%d" % a) for a in range(2)]
-        dop_raw = kept([P, 4, N], F32, "dop_raw")
-        noise_t = kept([P, 3], F32, "noise_t")
-        wr_raw = kept([P, 3 * 2 * H], U8, "wr_raw")
-        dop_v = dop.rearrange("(g t q) n -> t g q n", t=4, q=8)
-
-        for i in range(8):
-            nc.sync.dma_start(page[i][:], base_v[i // 4, i % 4])
+        base_planes = base.rearrange("(a p i) t -> a i p t", a=M_PASSES, i=SLOTS)
+        xs_planes = xs.rearrange("(a p i) t -> a i p t", a=M_PASSES, i=SLOTS)
+        dop_slots = dop.rearrange("(g t q) n -> t g q n", t=SLOTS, q=8)
+        page = [placed([P, T2], F32, "page%d" % i, PAGE_AT[i]) for i in range(PLANES)]
+        xs_sb = [placed([P, S], F32, "xs%d" % i, XS_AT[i]) for i in range(PLANES)]
+        we_raw = [kept([P, SLOTS, H], F32, "we_raw%d" % a) for a in range(M_PASSES)]
+        dop_raw = kept([P, SLOTS, N], F32, "dop_raw")
+        noise_sb = kept([P, N_SLICES], F32, "noise_sb")
+        wr_raw = kept([P, K_PASSES * 2 * H], U8, "wr_raw")
+        parts = [[(0, S // 2), (S // 2, S)] if i == 0 else [(0, S)] for i in range(PLANES)]
+        we_after_plane = {1: 0, 2: 1}
+        dop_load_after, dop_round_after = 3, 4
+        for i in range(PLANES):
+            nc.sync.dma_start(page[i][:], base_planes[i // SLOTS, i % SLOTS])
             if i == 0:
                 nc.sync.dma_start(idx2[:], offs2)
-                for hf in range(2):
-                    cols = slice(hf * S // 2, (hf + 1) * S // 2)
-                    nc.sync.dma_start(xt[i][:, cols], xs_v[0, 0][:, cols])
-            else:
-                nc.sync.dma_start(xt[i][:], xs_v[i // 4, i % 4])
-            if i in (1, 2):
-                a = i - 1
-                nc.sync.dma_start(we_raw[a][:], we[512 * a : 512 * (a + 1), :].rearrange("(p j) c -> p j c", j=4))
-            if i == 3:
-                for t in range(4):
-                    nc.sync.dma_start(dop_raw[:, t, :], dop_v[t])
-        nc.sync.dma_start(idx[:], offs)
+            for lo, hi in parts[i]:
+                nc.sync.dma_start(xs_sb[i][:, lo:hi], xs_planes[i // SLOTS, i % SLOTS][:, lo:hi])
+            if i in we_after_plane:
+                a = we_after_plane[i]
+                rows = we[PASS * a : PASS * (a + 1), :]
+                nc.sync.dma_start(we_raw[a][:], rows.rearrange("(p j) c -> p j c", j=SLOTS))
+            if i == dop_load_after:
+                for t in range(SLOTS):
+                    nc.sync.dma_start(dop_raw[:, t, :], dop_slots[t])
         nc.sync.dma_start(idx3[:], offs3)
-        nc.sync.dma_start(noise_t[:], noise.rearrange("(p c) -> p c", c=3))
+        nc.sync.dma_start(noise_sb[:], noise.rearrange("(p c) -> p c", c=N_SLICES))
         nc.sync.dma_start(
-            wr_raw[:].bitcast(I32).rearrange("p (a n) -> p a n", a=3), wr_words.bitcast(I32).rearrange("a p n -> p a n")
+            wr_raw[:].bitcast(I32).rearrange("p (a n) -> p a n", a=K_PASSES),
+            wr_words.bitcast(I32).rearrange("a p n -> p a n"),
         )
         for q in range(4):
             nc.sync.dma_start(
-                wr_sc_raw[32 * q : 32 * q + 4, :].bitcast(I32).rearrange("p (a n) -> p a n", a=3),
+                wr_sc_raw[32 * q : 32 * q + 4, :].bitcast(I32).rearrange("p (a n) -> p a n", a=K_PASSES),
                 wr_scales[:, 4 * q : 4 * q + 4, :].bitcast(I32).rearrange("a r n -> r a n"),
             )
-        for q in range(4):
-            nc.sync.dma_start(
-                tab_sc[32 * q : 32 * q + 12, :].bitcast(I32), tab_scales[:, 4 * q : 4 * q + 4, :].bitcast(I32)
-            )
+        for a in range(K_PASSES):
+            for q in range(4):
+                row = SCALE_ROW0 + SCALE_ROWS * a + 4 * q
+                nc.sync.dma_start(
+                    v_sc[a][32 * q : 32 * q + 4, :].bitcast(I32), v_sc_rows[row : row + 4, :].bitcast(I32)
+                )
 
-        we_il = kept([P, 2 * 4 * H], BF16, "we_il")
-        dop_il = kept([P, 4 * N], BF16, "dop_il")
-        pg_sc = [kept([P, T2], U8, "pg_sc%d" % a) for a in range(2)]
-        pg_codes = [[None] * NCH, [None] * NCH]
-        tab = [None] * 3
-        v_w = [None] * 3
-
-        def scatter(i):
-            if i == 0:
-                for hf in range(2):
-                    nc.vector.tensor_copy(
-                        page[i][:].indirect(idx2[:, 32 * hf : 32 * (hf + 1)]), xt[i][:, hf * S // 2 : (hf + 1) * S // 2]
-                    )
-            else:
-                nc.vector.tensor_copy(page[i][:].indirect(idx2[:]), xt[i][:])
+        we_woven = kept([P, M_PASSES * SLOTS * H], BF16, "we_woven")
+        dop_woven = kept([P, SLOTS * N], BF16, "dop_woven")
+        page_sc = [kept([P, T2], U8, "page_sc%d" % a) for a in range(M_PASSES)]
+        page_codes = []
+        page_woven = []
+        table = []
+        v_words = []
 
         def round_chunk(i, c, pairs):
-            nc.scalar.copy(pairs[c][:, (i % 4) // 2, :, i % 2], page[i][:, c * CH : (c + 1) * CH])
+            nc.scalar.copy(pairs[c][:, (i % SLOTS) // 2, :, i % 2], page[i][:, c * CHUNK : (c + 1) * CHUNK])
 
-        def weave_chunk(c, pairs):
-            il = keep.tile([P, 4 * CH], BF16, name="il%d" % c, align_bytes=64)
+        def weave_chunk(c, pairs, woven):
+            half = woven[c // 2][:].bitcast(F32)[:, (c % 2) * 2 * CHUNK : (c % 2 + 1) * 2 * CHUNK]
             nc.scalar.copy(
-                il[:].bitcast(F32).rearrange("p (c u) -> p c u", u=2),
+                half.rearrange("p (c u) -> p c u", u=2),
                 pairs[c][:].rearrange("p u c e -> p u (c e)").bitcast(F32).rearrange("p u c -> p c u"),
             )
-            return il
 
-        def quantize_chunk(a, c, il):
-            at = (xs_at[4] if a == 0 else 0) + 2 * KB * c
-            pg_codes[a][c] = placed([P, CH], U32, "pg_codes%d_%d" % (a, c), at)
-            nc.vector.quantize_mx(pg_codes[a][c][:].bitcast(FP8X4), pg_sc[a][:, c * CH : (c + 1) * CH], il[:])
-
-        def load_table(a):
-            tab[a] = placed([P, T], I32, "tab%d" % a, 16 * KB * a)
-            nc.sync.dma_start(tab[a][:], tab_words[a].rearrange("p t i -> p (t i)").bitcast(I32))
+        def quantize_page(a, at):
+            codes = placed([P, T2], U32, "page_codes%d" % a, at)
+            page_codes.append(codes)
+            for half in range(2):
+                cols = slice(half * T2 // 2, (half + 1) * T2 // 2)
+                nc.vector.quantize_mx(codes[:, cols].bitcast(FP8X4), page_sc[a][:, cols], page_woven[a][half][:])
 
         def gather_table(a):
-            v_w[a] = placed([P, PJ], U32, "v_w0", xs_at[7]) if a == 0 else kept([P, PJ], U32, "v_w%d" % a)
-            nc.vector.tensor_copy(v_w[a][:], tab[a][:].bitcast(U32).indirect(idx[:]))
+            if a == 0:
+                words = placed([P, J], U32, "v_words0", PICKED_FIRST_AT)
+            else:
+                words = kept([P, J], U32, "v_words%d" % a)
+            v_words.append(words)
+            nc.vector.tensor_copy(words[:], table[a][:].bitcast(U32).indirect(idx[:]))
 
-        ils = [None, None]
-        for a in range(2):
-            pairs = [keep.tile([P, 2, CH, 2], BF16, name="pairs%d" % c, align_bytes=64) for c in range(NCH)]
-            for i in range(4 * a, 4 * a + 4):
-                scatter(i)
-                if i == 5:
-                    for c in range(NCH):
-                        quantize_chunk(0, c, ils[0][c])
-                if i == 6:
-                    we_codes = placed([P, 2 * H], U32, "we_codes", 88 * KB)
-                    we_sc = kept([P, 2 * H], U8, "we_sc")
-                    nc.vector.quantize_mx(we_codes[:].bitcast(FP8X4), we_sc[:], we_il[:])
-                    dop_codes = placed([P, N], U32, "dop_codes", 92 * KB)
+        for a in range(M_PASSES):
+            pairs = [kept([P, 2, CHUNK, 2], BF16, "pairs%d" % c) for c in range(CHUNKS)]
+            for i in range(SLOTS * a, SLOTS * (a + 1)):
+                for lo, hi in parts[i]:
+                    window = page[i][:].indirect(idx2[:, lo // PER_COLUMN : hi // PER_COLUMN])
+                    nc.vector.tensor_copy(window, xs_sb[i][:, lo:hi])
+                if i == PLANES - 1:
+                    quantize_page(0, PAGE_CODES_FIRST_AT)
+                    we_codes = placed([P, M_PASSES * H], U32, "we_codes", WE_CODES_AT)
+                    we_sc = kept([P, M_PASSES * H], U8, "we_sc")
+                    nc.vector.quantize_mx(we_codes[:].bitcast(FP8X4), we_sc[:], we_woven[:])
+                    dop_codes = placed([P, N], U32, "dop_codes", DOP_CODES_AT)
                     dop_sc = kept([P, N], U8, "dop_sc")
-                    for lo, hi in ((0, 256), (256, 384)):
+                    for lo, hi in ((0, 2 * P), (2 * P, N)):
                         nc.vector.quantize_mx(
-                            dop_codes[:, lo:hi].bitcast(FP8X4), dop_sc[:, lo:hi], dop_il[:, 4 * lo : 4 * hi]
+                            dop_codes[:, lo:hi].bitcast(FP8X4), dop_sc[:, lo:hi], dop_woven[:, SLOTS * lo : SLOTS * hi]
                         )
-                if i % 4 < 3:
-                    for c in range(NCH):
+                if i % SLOTS < SLOTS - 1:
+                    for c in range(CHUNKS):
                         round_chunk(i, c, pairs)
                 else:
-                    ils[a] = []
-                    for c in range(NCH):
+                    page_woven.append([kept([P, SLOTS * T2 // 2], BF16, "page_woven%d" % half) for half in range(2)])
+                    for c in range(CHUNKS):
                         round_chunk(i, c, pairs)
-                        ils[a].append(weave_chunk(c, pairs))
-                if i in (1, 2):
-                    b = i - 1
+                        weave_chunk(c, pairs, page_woven[a])
+                if i in we_after_plane:
+                    b = we_after_plane[i]
                     nc.scalar.copy(
-                        we_il[:, 4 * H * b : 4 * H * (b + 1)].rearrange("p (t g q j) -> p t g q j", t=4, g=16, q=8),
-                        we_raw[b][:].rearrange("p j (g t q) -> p t g q j", t=4, q=8),
+                        we_woven[:, SLOTS * H * b : SLOTS * H * (b + 1)].rearrange(
+                            "p (t g q j) -> p t g q j", t=SLOTS, g=16, q=8
+                        ),
+                        we_raw[b][:].rearrange("p j (g t q) -> p t g q j", t=SLOTS, q=8),
                     )
-                if i == 4:
+                if i == dop_round_after:
                     nc.scalar.copy(
-                        dop_il[:].rearrange("p (c m t) -> p c m t", c=3, t=4),
-                        dop_raw[:].rearrange("p t (m c) -> p c m t", c=3),
+                        dop_woven[:].rearrange("p (c m t) -> p c m t", c=N_SLICES, t=SLOTS),
+                        dop_raw[:].rearrange("p t (m c) -> p c m t", c=N_SLICES),
                     )
-                if i in (1, 3, 5):
-                    load_table(i // 2)
+                if i % 2 == 1 and i // 2 < K_PASSES:
+                    words = placed([P, T], I32, "table%d" % (i // 2), TABLE_AT[i // 2])
+                    table.append(words)
+                    nc.sync.dma_start(words[:], tab_words[i // 2].rearrange("p t i -> p (t i)").bitcast(I32))
 
-        wr_w = kept([P, 3 * 2 * H], U8, "wr_w")
-        wr_sc = kept([P, 3 * H], U8, "wr_sc")
-        nc.vector.tensor_copy(
-            wr_w[:].bitcast(I32).rearrange("p (a t g w) -> p a t g w", a=3, t=4, g=16),
-            wr_raw[:].bitcast(I32).rearrange("p (a g t w) -> p a t g w", a=3, t=4, g=16),
-        )
-        nc.vector.tensor_copy(
-            wr_sc[:].bitcast(I32).rearrange("p (a t g w) -> p a t g w", a=3, t=4, g=16),
-            wr_sc_raw[:].bitcast(I32).rearrange("p (a g t w) -> p a t g w", a=3, t=4, g=16),
-        )
-        nc.vector.tensor_copy(v_sc[0][:], tab_sc[:].indirect(idx[:]))
-        for a in (1, 2):
-            nc.sync.dma_start(v_sc[a][0:112, :].bitcast(I32), v_sc[0][4 * a : 4 * a + 112, :].bitcast(I32))
+        wr_w = kept([P, K_PASSES * 2 * H], U8, "wr_w")
+        wr_sc = kept([P, K_PASSES * H], U8, "wr_sc")
+        for dst, src in ((wr_w, wr_raw), (wr_sc, wr_sc_raw)):
+            nc.vector.tensor_copy(
+                dst[:].bitcast(I32).rearrange("p (a t g w) -> p a t g w", a=K_PASSES, t=SLOTS, g=16),
+                src[:].bitcast(I32).rearrange("p (a g t w) -> p a t g w", a=K_PASSES, t=SLOTS, g=16),
+            )
         gather_table(0)
-        for c in range(NCH):
-            quantize_chunk(1, c, ils[1][c])
+        quantize_page(1, PAGE_CODES_SECOND_AT)
         gather_table(1)
         gather_table(2)
 
-        a_at = [xs_at[0], xs_at[2], page_at[6], page_at[7]]
         a_sb = []
-        for t in range(4):
-            a_t = placed([P, T2], F32, "a%d" % t, a_at[t])
+        for t in range(SLOTS):
+            a_t = placed([P, T2], F32, "a%d" % t, A_AT[t])
             a_sb.append(a_t)
-            for c in range(NCH):
-                bank = psum.tile([P, CH], F32, name="bank%d" % ((NCH * t + c) % 8))
-                for a in range(2):
-                    wc = slice(H * a + P * t, H * a + P * (t + 1))
+            for c in range(CHUNKS):
+                cols = slice(c * CHUNK, (c + 1) * CHUNK)
+                bank = bank_tile(CHUNK, (CHUNKS * t + c) % BANKS)
+                for a in range(M_PASSES):
+                    we_cols = slice(H * a + P * t, H * a + P * (t + 1))
                     nc.tensor.matmul_mx(
                         bank[:],
-                        lhsT=we_codes[:, wc].bitcast(FP8X4),
-                        lhsT_scale=we_sc[:, wc],
-                        rhs=pg_codes[a][c][:].bitcast(FP8X4),
-                        rhs_scale=pg_sc[a][:, c * CH : (c + 1) * CH],
+                        lhsT=we_codes[:, we_cols].bitcast(FP8X4),
+                        lhsT_scale=we_sc[:, we_cols],
+                        rhs=page_codes[a][:, cols].bitcast(FP8X4),
+                        rhs_scale=page_sc[a][:, cols],
                         start=(a == 0),
-                        stop=(a == 1),
+                        stop=(a == M_PASSES - 1),
                     )
-                nc.scalar.copy(a_t[:, c * CH : (c + 1) * CH], bank[:])
+                nc.scalar.copy(a_t[:, cols], bank[:])
 
-        b_ps = []
-        for u in range(PJ // UJ):
-            js = slice(u * UJ, (u + 1) * UJ)
-            bank = psum.tile([P, 4 * UJ], F32, name="bank%d" % u)
-            b_ps.append(bank)
-            for t in range(4):
-                for a in range(3):
-                    c0 = H * a + P * t
+        b_banks = []
+        for u in range(J // UNIT):
+            entries = slice(u * UNIT, (u + 1) * UNIT)
+            bank = bank_tile(SLOTS * UNIT, u)
+            b_banks.append(bank)
+            for t in range(SLOTS):
+                for a in range(K_PASSES):
+                    col = H * a + P * t
                     nc.tensor.matmul_mx(
-                        bank[:, t * UJ : (t + 1) * UJ],
-                        lhsT=wr_w[:, 2 * c0 : 2 * (c0 + P)].bitcast(FP4X4),
-                        lhsT_scale=wr_sc[:, c0 : c0 + P],
-                        rhs=v_w[a][:, js].bitcast(FP8X4),
-                        rhs_scale=v_sc[a][:, js],
+                        bank[:, t * UNIT : (t + 1) * UNIT],
+                        lhsT=wr_w[:, 2 * col : 2 * (col + P)].bitcast(FP4X4),
+                        lhsT_scale=wr_sc[:, col : col + P],
+                        rhs=v_words[a][:, entries].bitcast(FP8X4),
+                        rhs_scale=v_sc[a][:, entries],
                         start=(a == 0),
-                        stop=(a == 2),
+                        stop=(a == K_PASSES - 1),
                     )
 
-        out_v = out.rearrange("(p c) j -> p c j", c=3)
+        out_slices = out.rearrange("(p c) j -> p c j", c=N_SLICES)
 
         def gather_cells(cells, t, lo, hi):
-            nc.vector.tensor_copy(cells[:, t, :], a_sb[t][:].indirect(idx3[:, lo // 16 : hi // 16]))
+            window = a_sb[t][:].indirect(idx3[:, lo // PER_COLUMN : hi // PER_COLUMN])
+            nc.vector.tensor_copy(cells[:, t, :], window)
 
-        def multiply(cells, first, h_il, lo, j):
+        def multiply(cells, first, n, j):
+            lo = PIECES[n][0]
             nc.vector.tensor_tensor(
-                h_il[:, 4 * (j - lo) : 4 * (j - lo + UJ)].rearrange("p (c i t) -> p c t i", i=2, t=4),
-                cells[:, :, j - first : j - first + UJ].rearrange("p t (c i) -> p c t i", i=2),
-                b_ps[j // UJ][:].rearrange("p (t c i) -> p c t i", t=4, i=2),
-                MULT,
+                h_woven[n][:, SLOTS * (j - lo) : SLOTS * (j - lo + UNIT)].rearrange(
+                    "p (c i t) -> p c t i", i=2, t=SLOTS
+                ),
+                cells[:, :, j - first : j - first + UNIT].rearrange("p t (c i) -> p c t i", i=2),
+                b_banks[j // UNIT][:].rearrange("p (t c i) -> p c t i", t=SLOTS, i=2),
+                mybir.AluOpType.mult,
             )
 
-        def finish(h_il, lo, hi):
-            w = hi - lo
-            h_codes = keep.tile([P, w], U32, name="h_codes%d" % lo, align_bytes=64)
-            h_sc = keep.tile([P, w], U8, name="h_sc%d" % lo, align_bytes=64)
-            nc.vector.quantize_mx(h_codes[:].bitcast(FP8X4), h_sc[:], h_il[:])
-            sq = ring.tile([P, 3, w], F32, name="sq")
-            res = placed([P, 3, w], F32, "res%d" % lo, 16 * KB + 12 * lo)
-            groups = ((0, 1), (2,)) if w > UJ else ((0, 1, 2),)
-            for n, group in enumerate(groups):
-                bank = psum.tile([P, len(group) * w], F32, name="bank%d" % (lo // UJ + n))
+        def finish(n):
+            lo, hi = PIECES[n]
+            width = hi - lo
+            h_codes = kept([P, width], U32, "h_codes%d" % n)
+            h_sc = kept([P, width], U8, "h_sc%d" % n)
+            nc.vector.quantize_mx(h_codes[:].bitcast(FP8X4), h_sc[:], h_woven[n][:])
+            squares = ring.tile([P, N_SLICES, width], F32, name="squares")
+            result = placed([P, N_SLICES, width], F32, "result%d" % n, RESULT_AT + 4 * N_SLICES * lo)
+            groups = ((0, 1), (2,)) if width > UNIT else ((0, 1, 2),)
+            for g, group in enumerate(groups):
+                bank = bank_tile(len(group) * width, lo // UNIT + g)
                 for k, c in enumerate(group):
                     nc.tensor.matmul_mx(
-                        bank[:, k * w : (k + 1) * w],
+                        bank[:, k * width : (k + 1) * width],
                         lhsT=dop_codes[:, c * P : (c + 1) * P].bitcast(FP8X4),
                         lhsT_scale=dop_sc[:, c * P : (c + 1) * P],
                         rhs=h_codes[:].bitcast(FP8X4),
@@ -273,30 +296,27 @@ def tile_list_passive_radar_doppler_kernel(
                         stop=True,
                     )
                 nc.scalar.activation(
-                    sq[:, group[0] : group[-1] + 1, :].rearrange("p c j -> p (c j)"), bank[:], ACT.Square
+                    squares[:, group[0] : group[-1] + 1, :].rearrange("p c j -> p (c j)"), bank[:], ACT.Square
                 )
                 for c in group:
-                    nc.scalar.activation(res[:, c, :], sq[:, c, :], ACT.Ln, bias=noise_t[:, c : c + 1])
-            (nc.scalar if hi == PJ else nc.sync).dma_start(out_v[:, :, lo:hi], res[:])
+                    nc.scalar.activation(result[:, c, :], squares[:, c, :], ACT.Ln, bias=noise_sb[:, c : c + 1])
+            (nc.scalar if hi == J else nc.sync).dma_start(out_slices[:, :, lo:hi], result[:])
 
-        SPLIT = 3 * QJ
-        pieces = [(0, QJ), (QJ, 2 * QJ), (2 * QJ, SPLIT), (SPLIT, SPLIT + UJ), (SPLIT + UJ, PJ)]
-        h_ils = [keep.tile([P, 4 * (hi - lo)], BF16, name="h_il%d" % lo, align_bytes=64) for lo, hi in pieces]
-        cells = placed([P, 4, SPLIT], F32, "cells_head", 32 * KB)
-        for t in range(4):
+        h_woven = [kept([P, SLOTS * (hi - lo)], BF16, "h_woven%d" % n) for n, (lo, hi) in enumerate(PIECES)]
+        first_pieces = [n for n, (lo, hi) in enumerate(PIECES) if hi <= SPLIT]
+        cells = placed([P, SLOTS, SPLIT], F32, "cells_first", CELLS_AT)
+        for t in range(SLOTS):
             gather_cells(cells, t, 0, SPLIT)
-        for n in range(3):
-            lo, hi = pieces[n]
-            multiply(cells, 0, h_ils[n], lo, lo)
+        for n in first_pieces:
+            multiply(cells, 0, n, PIECES[n][0])
             if n > 0:
-                finish(h_ils[n - 1], *pieces[n - 1])
-            multiply(cells, 0, h_ils[n], lo, lo + UJ)
-        cells = placed([P, 4, PJ - SPLIT], F32, "cells_tail", 32 * KB)
-        for t in range(4):
-            gather_cells(cells, t, SPLIT, PJ)
+                finish(n - 1)
+            multiply(cells, 0, n, PIECES[n][0] + UNIT)
+        cells = placed([P, SLOTS, J - SPLIT], F32, "cells_second", CELLS_AT)
+        for t in range(SLOTS):
+            gather_cells(cells, t, SPLIT, J)
             if t == 0:
-                finish(h_ils[2], *pieces[2])
-        for n in (3, 4):
-            lo, hi = pieces[n]
-            multiply(cells, SPLIT, h_ils[n], lo, lo)
-            finish(h_ils[n], lo, hi)
+                finish(first_pieces[-1])
+        for n in range(len(first_pieces), len(PIECES)):
+            multiply(cells, SPLIT, n, PIECES[n][0])
+            finish(n)

@@ -82,6 +82,10 @@ def tile_list_passive_radar_doppler_kernel(
         for a in range(K_PASSES):
             nc.gpsimd.memset(v_sc[a][:].bitcast(I32), 0)
 
+        warm = kept([P, 2], F32, "warm")
+        nc.vector.memset(warm[:, 0:1], 1.0)
+        nc.scalar.activation(warm[:, 1:2], warm[:, 0:1], ACT.Ln)
+
         sc_rows = tab_scales.rearrange("a q t -> (a q) t").bitcast(I32)
         nc.sync.dma_start(idx[:], offs)
         nc.sync.dma_start(tab_sc[SCALE_ROW0 : SCALE_ROW0 + SCALE_ROWS, :].bitcast(I32), sc_rows[0:SCALE_ROWS, :])
@@ -97,7 +101,7 @@ def tile_list_passive_radar_doppler_kernel(
         dop_raw = kept([P, SLOTS, N], F32, "dop_raw")
         noise_sb = kept([P, N_SLICES], F32, "noise_sb")
         wr_raw = kept([P, K_PASSES * 2 * H], U8, "wr_raw")
-        parts = [[(0, S // 2), (S // 2, S)] if i == 0 else [(0, S)] for i in range(PLANES)]
+        parts = [[(0, S // 4), (S // 4, S)] if i == 0 else [(0, S)] for i in range(PLANES)]
         we_after_plane = {1: 0, 2: 1}
         dop_load_after, dop_round_after = 3, 4
         for i in range(PLANES):
@@ -240,7 +244,8 @@ def tile_list_passive_radar_doppler_kernel(
                 nc.scalar.copy(a_t[:, cols], bank[:])
 
         b_banks = []
-        for u in range(J // UNIT):
+
+        def project_references(u):
             entries = slice(u * UNIT, (u + 1) * UNIT)
             bank = bank_tile(SLOTS * UNIT, u)
             b_banks.append(bank)
@@ -256,6 +261,9 @@ def tile_list_passive_radar_doppler_kernel(
                         start=(a == 0),
                         stop=(a == K_PASSES - 1),
                     )
+
+        for u in range(SPLIT // UNIT):
+            project_references(u)
 
         out_slices = out.rearrange("(p c) j -> p c j", c=N_SLICES)
 
@@ -312,6 +320,8 @@ def tile_list_passive_radar_doppler_kernel(
             if n > 0:
                 finish(n - 1)
             multiply(cells, 0, n, PIECES[n][0] + UNIT)
+        for u in range(SPLIT // UNIT, J // UNIT):
+            project_references(u)
         cells = placed([P, SLOTS, J - SPLIT], F32, "cells_second", CELLS_AT)
         for t in range(SLOTS):
             gather_cells(cells, t, SPLIT, J)

@@ -30,21 +30,28 @@ PER_COLUMN = 16
 SCALE_ROWS = 16
 SCALE_ROW0 = 48
 
-SPLIT = 6 * UNIT
-PIECES = [(0, 256), (256, 512), (512, SPLIT), (SPLIT, SPLIT + UNIT), (SPLIT + UNIT, J)]
+HALF = J // 2
+QUARTER = J // 4
+PIECES = [(0, QUARTER), (QUARTER, HALF), (HALF, HALF + QUARTER), (HALF + QUARTER, J - UNIT), (J - UNIT, J)]
 
 KB = 1024
 PAGE_AT = [8 * KB * i for i in range(PLANES)]
 XS_AT = [64 * KB + 4 * KB * i for i in range(PLANES)]
-TABLE_AT = [16 * KB * a for a in range(K_PASSES)]
-PAGE_CODES_FIRST_AT = XS_AT[-1] - 7 * KB
-DOP_CODES_AT = XS_AT[-1] + KB
-WE_CODES_AT = XS_AT[-1] + 3 * KB
-PAGE_CODES_SECOND_AT = TABLE_AT[0]
-PICKED_FIRST_AT = XS_AT[4]
+WE_RAW_AT = [96 * KB, 104 * KB]
+PAIRS_AT = [112 * KB + 4 * KB * c for c in range(CHUNKS)]
+WE_WOVEN_AT = 128 * KB
+WOVEN_AT = [[136 * KB, 144 * KB], [PAGE_AT[4], PAGE_AT[5]]]
+SCALE_ROWS_AT = 152 * KB
+TABLE_AT = [PAGE_AT[0], PAGE_AT[2], WE_RAW_AT[0]]
+PICKED_AT = [XS_AT[6], WOVEN_AT[1][1]]
+WE_SC_AT = SCALE_ROWS_AT
+PAGE_CODES_AT = [WE_WOVEN_AT, WOVEN_AT[0][1]]
+DOP_CODES_AT = WOVEN_AT[1][0]
+B_AT = PAIRS_AT[2]
 A_AT = [XS_AT[0], XS_AT[2], PAGE_AT[6], PAGE_AT[7]]
-CELLS_AT = TABLE_AT[2]
-RESULT_AT = TABLE_AT[1]
+WORK_AT = TABLE_AT[2]
+RESULT_AT = TABLE_AT[0]
+H_WOVEN_AT = TABLE_AT[1]
 
 
 def tile_list_passive_radar_doppler_kernel(
@@ -75,7 +82,7 @@ def tile_list_passive_radar_doppler_kernel(
         tab_sc = kept([P, T], U8, "tab_sc")
         wr_sc_raw = kept([P, K_PASSES * H], U8, "wr_sc_raw")
         v_sc = [kept([P, J], U8, "v_sc%d" % a) for a in range(K_PASSES)]
-        v_sc_rows = kept([P, J], U8, "v_sc_rows")
+        v_sc_rows = placed([P, J], U8, "v_sc_rows", SCALE_ROWS_AT)
         nc.vector.memset(tab_sc[0:SCALE_ROW0, :].bitcast(I32), 0)
         nc.vector.memset(tab_sc[scale_end:P, :].bitcast(I32), 0)
         nc.gpsimd.memset(wr_sc_raw[:].bitcast(I32), 0)
@@ -97,13 +104,13 @@ def tile_list_passive_radar_doppler_kernel(
         dop_slots = dop.rearrange("(g t q) n -> t g q n", t=SLOTS, q=8)
         page = [placed([P, T2], F32, "page%d" % i, PAGE_AT[i]) for i in range(PLANES)]
         xs_sb = [placed([P, S], F32, "xs%d" % i, XS_AT[i]) for i in range(PLANES)]
-        we_raw = [kept([P, SLOTS, H], F32, "we_raw%d" % a) for a in range(M_PASSES)]
+        we_raw = [placed([P, SLOTS, H], F32, "we_raw%d" % a, WE_RAW_AT[a]) for a in range(M_PASSES)]
         dop_raw = kept([P, SLOTS, N], F32, "dop_raw")
         noise_sb = kept([P, N_SLICES], F32, "noise_sb")
         wr_raw = kept([P, K_PASSES * 2 * H], U8, "wr_raw")
         parts = [[(0, S // 4), (S // 4, S)] if i == 0 else [(0, S)] for i in range(PLANES)]
         we_after_plane = {1: 0, 2: 1}
-        dop_load_after, dop_round_after = 3, 4
+        dop_load_after, dop_round_after, wr_load_after = 3, 4, 4
         for i in range(PLANES):
             nc.sync.dma_start(page[i][:], base_planes[i // SLOTS, i % SLOTS])
             if i == 0:
@@ -117,31 +124,24 @@ def tile_list_passive_radar_doppler_kernel(
             if i == dop_load_after:
                 for t in range(SLOTS):
                     nc.sync.dma_start(dop_raw[:, t, :], dop_slots[t])
+            if i == wr_load_after:
+                nc.sync.dma_start(
+                    wr_raw[:].bitcast(I32).rearrange("p (a n) -> p a n", a=K_PASSES),
+                    wr_words.bitcast(I32).rearrange("a p n -> p a n"),
+                )
+                for q in range(4):
+                    nc.sync.dma_start(
+                        wr_sc_raw[32 * q : 32 * q + 4, :].bitcast(I32).rearrange("p (a n) -> p a n", a=K_PASSES),
+                        wr_scales[:, 4 * q : 4 * q + 4, :].bitcast(I32).rearrange("a r n -> r a n"),
+                    )
         nc.sync.dma_start(idx3[:], offs3)
         nc.sync.dma_start(noise_sb[:], noise.rearrange("(p c) -> p c", c=N_SLICES))
-        nc.sync.dma_start(
-            wr_raw[:].bitcast(I32).rearrange("p (a n) -> p a n", a=K_PASSES),
-            wr_words.bitcast(I32).rearrange("a p n -> p a n"),
-        )
-        for q in range(4):
-            nc.sync.dma_start(
-                wr_sc_raw[32 * q : 32 * q + 4, :].bitcast(I32).rearrange("p (a n) -> p a n", a=K_PASSES),
-                wr_scales[:, 4 * q : 4 * q + 4, :].bitcast(I32).rearrange("a r n -> r a n"),
-            )
-        for a in range(K_PASSES):
-            for q in range(4):
-                row = SCALE_ROW0 + SCALE_ROWS * a + 4 * q
-                nc.sync.dma_start(
-                    v_sc[a][32 * q : 32 * q + 4, :].bitcast(I32), v_sc_rows[row : row + 4, :].bitcast(I32)
-                )
 
-        we_woven = kept([P, M_PASSES * SLOTS * H], BF16, "we_woven")
+        we_woven = placed([P, M_PASSES * SLOTS * H], BF16, "we_woven", WE_WOVEN_AT)
         dop_woven = kept([P, SLOTS * N], BF16, "dop_woven")
         page_sc = [kept([P, T2], U8, "page_sc%d" % a) for a in range(M_PASSES)]
-        page_codes = []
         page_woven = []
-        table = []
-        v_words = []
+        table = {}
 
         def round_chunk(i, c, pairs):
             nc.scalar.copy(pairs[c][:, (i % SLOTS) // 2, :, i % 2], page[i][:, c * CHUNK : (c + 1) * CHUNK])
@@ -153,46 +153,36 @@ def tile_list_passive_radar_doppler_kernel(
                 pairs[c][:].rearrange("p u c e -> p u (c e)").bitcast(F32).rearrange("p u c -> p c u"),
             )
 
-        def quantize_page(a, at):
-            codes = placed([P, T2], U32, "page_codes%d" % a, at)
-            page_codes.append(codes)
-            for half in range(2):
-                cols = slice(half * T2 // 2, (half + 1) * T2 // 2)
-                nc.vector.quantize_mx(codes[:, cols].bitcast(FP8X4), page_sc[a][:, cols], page_woven[a][half][:])
+        wr_w = kept([P, K_PASSES * 2 * H], U8, "wr_w")
+        wr_sc = kept([P, K_PASSES * H], U8, "wr_sc")
+        for dst, src in ((wr_w, wr_raw), (wr_sc, wr_sc_raw)):
+            nc.vector.tensor_copy(
+                dst[:].bitcast(I32).rearrange("p (a t g w) -> p a t g w", a=K_PASSES, t=SLOTS, g=16),
+                src[:].bitcast(I32).rearrange("p (a g t w) -> p a t g w", a=K_PASSES, t=SLOTS, g=16),
+            )
 
-        def gather_table(a):
-            if a == 0:
-                words = placed([P, J], U32, "v_words0", PICKED_FIRST_AT)
-            else:
-                words = kept([P, J], U32, "v_words%d" % a)
-            v_words.append(words)
-            nc.vector.tensor_copy(words[:], table[a][:].bitcast(U32).indirect(idx[:]))
-
+        table_after_plane = {1: 0, 2: 2, 3: 1}
         for a in range(M_PASSES):
-            pairs = [kept([P, 2, CHUNK, 2], BF16, "pairs%d" % c) for c in range(CHUNKS)]
+            pairs = [placed([P, 2, CHUNK, 2], BF16, "pairs%d_%d" % (a, c), PAIRS_AT[c]) for c in range(CHUNKS)]
             for i in range(SLOTS * a, SLOTS * (a + 1)):
                 for lo, hi in parts[i]:
                     window = page[i][:].indirect(idx2[:, lo // PER_COLUMN : hi // PER_COLUMN])
                     nc.vector.tensor_copy(window, xs_sb[i][:, lo:hi])
-                if i == PLANES - 1:
-                    quantize_page(0, PAGE_CODES_FIRST_AT)
-                    we_codes = placed([P, M_PASSES * H], U32, "we_codes", WE_CODES_AT)
-                    we_sc = kept([P, M_PASSES * H], U8, "we_sc")
-                    nc.vector.quantize_mx(we_codes[:].bitcast(FP8X4), we_sc[:], we_woven[:])
-                    dop_codes = placed([P, N], U32, "dop_codes", DOP_CODES_AT)
-                    dop_sc = kept([P, N], U8, "dop_sc")
-                    for lo, hi in ((0, 2 * P), (2 * P, N)):
-                        nc.vector.quantize_mx(
-                            dop_codes[:, lo:hi].bitcast(FP8X4), dop_sc[:, lo:hi], dop_woven[:, SLOTS * lo : SLOTS * hi]
-                        )
                 if i % SLOTS < SLOTS - 1:
                     for c in range(CHUNKS):
                         round_chunk(i, c, pairs)
                 else:
-                    page_woven.append([kept([P, SLOTS * T2 // 2], BF16, "page_woven%d" % half) for half in range(2)])
-                    for c in range(CHUNKS):
-                        round_chunk(i, c, pairs)
-                        weave_chunk(c, pairs, page_woven[a])
+                    page_woven.append(
+                        [
+                            placed([P, SLOTS * T2 // 2], BF16, "page_woven%d_%d" % (a, half), WOVEN_AT[a][half])
+                            for half in range(2)
+                        ]
+                    )
+                    for c in range(CHUNKS + 1):
+                        if c < CHUNKS:
+                            round_chunk(i, c, pairs)
+                        if c > 0:
+                            weave_chunk(c - 1, pairs, page_woven[a])
                 if i in we_after_plane:
                     b = we_after_plane[i]
                     nc.scalar.copy(
@@ -206,22 +196,67 @@ def tile_list_passive_radar_doppler_kernel(
                         dop_woven[:].rearrange("p (c m t) -> p c m t", c=N_SLICES, t=SLOTS),
                         dop_raw[:].rearrange("p t (m c) -> p c m t", c=N_SLICES),
                     )
-                if i % 2 == 1 and i // 2 < K_PASSES:
-                    words = placed([P, T], I32, "table%d" % (i // 2), TABLE_AT[i // 2])
-                    table.append(words)
-                    nc.sync.dma_start(words[:], tab_words[i // 2].rearrange("p t i -> p (t i)").bitcast(I32))
+                if i in table_after_plane:
+                    k = table_after_plane[i]
+                    table[k] = placed([P, T], I32, "table%d" % k, TABLE_AT[k])
+                    nc.sync.dma_start(table[k][:], tab_words[k].rearrange("p t i -> p (t i)").bitcast(I32))
+                if i == SLOTS - 1:
+                    for a in range(K_PASSES):
+                        for q in range(4):
+                            row = SCALE_ROW0 + SCALE_ROWS * a + 4 * q
+                            nc.sync.dma_start(
+                                v_sc[a][32 * q : 32 * q + 4, :].bitcast(I32), v_sc_rows[row : row + 4, :].bitcast(I32)
+                            )
 
-        wr_w = kept([P, K_PASSES * 2 * H], U8, "wr_w")
-        wr_sc = kept([P, K_PASSES * H], U8, "wr_sc")
-        for dst, src in ((wr_w, wr_raw), (wr_sc, wr_sc_raw)):
-            nc.vector.tensor_copy(
-                dst[:].bitcast(I32).rearrange("p (a t g w) -> p a t g w", a=K_PASSES, t=SLOTS, g=16),
-                src[:].bitcast(I32).rearrange("p (a g t w) -> p a t g w", a=K_PASSES, t=SLOTS, g=16),
-            )
+        def offsets(tile, lo, hi):
+            return tile[:, lo // PER_COLUMN : hi // PER_COLUMN]
+
+        v_words = []
+
+        def gather_table(part):
+            words = placed([P, K_PASSES, HALF], U32, "v_words%d" % part, PICKED_AT[part])
+            v_words.append(words)
+            for a in range(K_PASSES):
+                window = table[a][:].bitcast(U32).indirect(offsets(idx, part * HALF, (part + 1) * HALF))
+                nc.vector.tensor_copy(words[:, a, :], window)
+
+        def project_references(bank, t, lo, hi):
+            for a in range(K_PASSES):
+                col = H * a + P * t
+                nc.tensor.matmul_mx(
+                    bank,
+                    lhsT=wr_w[:, 2 * col : 2 * (col + P)].bitcast(FP4X4),
+                    lhsT_scale=wr_sc[:, col : col + P],
+                    rhs=v_words[lo // HALF][:, a, lo % HALF : lo % HALF + hi - lo].bitcast(FP8X4),
+                    rhs_scale=v_sc[a][:, lo:hi],
+                    start=(a == 0),
+                    stop=(a == K_PASSES - 1),
+                )
+
         gather_table(0)
-        quantize_page(1, PAGE_CODES_SECOND_AT)
+        b_sb = placed([P, SLOTS, HALF], F32, "b_sb", B_AT)
+        for t in range(SLOTS):
+            bank = bank_tile(HALF, t)
+            project_references(bank[:], t, 0, HALF)
+            nc.scalar.copy(b_sb[:, t, :], bank[:])
+
+        we_codes = kept([P, M_PASSES * H], U32, "we_codes")
+        we_sc = placed([P, M_PASSES * H], U8, "we_sc", WE_SC_AT)
+        nc.vector.quantize_mx(we_codes[:].bitcast(FP8X4), we_sc[:], we_woven[:])
+        page_codes = []
+        for a in range(M_PASSES):
+            codes = placed([P, T2], U32, "page_codes%d" % a, PAGE_CODES_AT[a])
+            page_codes.append(codes)
+            for half in range(2):
+                cols = slice(half * T2 // 2, (half + 1) * T2 // 2)
+                nc.vector.quantize_mx(codes[:, cols].bitcast(FP8X4), page_sc[a][:, cols], page_woven[a][half][:])
+        dop_codes = placed([P, N], U32, "dop_codes", DOP_CODES_AT)
+        dop_sc = kept([P, N], U8, "dop_sc")
+        for lo, hi in ((0, 2 * P), (2 * P, N)):
+            nc.vector.quantize_mx(
+                dop_codes[:, lo:hi].bitcast(FP8X4), dop_sc[:, lo:hi], dop_woven[:, SLOTS * lo : SLOTS * hi]
+            )
         gather_table(1)
-        gather_table(2)
 
         a_sb = []
         for t in range(SLOTS):
@@ -229,7 +264,7 @@ def tile_list_passive_radar_doppler_kernel(
             a_sb.append(a_t)
             for c in range(CHUNKS):
                 cols = slice(c * CHUNK, (c + 1) * CHUNK)
-                bank = bank_tile(CHUNK, (CHUNKS * t + c) % BANKS)
+                bank = bank_tile(CHUNK, (CHUNKS * (t + 1) + c) % BANKS)
                 for a in range(M_PASSES):
                     we_cols = slice(H * a + P * t, H * a + P * (t + 1))
                     nc.tensor.matmul_mx(
@@ -243,41 +278,40 @@ def tile_list_passive_radar_doppler_kernel(
                     )
                 nc.scalar.copy(a_t[:, cols], bank[:])
 
-        b_banks = []
-
-        def project_references(u):
-            entries = slice(u * UNIT, (u + 1) * UNIT)
-            bank = bank_tile(SLOTS * UNIT, u)
-            b_banks.append(bank)
+        b_banks = {}
+        for u in range(HALF // UNIT, J // UNIT):
+            b_banks[u] = bank_tile(SLOTS * UNIT, u)
             for t in range(SLOTS):
-                for a in range(K_PASSES):
-                    col = H * a + P * t
-                    nc.tensor.matmul_mx(
-                        bank[:, t * UNIT : (t + 1) * UNIT],
-                        lhsT=wr_w[:, 2 * col : 2 * (col + P)].bitcast(FP4X4),
-                        lhsT_scale=wr_sc[:, col : col + P],
-                        rhs=v_words[a][:, entries].bitcast(FP8X4),
-                        rhs_scale=v_sc[a][:, entries],
-                        start=(a == 0),
-                        stop=(a == K_PASSES - 1),
-                    )
-
-        for u in range(SPLIT // UNIT):
-            project_references(u)
+                project_references(b_banks[u][:, t * UNIT : (t + 1) * UNIT], t, u * UNIT, (u + 1) * UNIT)
 
         out_slices = out.rearrange("(p c) j -> p c j", c=N_SLICES)
+        work = placed([P, SLOTS + 2, HALF], F32, "work", WORK_AT)
+        h_woven = [
+            placed([P, SLOTS * (hi - lo)], BF16, "h_woven%d" % n, H_WOVEN_AT + 2 * SLOTS * lo)
+            for n, (lo, hi) in enumerate(PIECES)
+        ]
 
-        def gather_cells(cells, t, lo, hi):
-            window = a_sb[t][:].indirect(idx3[:, lo // PER_COLUMN : hi // PER_COLUMN])
-            nc.vector.tensor_copy(cells[:, t, :], window)
+        def gather_product(t, lo, hi):
+            window = a_sb[t][:].indirect(offsets(idx3, lo, hi))
+            nc.vector.tensor_tensor(work[:, 2 + t, lo:hi], window, b_sb[:, t, lo:hi], mybir.AluOpType.mult)
 
-        def multiply(cells, first, n, j):
+        def gather_cells(t, lo, hi):
+            nc.vector.tensor_copy(work[:, t, lo - HALF : hi - HALF], a_sb[t][:].indirect(offsets(idx3, lo, hi)))
+
+        def weave_h(n, copy):
+            lo, hi = PIECES[n]
+            copy(
+                h_woven[n][:].rearrange("p (c i t) -> p c t i", i=4, t=SLOTS),
+                work[:, 2:, lo:hi].rearrange("p t (c i) -> p c t i", i=4),
+            )
+
+        def multiply(n, j):
             lo = PIECES[n][0]
             nc.vector.tensor_tensor(
                 h_woven[n][:, SLOTS * (j - lo) : SLOTS * (j - lo + UNIT)].rearrange(
                     "p (c i t) -> p c t i", i=2, t=SLOTS
                 ),
-                cells[:, :, j - first : j - first + UNIT].rearrange("p t (c i) -> p c t i", i=2),
+                work[:, 0:SLOTS, j - HALF : j - HALF + UNIT].rearrange("p t (c i) -> p c t i", i=2),
                 b_banks[j // UNIT][:].rearrange("p (t c i) -> p c t i", t=SLOTS, i=2),
                 mybir.AluOpType.mult,
             )
@@ -310,23 +344,24 @@ def tile_list_passive_radar_doppler_kernel(
                     nc.scalar.activation(result[:, c, :], squares[:, c, :], ACT.Ln, bias=noise_sb[:, c : c + 1])
             (nc.scalar if hi == J else nc.sync).dma_start(out_slices[:, :, lo:hi], result[:])
 
-        h_woven = [kept([P, SLOTS * (hi - lo)], BF16, "h_woven%d" % n) for n, (lo, hi) in enumerate(PIECES)]
-        first_pieces = [n for n, (lo, hi) in enumerate(PIECES) if hi <= SPLIT]
-        cells = placed([P, SLOTS, SPLIT], F32, "cells_first", CELLS_AT)
-        for t in range(SLOTS):
-            gather_cells(cells, t, 0, SPLIT)
-        for n in first_pieces:
-            multiply(cells, 0, n, PIECES[n][0])
-            if n > 0:
-                finish(n - 1)
-            multiply(cells, 0, n, PIECES[n][0] + UNIT)
-        for u in range(SPLIT // UNIT, J // UNIT):
-            project_references(u)
-        cells = placed([P, SLOTS, J - SPLIT], F32, "cells_second", CELLS_AT)
-        for t in range(SLOTS):
-            gather_cells(cells, t, SPLIT, J)
-            if t == 0:
-                finish(first_pieces[-1])
-        for n in range(len(first_pieces), len(PIECES)):
-            multiply(cells, SPLIT, n, PIECES[n][0])
-            finish(n)
+        for t in range(SLOTS - 1):
+            gather_product(t, 0, HALF)
+            if t < 2:
+                gather_cells(t, HALF, J)
+        gather_product(SLOTS - 1, *PIECES[0])
+        gather_product(SLOTS - 1, *PIECES[1])
+        weave_h(0, nc.vector.tensor_copy)
+        weave_h(1, nc.scalar.copy)
+        gather_cells(2, *PIECES[2])
+        finish(0)
+        gather_cells(3, *PIECES[2])
+        gather_cells(2, PIECES[3][0], J)
+        finish(1)
+        multiply(2, PIECES[2][0])
+        multiply(2, PIECES[2][0] + UNIT)
+        gather_cells(3, PIECES[3][0], J)
+        finish(2)
+        multiply(3, PIECES[3][0])
+        multiply(4, PIECES[4][0])
+        finish(3)
+        finish(4)

@@ -38,7 +38,7 @@ KB = 1024
 PAGE_AT = [8 * KB * i for i in range(PLANES)]
 XS_AT = [64 * KB + 4 * KB * i for i in range(PLANES)]
 WE_RAW_AT = [96 * KB, 104 * KB]
-PAIRS_AT = [112 * KB + 4 * KB * c for c in range(CHUNKS)]
+PAIRS_AT = [112 * KB, 120 * KB]
 WE_WOVEN_AT = 128 * KB
 WOVEN_AT = [[136 * KB, 144 * KB], [PAGE_AT[4], PAGE_AT[5]]]
 SCALE_ROWS_AT = 152 * KB
@@ -47,7 +47,7 @@ PICKED_AT = [XS_AT[6], WOVEN_AT[1][1]]
 WE_SC_AT = SCALE_ROWS_AT
 PAGE_CODES_AT = [WE_WOVEN_AT, WOVEN_AT[0][1]]
 DOP_CODES_AT = WOVEN_AT[1][0]
-B_AT = PAIRS_AT[2]
+B_AT = PAIRS_AT[1]
 A_AT = [XS_AT[0], XS_AT[2], PAGE_AT[6], PAGE_AT[7]]
 WORK_AT = TABLE_AT[2]
 RESULT_AT = TABLE_AT[0]
@@ -144,10 +144,10 @@ def tile_list_passive_radar_doppler_kernel(
         table = {}
 
         def round_chunk(i, c, pairs):
-            nc.scalar.copy(pairs[c][:, (i % SLOTS) // 2, :, i % 2], page[i][:, c * CHUNK : (c + 1) * CHUNK])
+            nc.scalar.copy(pairs[c][:, (i % SLOTS) // 2, :, i % 2], page[i][:, c * T2 // 2 : (c + 1) * T2 // 2])
 
         def weave_chunk(c, pairs, woven):
-            half = woven[c // 2][:].bitcast(F32)[:, (c % 2) * 2 * CHUNK : (c % 2 + 1) * 2 * CHUNK]
+            half = woven[c][:].bitcast(F32)
             nc.scalar.copy(
                 half.rearrange("p (c u) -> p c u", u=2),
                 pairs[c][:].rearrange("p u c e -> p u (c e)").bitcast(F32).rearrange("p u c -> p c u"),
@@ -156,20 +156,20 @@ def tile_list_passive_radar_doppler_kernel(
         wr_w = kept([P, K_PASSES * 2 * H], U8, "wr_w")
         wr_sc = kept([P, K_PASSES * H], U8, "wr_sc")
         for dst, src in ((wr_w, wr_raw), (wr_sc, wr_sc_raw)):
-            nc.vector.tensor_copy(
+            nc.gpsimd.tensor_copy(
                 dst[:].bitcast(I32).rearrange("p (a t g w) -> p a t g w", a=K_PASSES, t=SLOTS, g=16),
                 src[:].bitcast(I32).rearrange("p (a g t w) -> p a t g w", a=K_PASSES, t=SLOTS, g=16),
             )
 
         table_after_plane = {1: 0, 2: 2, 3: 1}
         for a in range(M_PASSES):
-            pairs = [placed([P, 2, CHUNK, 2], BF16, "pairs%d_%d" % (a, c), PAIRS_AT[c]) for c in range(CHUNKS)]
+            pairs = [placed([P, 2, T2 // 2, 2], BF16, "pairs%d_%d" % (a, c), PAIRS_AT[c]) for c in range(2)]
             for i in range(SLOTS * a, SLOTS * (a + 1)):
                 for lo, hi in parts[i]:
                     window = page[i][:].indirect(idx2[:, lo // PER_COLUMN : hi // PER_COLUMN])
                     nc.vector.tensor_copy(window, xs_sb[i][:, lo:hi])
                 if i % SLOTS < SLOTS - 1:
-                    for c in range(CHUNKS):
+                    for c in range(2):
                         round_chunk(i, c, pairs)
                 else:
                     page_woven.append(
@@ -178,11 +178,10 @@ def tile_list_passive_radar_doppler_kernel(
                             for half in range(2)
                         ]
                     )
-                    for c in range(CHUNKS + 1):
-                        if c < CHUNKS:
-                            round_chunk(i, c, pairs)
-                        if c > 0:
-                            weave_chunk(c - 1, pairs, page_woven[a])
+                    for c in range(2):
+                        round_chunk(i, c, pairs)
+                    for c in range(2):
+                        weave_chunk(c, pairs, page_woven[a])
                 if i in we_after_plane:
                     b = we_after_plane[i]
                     nc.scalar.copy(
@@ -287,7 +286,7 @@ def tile_list_passive_radar_doppler_kernel(
         out_slices = out.rearrange("(p c) j -> p c j", c=N_SLICES)
         work = placed([P, SLOTS + 2, HALF], F32, "work", WORK_AT)
         h_woven = [
-            placed([P, SLOTS * (hi - lo)], BF16, "h_woven%d" % n, H_WOVEN_AT + 2 * SLOTS * lo)
+            placed([P, SLOTS * (hi - lo)], BF16, "h_woven%d" % n, H_WOVEN_AT + 2 * SLOTS * min(lo, PIECES[-2][0]))
             for n, (lo, hi) in enumerate(PIECES)
         ]
 
@@ -362,6 +361,6 @@ def tile_list_passive_radar_doppler_kernel(
         gather_cells(3, PIECES[3][0], J)
         finish(2)
         multiply(3, PIECES[3][0])
-        multiply(4, PIECES[4][0])
         finish(3)
+        multiply(4, PIECES[4][0])
         finish(4)

@@ -38,18 +38,19 @@ KB = 1024
 PAGE_AT = [8 * KB * i for i in range(PLANES)]
 XS_AT = [64 * KB + 4 * KB * i for i in range(PLANES)]
 WE_RAW_AT = [96 * KB, 104 * KB]
-PAIRS_AT = [112 * KB, 120 * KB]
-WE_WOVEN_AT = 128 * KB
-WOVEN_AT = [[136 * KB, 144 * KB], [PAGE_AT[4], PAGE_AT[5]]]
-SCALE_ROWS_AT = 152 * KB
+WE_WOVEN_AT = 112 * KB
+WOVEN_AT = [[120 * KB, 128 * KB], [PAGE_AT[4], PAGE_AT[5]]]
+SCALE_ROWS_AT = 136 * KB
+PAIRS_AT = [138 * KB, 146 * KB]
 TABLE_AT = [PAGE_AT[0], PAGE_AT[2], WE_RAW_AT[0]]
 PICKED_AT = [XS_AT[6], WOVEN_AT[1][1]]
 WE_SC_AT = SCALE_ROWS_AT
-PAGE_CODES_AT = [WE_WOVEN_AT, WOVEN_AT[0][1]]
+PAGE_CODES_AT = [WE_WOVEN_AT, WOVEN_AT[0][0]]
 DOP_CODES_AT = WOVEN_AT[1][0]
-B_AT = PAIRS_AT[1]
 A_AT = [XS_AT[0], XS_AT[2], PAGE_AT[6], PAGE_AT[7]]
-WORK_AT = TABLE_AT[2]
+WORK_AT = PAIRS_AT[1]
+H_ROW = 2
+B_ROW = H_ROW + SLOTS
 RESULT_AT = TABLE_AT[0]
 H_WOVEN_AT = TABLE_AT[1]
 
@@ -144,7 +145,11 @@ def tile_list_passive_radar_doppler_kernel(
         table = {}
 
         def round_chunk(i, c, pairs):
-            nc.scalar.copy(pairs[c][:, (i % SLOTS) // 2, :, i % 2], page[i][:, c * T2 // 2 : (c + 1) * T2 // 2])
+            dst, src = pairs[c][:, (i % SLOTS) // 2, :, i % 2], page[i][:, c * T2 // 2 : (c + 1) * T2 // 2]
+            if i >= PLANES - 2:
+                nc.gpsimd.tensor_scalar(dst, src, 1.0, 0.0, mybir.AluOpType.mult, mybir.AluOpType.add)
+            else:
+                nc.scalar.copy(dst, src)
 
         def weave_chunk(c, pairs, woven):
             half = woven[c][:].bitcast(F32)
@@ -233,22 +238,32 @@ def tile_list_passive_radar_doppler_kernel(
                 )
 
         gather_table(0)
-        b_sb = placed([P, SLOTS, HALF], F32, "b_sb", B_AT)
+        work = placed([P, B_ROW + SLOTS, HALF], F32, "work", WORK_AT)
+
+        def b_rows(t, n):
+            if (t, n) == (SLOTS - 1, 0):
+                return work[:, 1, QUARTER:HALF]
+            return work[:, B_ROW + t, PIECES[n][0] : PIECES[n][1]]
+
         for t in range(SLOTS):
             bank = bank_tile(HALF, t)
             project_references(bank[:], t, 0, HALF)
-            nc.scalar.copy(b_sb[:, t, :], bank[:])
+            if t < SLOTS - 1:
+                nc.scalar.copy(work[:, B_ROW + t, :], bank[:])
+            else:
+                for n in range(2):
+                    nc.scalar.copy(b_rows(t, n), bank[:, PIECES[n][0] : PIECES[n][1]])
 
         we_codes = kept([P, M_PASSES * H], U32, "we_codes")
         we_sc = placed([P, M_PASSES * H], U8, "we_sc", WE_SC_AT)
         nc.vector.quantize_mx(we_codes[:].bitcast(FP8X4), we_sc[:], we_woven[:])
-        page_codes = []
-        for a in range(M_PASSES):
-            codes = placed([P, T2], U32, "page_codes%d" % a, PAGE_CODES_AT[a])
-            page_codes.append(codes)
-            for half in range(2):
-                cols = slice(half * T2 // 2, (half + 1) * T2 // 2)
-                nc.vector.quantize_mx(codes[:, cols].bitcast(FP8X4), page_sc[a][:, cols], page_woven[a][half][:])
+        page_codes = [placed([P, T2], U32, "page_codes%d" % a, PAGE_CODES_AT[a]) for a in range(M_PASSES)]
+        for half in range(2):
+            cols = slice(half * T2 // 2, (half + 1) * T2 // 2)
+            for a in range(M_PASSES):
+                nc.vector.quantize_mx(
+                    page_codes[a][:, cols].bitcast(FP8X4), page_sc[a][:, cols], page_woven[a][half][:]
+                )
         dop_codes = placed([P, N], U32, "dop_codes", DOP_CODES_AT)
         dop_sc = kept([P, N], U8, "dop_sc")
         for lo, hi in ((0, 2 * P), (2 * P, N)):
@@ -257,25 +272,23 @@ def tile_list_passive_radar_doppler_kernel(
             )
         gather_table(1)
 
-        a_sb = []
-        for t in range(SLOTS):
-            a_t = placed([P, T2], F32, "a%d" % t, A_AT[t])
-            a_sb.append(a_t)
-            for c in range(CHUNKS):
-                cols = slice(c * CHUNK, (c + 1) * CHUNK)
-                bank = bank_tile(CHUNK, (CHUNKS * (t + 1) + c) % BANKS)
-                for a in range(M_PASSES):
-                    we_cols = slice(H * a + P * t, H * a + P * (t + 1))
-                    nc.tensor.matmul_mx(
-                        bank[:],
-                        lhsT=we_codes[:, we_cols].bitcast(FP8X4),
-                        lhsT_scale=we_sc[:, we_cols],
-                        rhs=page_codes[a][:, cols].bitcast(FP8X4),
-                        rhs_scale=page_sc[a][:, cols],
-                        start=(a == 0),
-                        stop=(a == M_PASSES - 1),
-                    )
-                nc.scalar.copy(a_t[:, cols], bank[:])
+        a_sb = [placed([P, T2], F32, "a%d" % t, A_AT[t]) for t in range(SLOTS)]
+        early = [(t, c) for half in range(2) for t in range(2) for c in range(2 * half, 2 * half + 2)]
+        for k, (t, c) in enumerate(early + [(t, c) for t in range(2, SLOTS) for c in range(CHUNKS)]):
+            cols = slice(c * CHUNK, (c + 1) * CHUNK)
+            bank = bank_tile(CHUNK, (SLOTS + k) % BANKS)
+            for a in range(M_PASSES):
+                we_cols = slice(H * a + P * t, H * a + P * (t + 1))
+                nc.tensor.matmul_mx(
+                    bank[:],
+                    lhsT=we_codes[:, we_cols].bitcast(FP8X4),
+                    lhsT_scale=we_sc[:, we_cols],
+                    rhs=page_codes[a][:, cols].bitcast(FP8X4),
+                    rhs_scale=page_sc[a][:, cols],
+                    start=(a == 0),
+                    stop=(a == M_PASSES - 1),
+                )
+            nc.scalar.copy(a_sb[t][:, cols], bank[:])
 
         b_banks = {}
         for u in range(HALF // UNIT, J // UNIT):
@@ -284,7 +297,6 @@ def tile_list_passive_radar_doppler_kernel(
                 project_references(b_banks[u][:, t * UNIT : (t + 1) * UNIT], t, u * UNIT, (u + 1) * UNIT)
 
         out_slices = out.rearrange("(p c) j -> p c j", c=N_SLICES)
-        work = placed([P, SLOTS + 2, HALF], F32, "work", WORK_AT)
         h_woven = [
             placed([P, SLOTS * (hi - lo)], BF16, "h_woven%d" % n, H_WOVEN_AT + 2 * SLOTS * min(lo, PIECES[-2][0]))
             for n, (lo, hi) in enumerate(PIECES)
@@ -292,16 +304,17 @@ def tile_list_passive_radar_doppler_kernel(
 
         def gather_product(t, lo, hi):
             window = a_sb[t][:].indirect(offsets(idx3, lo, hi))
-            nc.vector.tensor_tensor(work[:, 2 + t, lo:hi], window, b_sb[:, t, lo:hi], mybir.AluOpType.mult)
+            nc.vector.tensor_tensor(work[:, H_ROW + t, lo:hi], window, work[:, B_ROW + t, :] if t < SLOTS - 1 else b_rows(t, lo // QUARTER), mybir.AluOpType.mult)
 
         def gather_cells(t, lo, hi):
-            nc.vector.tensor_copy(work[:, t, lo - HALF : hi - HALF], a_sb[t][:].indirect(offsets(idx3, lo, hi)))
+            dst = work[:, t, lo - HALF : hi - HALF]
+            nc.vector.tensor_copy(dst, a_sb[t][:].indirect(offsets(idx3, lo, hi)))
 
         def weave_h(n, copy):
             lo, hi = PIECES[n]
             copy(
                 h_woven[n][:].rearrange("p (c i t) -> p c t i", i=4, t=SLOTS),
-                work[:, 2:, lo:hi].rearrange("p t (c i) -> p c t i", i=4),
+                work[:, H_ROW:B_ROW, lo:hi].rearrange("p t (c i) -> p c t i", i=4),
             )
 
         def multiply(n, j):
@@ -324,8 +337,10 @@ def tile_list_passive_radar_doppler_kernel(
             squares = ring.tile([P, N_SLICES, width], F32, name="squares")
             result = placed([P, N_SLICES, width], F32, "result%d" % n, RESULT_AT + 4 * N_SLICES * lo)
             groups = ((0, 1), (2,)) if width > UNIT else ((0, 1, 2),)
+            if hi == J:
+                groups = ((0,), (1,), (2,))
             for g, group in enumerate(groups):
-                bank = bank_tile(len(group) * width, lo // UNIT + g)
+                bank = bank_tile(len(group) * width, (lo // UNIT + g) % BANKS)
                 for k, c in enumerate(group):
                     nc.tensor.matmul_mx(
                         bank[:, k * width : (k + 1) * width],
@@ -345,21 +360,22 @@ def tile_list_passive_radar_doppler_kernel(
 
         for t in range(SLOTS - 1):
             gather_product(t, 0, HALF)
-            if t < 2:
-                gather_cells(t, HALF, J)
-        gather_product(SLOTS - 1, *PIECES[0])
-        gather_product(SLOTS - 1, *PIECES[1])
-        weave_h(0, nc.vector.tensor_copy)
+            if t == 0:
+                gather_cells(0, HALF, J)
+        gather_product(3, *PIECES[0])
+        gather_product(3, *PIECES[1])
+        weave_h(0, nc.scalar.copy)
         weave_h(1, nc.scalar.copy)
-        gather_cells(2, *PIECES[2])
+        gather_cells(1, HALF, J)
         finish(0)
+        gather_cells(2, *PIECES[2])
         gather_cells(3, *PIECES[2])
-        gather_cells(2, PIECES[3][0], J)
         finish(1)
         multiply(2, PIECES[2][0])
         multiply(2, PIECES[2][0] + UNIT)
-        gather_cells(3, PIECES[3][0], J)
+        gather_cells(2, PIECES[3][0], J)
         finish(2)
+        gather_cells(3, PIECES[3][0], J)
         multiply(3, PIECES[3][0])
         finish(3)
         multiply(4, PIECES[4][0])

@@ -39,7 +39,7 @@ PAGE_AT = [8 * KB * i for i in range(PLANES)]
 XS_AT = [64 * KB + 4 * KB * i for i in range(PLANES)]
 WE_RAW_AT = [96 * KB, 104 * KB]
 WE_WOVEN_AT = 112 * KB
-WOVEN_AT = [[120 * KB, 128 * KB], [PAGE_AT[4], PAGE_AT[5]]]
+WOVEN_AT = [[120 * KB, 128 * KB], [154 * KB, 162 * KB]]
 SCALE_ROWS_AT = 136 * KB
 PAIRS_AT = [138 * KB, 146 * KB]
 TABLE_AT = [PAGE_AT[0], PAGE_AT[2], WE_RAW_AT[0]]
@@ -47,8 +47,8 @@ PICKED_AT = [XS_AT[6], WOVEN_AT[1][1]]
 WE_SC_AT = SCALE_ROWS_AT
 PAGE_CODES_AT = [WE_WOVEN_AT, WOVEN_AT[0][0]]
 DOP_CODES_AT = WOVEN_AT[1][0]
-A_AT = [XS_AT[0], XS_AT[2], PAGE_AT[6], PAGE_AT[7]]
-WORK_AT = PAIRS_AT[1]
+A_AT = [PAGE_AT[4], PAGE_AT[5], PAGE_AT[6], XS_AT[3]]
+WORK_AT = PAGE_AT[7]
 H_ROW = 2
 B_ROW = H_ROW + SLOTS
 RESULT_AT = TABLE_AT[0]
@@ -141,15 +141,10 @@ def tile_list_passive_radar_doppler_kernel(
         we_woven = placed([P, M_PASSES * SLOTS * H], BF16, "we_woven", WE_WOVEN_AT)
         dop_woven = kept([P, SLOTS * N], BF16, "dop_woven")
         page_sc = [kept([P, T2], U8, "page_sc%d" % a) for a in range(M_PASSES)]
-        page_woven = []
         table = {}
 
         def round_chunk(i, c, pairs):
-            dst, src = pairs[c][:, (i % SLOTS) // 2, :, i % 2], page[i][:, c * T2 // 2 : (c + 1) * T2 // 2]
-            if i >= PLANES - 2:
-                nc.gpsimd.tensor_scalar(dst, src, 1.0, 0.0, mybir.AluOpType.mult, mybir.AluOpType.add)
-            else:
-                nc.scalar.copy(dst, src)
+            nc.scalar.copy(pairs[c][:, (i % SLOTS) // 2, :, i % 2], page[i][:, c * T2 // 2 : (c + 1) * T2 // 2])
 
         def weave_chunk(c, pairs, woven):
             half = woven[c][:].bitcast(F32)
@@ -167,24 +162,27 @@ def tile_list_passive_radar_doppler_kernel(
             )
 
         table_after_plane = {1: 0, 2: 2, 3: 1}
+        pairs = [placed([P, 2, T2 // 2, 2], BF16, "pairs%d" % c, PAIRS_AT[c]) for c in range(2)]
+        page_woven = [
+            [placed([P, SLOTS * T2 // 2], BF16, "page_woven%d_%d" % (a, c), WOVEN_AT[a][c]) for c in range(2)]
+            for a in range(M_PASSES)
+        ]
         for a in range(M_PASSES):
-            pairs = [placed([P, 2, T2 // 2, 2], BF16, "pairs%d_%d" % (a, c), PAIRS_AT[c]) for c in range(2)]
             for i in range(SLOTS * a, SLOTS * (a + 1)):
                 for lo, hi in parts[i]:
                     window = page[i][:].indirect(idx2[:, lo // PER_COLUMN : hi // PER_COLUMN])
                     nc.vector.tensor_copy(window, xs_sb[i][:, lo:hi])
-                if i % SLOTS < SLOTS - 1:
-                    for c in range(2):
+                for c in range(2):
+                    if a == 0:
                         round_chunk(i, c, pairs)
-                else:
-                    page_woven.append(
-                        [
-                            placed([P, SLOTS * T2 // 2], BF16, "page_woven%d_%d" % (a, half), WOVEN_AT[a][half])
-                            for half in range(2)
-                        ]
-                    )
-                    for c in range(2):
-                        round_chunk(i, c, pairs)
+                    else:
+                        dst = page_woven[a][c][:].rearrange("p (c t) -> p c t", t=SLOTS)[:, :, i % SLOTS]
+                        src = page[i][:, c * T2 // 2 : (c + 1) * T2 // 2]
+                        if i % SLOTS < 2:
+                            nc.gpsimd.tensor_scalar(dst, src, 1.0, 0.0, mybir.AluOpType.mult, mybir.AluOpType.add)
+                        else:
+                            nc.scalar.copy(dst, src)
+                if i == SLOTS - 1:
                     for c in range(2):
                         weave_chunk(c, pairs, page_woven[a])
                 if i in we_after_plane:

@@ -32,7 +32,7 @@ SCALE_ROW0 = 48
 
 HALF = J // 2
 QUARTER = J // 4
-PIECES = [(0, QUARTER), (QUARTER, HALF), (HALF, HALF + QUARTER), (HALF + QUARTER, J - UNIT), (J - UNIT, J)]
+PIECES = [(0, UNIT), (UNIT, QUARTER), (QUARTER, HALF), (HALF, HALF + QUARTER), (HALF + QUARTER, J - UNIT), (J - UNIT, J)]
 
 KB = 1024
 PAGE_AT = [8 * KB * i for i in range(PLANES)]
@@ -90,6 +90,8 @@ def tile_list_passive_radar_doppler_kernel(
         for a in range(K_PASSES):
             nc.gpsimd.memset(v_sc[a][:].bitcast(I32), 0)
 
+        ones = kept([P, UNIT], F32, "ones")
+        nc.gpsimd.memset(ones[:], 1.0)
         warm = kept([P, 2], F32, "warm")
         nc.vector.memset(warm[:, 0:1], 1.0)
         nc.scalar.activation(warm[:, 1:2], warm[:, 0:1], ACT.Ln)
@@ -238,10 +240,10 @@ def tile_list_passive_radar_doppler_kernel(
         gather_table(0)
         work = placed([P, B_ROW + SLOTS, HALF], F32, "work", WORK_AT)
 
-        def b_rows(t, n):
-            if (t, n) == (SLOTS - 1, 0):
-                return work[:, 1, QUARTER:HALF]
-            return work[:, B_ROW + t, PIECES[n][0] : PIECES[n][1]]
+        def b_rows(t, lo, hi):
+            if t == SLOTS - 1 and lo == 0:
+                return work[:, 1, HALF - UNIT : HALF]
+            return work[:, B_ROW + t, lo:hi]
 
         for t in range(SLOTS):
             bank = bank_tile(HALF, t)
@@ -249,8 +251,8 @@ def tile_list_passive_radar_doppler_kernel(
             if t < SLOTS - 1:
                 nc.scalar.copy(work[:, B_ROW + t, :], bank[:])
             else:
-                for n in range(2):
-                    nc.scalar.copy(b_rows(t, n), bank[:, PIECES[n][0] : PIECES[n][1]])
+                for lo, hi in ((0, UNIT), (UNIT, HALF)):
+                    nc.scalar.copy(b_rows(t, lo, hi), bank[:, lo:hi])
 
         we_codes = kept([P, M_PASSES * H], U32, "we_codes")
         we_sc = placed([P, M_PASSES * H], U8, "we_sc", WE_SC_AT)
@@ -296,22 +298,29 @@ def tile_list_passive_radar_doppler_kernel(
 
         out_slices = out.rearrange("(p c) j -> p c j", c=N_SLICES)
         h_woven = [
-            placed([P, SLOTS * (hi - lo)], BF16, "h_woven%d" % n, H_WOVEN_AT + 2 * SLOTS * min(lo, PIECES[-2][0]))
+            placed([P, SLOTS * (hi - lo)], BF16, "h_woven%d" % n, H_WOVEN_AT + 2 * SLOTS * lo)[:]
             for n, (lo, hi) in enumerate(PIECES)
         ]
 
+        flat = work[:].rearrange("p r j -> p (r j)")
+        h_woven[3] = flat[:, SLOTS * HALF - UNIT : (SLOTS + 1) * HALF - UNIT].bitcast(BF16)
+
         def gather_product(t, lo, hi):
             window = a_sb[t][:].indirect(offsets(idx3, lo, hi))
-            nc.vector.tensor_tensor(work[:, H_ROW + t, lo:hi], window, work[:, B_ROW + t, :] if t < SLOTS - 1 else b_rows(t, lo // QUARTER), mybir.AluOpType.mult)
+            nc.vector.tensor_tensor(work[:, H_ROW + t, lo:hi], window, b_rows(t, lo, hi), mybir.AluOpType.mult)
 
         def gather_cells(t, lo, hi):
             dst = work[:, t, lo - HALF : hi - HALF]
-            nc.vector.tensor_copy(dst, a_sb[t][:].indirect(offsets(idx3, lo, hi)))
+            window = a_sb[t][:].indirect(offsets(idx3, lo, hi))
+            if hi - lo > UNIT:
+                nc.vector.tensor_copy(dst, window)
+            else:
+                nc.vector.tensor_tensor(dst, window, ones[:], mybir.AluOpType.mult)
 
         def weave_h(n, copy):
             lo, hi = PIECES[n]
             copy(
-                h_woven[n][:].rearrange("p (c i t) -> p c t i", i=4, t=SLOTS),
+                h_woven[n].rearrange("p (c i t) -> p c t i", i=4, t=SLOTS),
                 work[:, H_ROW:B_ROW, lo:hi].rearrange("p t (c i) -> p c t i", i=4),
             )
 
@@ -331,7 +340,7 @@ def tile_list_passive_radar_doppler_kernel(
             width = hi - lo
             h_codes = kept([P, width], U32, "h_codes%d" % n)
             h_sc = kept([P, width], U8, "h_sc%d" % n)
-            nc.vector.quantize_mx(h_codes[:].bitcast(FP8X4), h_sc[:], h_woven[n][:])
+            nc.vector.quantize_mx(h_codes[:].bitcast(FP8X4), h_sc[:], h_woven[n])
             squares = ring.tile([P, N_SLICES, width], F32, name="squares")
             result = placed([P, N_SLICES, width], F32, "result%d" % n, RESULT_AT + 4 * N_SLICES * lo)
             groups = ((0, 1), (2,)) if width > UNIT else ((0, 1, 2),)
@@ -354,27 +363,33 @@ def tile_list_passive_radar_doppler_kernel(
                 )
                 for c in group:
                     nc.scalar.activation(result[:, c, :], squares[:, c, :], ACT.Ln, bias=noise_sb[:, c : c + 1])
-            (nc.scalar if hi == J else nc.sync).dma_start(out_slices[:, :, lo:hi], result[:])
+            if hi < J:
+                nc.sync.dma_start(out_slices[:, :, lo:hi], result[:])
+            else:
+                nc.sync.dma_start(out_slices[:, 0:2, lo:hi], result[:, 0:2, :])
+                nc.scalar.dma_start(out_slices[:, 2, lo:hi], result[:, 2, :])
 
         for t in range(SLOTS - 1):
             gather_product(t, 0, HALF)
             if t == 0:
                 gather_cells(0, HALF, J)
-        gather_product(3, *PIECES[0])
-        gather_product(3, *PIECES[1])
-        weave_h(0, nc.scalar.copy)
-        weave_h(1, nc.scalar.copy)
+        gather_product(3, 0, UNIT)
+        gather_product(3, UNIT, HALF)
+        for n in range(3):
+            weave_h(n, nc.scalar.copy)
         gather_cells(1, HALF, J)
         finish(0)
-        gather_cells(2, *PIECES[2])
-        gather_cells(3, *PIECES[2])
         finish(1)
-        multiply(2, PIECES[2][0])
-        multiply(2, PIECES[2][0] + UNIT)
-        gather_cells(2, PIECES[3][0], J)
+        gather_cells(2, *PIECES[3])
+        gather_cells(3, *PIECES[3])
         finish(2)
-        gather_cells(3, PIECES[3][0], J)
         multiply(3, PIECES[3][0])
+        multiply(3, PIECES[3][0] + UNIT)
+        gather_cells(2, PIECES[4][0], J)
+        gather_cells(3, *PIECES[4])
         finish(3)
         multiply(4, PIECES[4][0])
+        gather_cells(3, *PIECES[5])
         finish(4)
+        multiply(5, PIECES[5][0])
+        finish(5)

@@ -14,6 +14,8 @@ U8 = mybir.dt.uint8
 FP8X4 = mybir.dt.float8_e4m3fn_x4
 FP4X4 = mybir.dt.float4_e2m1fn_x4
 ACT = mybir.ActivationFunctionType
+MULT = mybir.AluOpType.mult
+ADD = mybir.AluOpType.add
 
 P = 128
 SLOTS = 4
@@ -29,10 +31,12 @@ UNIT = 128
 PER_COLUMN = 16
 SCALE_ROWS = 16
 SCALE_ROW0 = 48
+LAST = SLOTS - 1
 
 HALF = J // 2
 QUARTER = J // 4
-PIECES = [(0, UNIT), (UNIT, QUARTER), (QUARTER, HALF), (HALF, HALF + QUARTER), (HALF + QUARTER, J - UNIT), (J - UNIT, J)]
+PIECES = [(0, UNIT), (UNIT, QUARTER), (QUARTER, HALF), (HALF, J - QUARTER), (J - QUARTER, J - UNIT), (J - UNIT, J)]
+FUSED_PIECES = 3
 
 KB = 1024
 PAGE_AT = [8 * KB * i for i in range(PLANES)]
@@ -40,19 +44,20 @@ XS_AT = [64 * KB + 4 * KB * i for i in range(PLANES)]
 WE_RAW_AT = [96 * KB, 104 * KB]
 WE_WOVEN_AT = 112 * KB
 WOVEN_AT = [[120 * KB, 128 * KB], [154 * KB, 162 * KB]]
-SCALE_ROWS_AT = 136 * KB
 PAIRS_AT = [138 * KB, 146 * KB]
+SCALE_ROWS_AT = 171 * KB
 TABLE_AT = [PAGE_AT[0], PAGE_AT[2], WE_RAW_AT[0]]
-PICKED_AT = [XS_AT[6], WOVEN_AT[1][1]]
-WE_SC_AT = SCALE_ROWS_AT
-PAGE_CODES_AT = [WE_WOVEN_AT, WOVEN_AT[0][0]]
+PICKED_AT = [XS_AT[5], WOVEN_AT[1][1]]
+WE_SC_AT = SCALE_ROWS_AT - KB // 2
+PAGE_CODES_AT = [SCALE_ROWS_AT + KB // 2, WE_WOVEN_AT]
 DOP_CODES_AT = WOVEN_AT[1][0]
 A_AT = [PAGE_AT[4], PAGE_AT[5], PAGE_AT[6], XS_AT[3]]
 WORK_AT = PAGE_AT[7]
-H_ROW = 2
-B_ROW = H_ROW + SLOTS
 RESULT_AT = TABLE_AT[0]
 H_WOVEN_AT = TABLE_AT[1]
+
+H_ROW = 2
+B_ROW = H_ROW + SLOTS
 
 
 def tile_list_passive_radar_doppler_kernel(
@@ -92,6 +97,7 @@ def tile_list_passive_radar_doppler_kernel(
 
         ones = kept([P, UNIT], F32, "ones")
         nc.gpsimd.memset(ones[:], 1.0)
+
         warm = kept([P, 2], F32, "warm")
         nc.vector.memset(warm[:, 0:1], 1.0)
         nc.scalar.activation(warm[:, 1:2], warm[:, 0:1], ACT.Ln)
@@ -145,15 +151,11 @@ def tile_list_passive_radar_doppler_kernel(
         page_sc = [kept([P, T2], U8, "page_sc%d" % a) for a in range(M_PASSES)]
         table = {}
 
-        def round_chunk(i, c, pairs):
-            nc.scalar.copy(pairs[c][:, (i % SLOTS) // 2, :, i % 2], page[i][:, c * T2 // 2 : (c + 1) * T2 // 2])
+        def offsets(tile, lo, hi):
+            return tile[:, lo // PER_COLUMN : hi // PER_COLUMN]
 
-        def weave_chunk(c, pairs, woven):
-            half = woven[c][:].bitcast(F32)
-            nc.scalar.copy(
-                half.rearrange("p (c u) -> p c u", u=2),
-                pairs[c][:].rearrange("p u c e -> p u (c e)").bitcast(F32).rearrange("p u c -> p c u"),
-            )
+        def page_half(half):
+            return slice(half * T2 // 2, (half + 1) * T2 // 2)
 
         wr_w = kept([P, K_PASSES * 2 * H], U8, "wr_w")
         wr_sc = kept([P, K_PASSES * H], U8, "wr_sc")
@@ -164,56 +166,54 @@ def tile_list_passive_radar_doppler_kernel(
             )
 
         table_after_plane = {1: 0, 2: 2, 3: 1}
-        pairs = [placed([P, 2, T2 // 2, 2], BF16, "pairs%d" % c, PAIRS_AT[c]) for c in range(2)]
+        pairs = [placed([P, 2, T2 // 2, 2], BF16, "pairs%d" % half, PAIRS_AT[half]) for half in range(2)]
         page_woven = [
-            [placed([P, SLOTS * T2 // 2], BF16, "page_woven%d_%d" % (a, c), WOVEN_AT[a][c]) for c in range(2)]
+            [placed([P, SLOTS * T2 // 2], BF16, "woven%d_%d" % (a, half), WOVEN_AT[a][half]) for half in range(2)]
             for a in range(M_PASSES)
         ]
-        for a in range(M_PASSES):
-            for i in range(SLOTS * a, SLOTS * (a + 1)):
-                for lo, hi in parts[i]:
-                    window = page[i][:].indirect(idx2[:, lo // PER_COLUMN : hi // PER_COLUMN])
-                    nc.vector.tensor_copy(window, xs_sb[i][:, lo:hi])
-                for c in range(2):
-                    if a == 0:
-                        round_chunk(i, c, pairs)
-                    else:
-                        dst = page_woven[a][c][:].rearrange("p (c t) -> p c t", t=SLOTS)[:, :, i % SLOTS]
-                        src = page[i][:, c * T2 // 2 : (c + 1) * T2 // 2]
-                        if i % SLOTS < 2:
-                            nc.gpsimd.tensor_scalar(dst, src, 1.0, 0.0, mybir.AluOpType.mult, mybir.AluOpType.add)
-                        else:
-                            nc.scalar.copy(dst, src)
-                if i == SLOTS - 1:
-                    for c in range(2):
-                        weave_chunk(c, pairs, page_woven[a])
-                if i in we_after_plane:
-                    b = we_after_plane[i]
+        for i in range(PLANES):
+            a, slot = divmod(i, SLOTS)
+            for lo, hi in parts[i]:
+                nc.vector.tensor_copy(page[i][:].indirect(offsets(idx2, lo, hi)), xs_sb[i][:, lo:hi])
+            for half in range(2):
+                src = page[i][:, page_half(half)]
+                in_slot = page_woven[a][half][:].rearrange("p (c t) -> p c t", t=SLOTS)[:, :, slot]
+                if a == 0:
+                    nc.scalar.copy(pairs[half][:, slot // 2, :, slot % 2], src)
+                elif slot < 2:
+                    nc.gpsimd.tensor_scalar(in_slot, src, 1.0, 0.0, MULT, ADD)
+                else:
+                    nc.scalar.copy(in_slot, src)
+            if i == SLOTS - 1:
+                for half in range(2):
                     nc.scalar.copy(
-                        we_woven[:, SLOTS * H * b : SLOTS * H * (b + 1)].rearrange(
-                            "p (t g q j) -> p t g q j", t=SLOTS, g=16, q=8
-                        ),
-                        we_raw[b][:].rearrange("p j (g t q) -> p t g q j", t=SLOTS, q=8),
+                        page_woven[0][half][:].bitcast(F32).rearrange("p (c u) -> p c u", u=2),
+                        pairs[half][:].rearrange("p u c e -> p u (c e)").bitcast(F32).rearrange("p u c -> p c u"),
                     )
-                if i == dop_round_after:
-                    nc.scalar.copy(
-                        dop_woven[:].rearrange("p (c m t) -> p c m t", c=N_SLICES, t=SLOTS),
-                        dop_raw[:].rearrange("p t (m c) -> p c m t", c=N_SLICES),
-                    )
-                if i in table_after_plane:
-                    k = table_after_plane[i]
-                    table[k] = placed([P, T], I32, "table%d" % k, TABLE_AT[k])
-                    nc.sync.dma_start(table[k][:], tab_words[k].rearrange("p t i -> p (t i)").bitcast(I32))
-                if i == SLOTS - 1:
-                    for a in range(K_PASSES):
-                        for q in range(4):
-                            row = SCALE_ROW0 + SCALE_ROWS * a + 4 * q
-                            nc.sync.dma_start(
-                                v_sc[a][32 * q : 32 * q + 4, :].bitcast(I32), v_sc_rows[row : row + 4, :].bitcast(I32)
-                            )
-
-        def offsets(tile, lo, hi):
-            return tile[:, lo // PER_COLUMN : hi // PER_COLUMN]
+            if i in we_after_plane:
+                w = we_after_plane[i]
+                nc.scalar.copy(
+                    we_woven[:, SLOTS * H * w : SLOTS * H * (w + 1)].rearrange(
+                        "p (t g q j) -> p t g q j", t=SLOTS, g=16, q=8
+                    ),
+                    we_raw[w][:].rearrange("p j (g t q) -> p t g q j", t=SLOTS, q=8),
+                )
+            if i == dop_round_after:
+                nc.scalar.copy(
+                    dop_woven[:].rearrange("p (c m t) -> p c m t", c=N_SLICES, t=SLOTS),
+                    dop_raw[:].rearrange("p t (m c) -> p c m t", c=N_SLICES),
+                )
+            if i in table_after_plane:
+                k = table_after_plane[i]
+                table[k] = placed([P, T], I32, "table%d" % k, TABLE_AT[k])
+                nc.sync.dma_start(table[k][:], tab_words[k].rearrange("p t i -> p (t i)").bitcast(I32))
+            if i == SLOTS - 1:
+                for k in range(K_PASSES):
+                    for q in range(4):
+                        row = SCALE_ROW0 + SCALE_ROWS * k + 4 * q
+                        nc.sync.dma_start(
+                            v_sc[k][32 * q : 32 * q + 4, :].bitcast(I32), v_sc_rows[row : row + 4, :].bitcast(I32)
+                        )
 
         v_words = []
 
@@ -240,26 +240,24 @@ def tile_list_passive_radar_doppler_kernel(
         gather_table(0)
         work = placed([P, B_ROW + SLOTS, HALF], F32, "work", WORK_AT)
 
-        def b_rows(t, lo, hi):
-            if t == SLOTS - 1 and lo == 0:
+        def b_row(t, lo, hi):
+            if t == LAST and lo == 0:
                 return work[:, 1, HALF - UNIT : HALF]
             return work[:, B_ROW + t, lo:hi]
 
+        last_cuts = ((0, UNIT), (UNIT, HALF))
         for t in range(SLOTS):
             bank = bank_tile(HALF, t)
             project_references(bank[:], t, 0, HALF)
-            if t < SLOTS - 1:
-                nc.scalar.copy(work[:, B_ROW + t, :], bank[:])
-            else:
-                for lo, hi in ((0, UNIT), (UNIT, HALF)):
-                    nc.scalar.copy(b_rows(t, lo, hi), bank[:, lo:hi])
+            for lo, hi in last_cuts if t == LAST else ((0, HALF),):
+                nc.scalar.copy(b_row(t, lo, hi), bank[:, lo:hi])
 
         we_codes = kept([P, M_PASSES * H], U32, "we_codes")
         we_sc = placed([P, M_PASSES * H], U8, "we_sc", WE_SC_AT)
         nc.vector.quantize_mx(we_codes[:].bitcast(FP8X4), we_sc[:], we_woven[:])
         page_codes = [placed([P, T2], U32, "page_codes%d" % a, PAGE_CODES_AT[a]) for a in range(M_PASSES)]
         for half in range(2):
-            cols = slice(half * T2 // 2, (half + 1) * T2 // 2)
+            cols = page_half(half)
             for a in range(M_PASSES):
                 nc.vector.quantize_mx(
                     page_codes[a][:, cols].bitcast(FP8X4), page_sc[a][:, cols], page_woven[a][half][:]
@@ -273,10 +271,10 @@ def tile_list_passive_radar_doppler_kernel(
         gather_table(1)
 
         a_sb = [placed([P, T2], F32, "a%d" % t, A_AT[t]) for t in range(SLOTS)]
-        early = [(t, c) for half in range(2) for t in range(2) for c in range(2 * half, 2 * half + 2)]
-        for k, (t, c) in enumerate(early + [(t, c) for t in range(2, SLOTS) for c in range(CHUNKS)]):
+        by_halves = [(t, c) for half in range(2) for t in range(2) for c in range(2 * half, 2 * half + 2)]
+        for turn, (t, c) in enumerate(by_halves + [(t, c) for t in range(2, SLOTS) for c in range(CHUNKS)]):
             cols = slice(c * CHUNK, (c + 1) * CHUNK)
-            bank = bank_tile(CHUNK, (SLOTS + k) % BANKS)
+            bank = bank_tile(CHUNK, (SLOTS + turn) % BANKS)
             for a in range(M_PASSES):
                 we_cols = slice(H * a + P * t, H * a + P * (t + 1))
                 nc.tensor.matmul_mx(
@@ -297,17 +295,19 @@ def tile_list_passive_radar_doppler_kernel(
                 project_references(b_banks[u][:, t * UNIT : (t + 1) * UNIT], t, u * UNIT, (u + 1) * UNIT)
 
         out_slices = out.rearrange("(p c) j -> p c j", c=N_SLICES)
-        h_woven = [
-            placed([P, SLOTS * (hi - lo)], BF16, "h_woven%d" % n, H_WOVEN_AT + 2 * SLOTS * lo)[:]
-            for n, (lo, hi) in enumerate(PIECES)
-        ]
 
-        flat = work[:].rearrange("p r j -> p (r j)")
-        h_woven[3] = flat[:, SLOTS * HALF - UNIT : (SLOTS + 1) * HALF - UNIT].bitcast(BF16)
+        def woven_piece(n):
+            lo, hi = PIECES[n]
+            if lo == HALF:
+                start = SLOTS * HALF - UNIT
+                return work[:].rearrange("p r j -> p (r j)")[:, start : start + HALF].bitcast(BF16)
+            return placed([P, SLOTS * (hi - lo)], BF16, "h_woven%d" % n, H_WOVEN_AT + 2 * SLOTS * lo)[:]
+
+        h_woven = [woven_piece(n) for n in range(len(PIECES))]
 
         def gather_product(t, lo, hi):
             window = a_sb[t][:].indirect(offsets(idx3, lo, hi))
-            nc.vector.tensor_tensor(work[:, H_ROW + t, lo:hi], window, b_rows(t, lo, hi), mybir.AluOpType.mult)
+            nc.vector.tensor_tensor(work[:, H_ROW + t, lo:hi], window, b_row(t, lo, hi), MULT)
 
         def gather_cells(t, lo, hi):
             dst = work[:, t, lo - HALF : hi - HALF]
@@ -315,11 +315,11 @@ def tile_list_passive_radar_doppler_kernel(
             if hi - lo > UNIT:
                 nc.vector.tensor_copy(dst, window)
             else:
-                nc.vector.tensor_tensor(dst, window, ones[:], mybir.AluOpType.mult)
+                nc.vector.tensor_tensor(dst, window, ones[:], MULT)
 
-        def weave_h(n, copy):
+        def weave_h(n):
             lo, hi = PIECES[n]
-            copy(
+            nc.scalar.copy(
                 h_woven[n].rearrange("p (c i t) -> p c t i", i=4, t=SLOTS),
                 work[:, H_ROW:B_ROW, lo:hi].rearrange("p t (c i) -> p c t i", i=4),
             )
@@ -332,7 +332,7 @@ def tile_list_passive_radar_doppler_kernel(
                 ),
                 work[:, 0:SLOTS, j - HALF : j - HALF + UNIT].rearrange("p t (c i) -> p c t i", i=2),
                 b_banks[j // UNIT][:].rearrange("p (t c i) -> p c t i", t=SLOTS, i=2),
-                mybir.AluOpType.mult,
+                MULT,
             )
 
         def finish(n):
@@ -343,9 +343,10 @@ def tile_list_passive_radar_doppler_kernel(
             nc.vector.quantize_mx(h_codes[:].bitcast(FP8X4), h_sc[:], h_woven[n])
             squares = ring.tile([P, N_SLICES, width], F32, name="squares")
             result = placed([P, N_SLICES, width], F32, "result%d" % n, RESULT_AT + 4 * N_SLICES * lo)
-            groups = ((0, 1), (2,)) if width > UNIT else ((0, 1, 2),)
             if hi == J:
                 groups = ((0,), (1,), (2,))
+            else:
+                groups = ((0, 1), (2,)) if width > UNIT else ((0, 1, 2),)
             for g, group in enumerate(groups):
                 bank = bank_tile(len(group) * width, (lo // UNIT + g) % BANKS)
                 for k, c in enumerate(group):
@@ -369,27 +370,28 @@ def tile_list_passive_radar_doppler_kernel(
                 nc.sync.dma_start(out_slices[:, 0:2, lo:hi], result[:, 0:2, :])
                 nc.scalar.dma_start(out_slices[:, 2, lo:hi], result[:, 2, :])
 
-        for t in range(SLOTS - 1):
+        piece_c, piece_d, piece_e = range(FUSED_PIECES, len(PIECES))
+        for t in range(LAST):
             gather_product(t, 0, HALF)
             if t == 0:
                 gather_cells(0, HALF, J)
-        gather_product(3, 0, UNIT)
-        gather_product(3, UNIT, HALF)
-        for n in range(3):
-            weave_h(n, nc.scalar.copy)
+        for lo, hi in last_cuts:
+            gather_product(LAST, lo, hi)
+        for n in range(FUSED_PIECES):
+            weave_h(n)
         gather_cells(1, HALF, J)
         finish(0)
         finish(1)
-        gather_cells(2, *PIECES[3])
-        gather_cells(3, *PIECES[3])
+        gather_cells(2, *PIECES[piece_c])
+        gather_cells(LAST, *PIECES[piece_c])
         finish(2)
-        multiply(3, PIECES[3][0])
-        multiply(3, PIECES[3][0] + UNIT)
-        gather_cells(2, PIECES[4][0], J)
-        gather_cells(3, *PIECES[4])
-        finish(3)
-        multiply(4, PIECES[4][0])
-        gather_cells(3, *PIECES[5])
-        finish(4)
-        multiply(5, PIECES[5][0])
-        finish(5)
+        multiply(piece_c, PIECES[piece_c][0])
+        multiply(piece_c, PIECES[piece_c][0] + UNIT)
+        gather_cells(2, PIECES[piece_d][0], J)
+        gather_cells(LAST, *PIECES[piece_d])
+        finish(piece_c)
+        multiply(piece_d, PIECES[piece_d][0])
+        gather_cells(LAST, *PIECES[piece_e])
+        finish(piece_d)
+        multiply(piece_e, PIECES[piece_e][0])
+        finish(piece_e)

@@ -180,7 +180,7 @@ def tile_list_passive_radar_doppler_kernel(
                 in_slot = page_woven[a][half][:].rearrange("p (c t) -> p c t", t=SLOTS)[:, :, slot]
                 if a == 0:
                     nc.scalar.copy(pairs[half][:, slot // 2, :, slot % 2], src)
-                elif slot < 2:
+                elif half == 1:
                     nc.gpsimd.tensor_scalar(in_slot, src, 1.0, 0.0, MULT, ADD)
                 else:
                     nc.scalar.copy(in_slot, src)
@@ -224,8 +224,8 @@ def tile_list_passive_radar_doppler_kernel(
                 window = table[a][:].bitcast(U32).indirect(offsets(idx, part * HALF, (part + 1) * HALF))
                 nc.vector.tensor_copy(words[:, a, :], window)
 
-        def project_references(bank, t, lo, hi):
-            for a in range(K_PASSES):
+        def project_references(bank, t, lo, hi, passes=range(K_PASSES)):
+            for a in passes:
                 col = H * a + P * t
                 nc.tensor.matmul_mx(
                     bank,
@@ -246,11 +246,13 @@ def tile_list_passive_radar_doppler_kernel(
             return work[:, B_ROW + t, lo:hi]
 
         last_cuts = ((0, UNIT), (UNIT, HALF))
+        first_banks = [bank_tile(HALF, t) for t in range(SLOTS)]
+        for a in range(K_PASSES):
+            for t in range(SLOTS):
+                project_references(first_banks[t][:], t, 0, HALF, (a,))
         for t in range(SLOTS):
-            bank = bank_tile(HALF, t)
-            project_references(bank[:], t, 0, HALF)
             for lo, hi in last_cuts if t == LAST else ((0, HALF),):
-                nc.scalar.copy(b_row(t, lo, hi), bank[:, lo:hi])
+                nc.scalar.copy(b_row(t, lo, hi), first_banks[t][:, lo:hi])
 
         we_codes = kept([P, M_PASSES * H], U32, "we_codes")
         we_sc = placed([P, M_PASSES * H], U8, "we_sc", WE_SC_AT)
@@ -362,7 +364,7 @@ def tile_list_passive_radar_doppler_kernel(
                 nc.scalar.activation(
                     squares[:, group[0] : group[-1] + 1, :].rearrange("p c j -> p (c j)"), bank[:], ACT.Square
                 )
-                for c in group:
+                for c in (groups[g - 1] if g else ()) + (group if g == len(groups) - 1 else ()):
                     nc.scalar.activation(result[:, c, :], squares[:, c, :], ACT.Ln, bias=noise_sb[:, c : c + 1])
             if hi < J:
                 nc.sync.dma_start(out_slices[:, :, lo:hi], result[:])

@@ -52,12 +52,14 @@ WE_SC_AT = SCALE_ROWS_AT - KB // 2
 PAGE_CODES_AT = [SCALE_ROWS_AT + KB // 2, WE_WOVEN_AT]
 DOP_CODES_AT = WOVEN_AT[1][0]
 A_AT = [PAGE_AT[4], PAGE_AT[5], PAGE_AT[6], XS_AT[3]]
-WORK_AT = PAGE_AT[7]
+B_AT = PAGE_AT[7]
+WORK_AT = 136 * KB
 RESULT_AT = TABLE_AT[0]
 H_WOVEN_AT = TABLE_AT[1]
 
-H_ROW = 2
-B_ROW = H_ROW + SLOTS
+CELL_STEP = HALF + QUARTER
+H_START = LAST * CELL_STEP
+WORK_COLUMNS = H_START + SLOTS * HALF
 
 
 def tile_list_passive_radar_doppler_kernel(
@@ -238,12 +240,15 @@ def tile_list_passive_radar_doppler_kernel(
                 )
 
         gather_table(0)
-        work = placed([P, B_ROW + SLOTS, HALF], F32, "work", WORK_AT)
+        work = placed([P, WORK_COLUMNS], F32, "work", WORK_AT)
+        cells = work[:, 0 : SLOTS * CELL_STEP].rearrange("p (t j) -> p t j", t=SLOTS)
+        h_rows = work[:, H_START:WORK_COLUMNS].rearrange("p (t j) -> p t j", t=SLOTS)
+        b_rows = placed([P, SLOTS, HALF], F32, "b_rows", B_AT)
 
         def b_row(t, lo, hi):
             if t == LAST and lo == 0:
-                return work[:, 1, HALF - UNIT : HALF]
-            return work[:, B_ROW + t, lo:hi]
+                return cells[:, 1, HALF - UNIT : HALF]
+            return b_rows[:, t, lo:hi]
 
         last_cuts = ((0, UNIT), (UNIT, HALF))
         first_banks = [bank_tile(HALF, t) for t in range(SLOTS)]
@@ -300,19 +305,20 @@ def tile_list_passive_radar_doppler_kernel(
 
         def woven_piece(n):
             lo, hi = PIECES[n]
-            if lo == HALF:
-                start = SLOTS * HALF - UNIT
-                return work[:].rearrange("p r j -> p (r j)")[:, start : start + HALF].bitcast(BF16)
+            row = 2 * CELL_STEP
+            held = {0: row + HALF, UNIT: row, QUARTER: row + QUARTER, HALF: H_START + HALF - UNIT}
+            if lo in held:
+                return work[:, held[lo] : held[lo] + 2 * (hi - lo)].bitcast(BF16)
             return placed([P, SLOTS * (hi - lo)], BF16, "h_woven%d" % n, H_WOVEN_AT + 2 * SLOTS * lo)[:]
 
         h_woven = [woven_piece(n) for n in range(len(PIECES))]
 
         def gather_product(t, lo, hi):
             window = a_sb[t][:].indirect(offsets(idx3, lo, hi))
-            nc.vector.tensor_tensor(work[:, H_ROW + t, lo:hi], window, b_row(t, lo, hi), MULT)
+            nc.vector.tensor_tensor(h_rows[:, t, lo:hi], window, b_row(t, lo, hi), MULT)
 
         def gather_cells(t, lo, hi):
-            dst = work[:, t, lo - HALF : hi - HALF]
+            dst = cells[:, t, lo - HALF : hi - HALF]
             window = a_sb[t][:].indirect(offsets(idx3, lo, hi))
             if hi - lo > UNIT:
                 nc.vector.tensor_copy(dst, window)
@@ -321,9 +327,13 @@ def tile_list_passive_radar_doppler_kernel(
 
         def weave_h(n):
             lo, hi = PIECES[n]
-            nc.scalar.copy(
-                h_woven[n].rearrange("p (c i t) -> p c t i", i=4, t=SLOTS),
-                work[:, H_ROW:B_ROW, lo:hi].rearrange("p t (c i) -> p c t i", i=4),
+            nc.gpsimd.tensor_scalar(
+                h_woven[n].rearrange("p (j t) -> p j t", t=SLOTS),
+                h_rows[:, :, lo:hi].rearrange("p t j -> p j t"),
+                1.0,
+                0.0,
+                MULT,
+                ADD,
             )
 
         def multiply(n, j):
@@ -332,7 +342,7 @@ def tile_list_passive_radar_doppler_kernel(
                 h_woven[n][:, SLOTS * (j - lo) : SLOTS * (j - lo + UNIT)].rearrange(
                     "p (c i t) -> p c t i", i=2, t=SLOTS
                 ),
-                work[:, 0:SLOTS, j - HALF : j - HALF + UNIT].rearrange("p t (c i) -> p c t i", i=2),
+                cells[:, :, j - HALF : j - HALF + UNIT].rearrange("p t (c i) -> p c t i", i=2),
                 b_banks[j // UNIT][:].rearrange("p (t c i) -> p c t i", t=SLOTS, i=2),
                 MULT,
             )
@@ -379,18 +389,19 @@ def tile_list_passive_radar_doppler_kernel(
                 gather_cells(0, HALF, J)
         for lo, hi in last_cuts:
             gather_product(LAST, lo, hi)
-        for n in range(FUSED_PIECES):
-            weave_h(n)
+        weave_h(0)
+        weave_h(1)
         gather_cells(1, HALF, J)
         finish(0)
         finish(1)
-        gather_cells(2, *PIECES[piece_c])
+        weave_h(2)
         gather_cells(LAST, *PIECES[piece_c])
+        gather_cells(2, *PIECES[piece_c])
         finish(2)
         multiply(piece_c, PIECES[piece_c][0])
         multiply(piece_c, PIECES[piece_c][0] + UNIT)
-        gather_cells(2, PIECES[piece_d][0], J)
         gather_cells(LAST, *PIECES[piece_d])
+        gather_cells(2, PIECES[piece_d][0], J)
         finish(piece_c)
         multiply(piece_d, PIECES[piece_d][0])
         gather_cells(LAST, *PIECES[piece_e])

@@ -33,10 +33,11 @@ SCALE_ROWS = 16
 SCALE_ROW0 = 48
 LAST = SLOTS - 1
 
+SCALAR_MORE = 256
 HALF = J // 2
 QUARTER = J // 4
-PIECES = [(0, UNIT), (UNIT, QUARTER), (QUARTER, HALF), (HALF, J - QUARTER), (J - QUARTER, J - UNIT), (J - UNIT, J)]
-FUSED_PIECES = 3
+PIECES = [(0, QUARTER), (QUARTER, HALF), (HALF, J - QUARTER), (J - QUARTER, J - UNIT), (J - UNIT, J)]
+FUSED_PIECES = 2
 
 KB = 1024
 PAGE_AT = [8 * KB * i for i in range(PLANES)]
@@ -48,7 +49,7 @@ PAIRS_AT = [138 * KB, 146 * KB]
 SCALE_ROWS_AT = 171 * KB
 TABLE_AT = [PAGE_AT[0], PAGE_AT[2], WE_RAW_AT[0]]
 PICKED_AT = [XS_AT[5], WOVEN_AT[1][1]]
-WE_SC_AT = SCALE_ROWS_AT - KB // 2
+WE_SC_AT = [SCALE_ROWS_AT, WOVEN_AT[0][1]]
 PAGE_CODES_AT = [SCALE_ROWS_AT + KB // 2, WE_WOVEN_AT]
 DOP_CODES_AT = WOVEN_AT[1][0]
 A_AT = [PAGE_AT[4], PAGE_AT[5], PAGE_AT[6], XS_AT[3]]
@@ -148,7 +149,7 @@ def tile_list_passive_radar_doppler_kernel(
         nc.sync.dma_start(idx3[:], offs3)
         nc.sync.dma_start(noise_sb[:], noise.rearrange("(p c) -> p c", c=N_SLICES))
 
-        we_woven = placed([P, M_PASSES * SLOTS * H], BF16, "we_woven", WE_WOVEN_AT)
+        we_woven = [placed([P, SLOTS * H], BF16, "we_woven0", WE_WOVEN_AT), kept([P, SLOTS * H], BF16, "we_woven1")]
         dop_woven = kept([P, SLOTS * N], BF16, "dop_woven")
         page_sc = [kept([P, T2], U8, "page_sc%d" % a) for a in range(M_PASSES)]
         table = {}
@@ -183,7 +184,8 @@ def tile_list_passive_radar_doppler_kernel(
                 if a == 0:
                     nc.scalar.copy(pairs[half][:, slot // 2, :, slot % 2], src)
                 elif half == 1:
-                    nc.gpsimd.tensor_scalar(in_slot, src, 1.0, 0.0, MULT, ADD)
+                    nc.scalar.copy(in_slot[:, 0:SCALAR_MORE], src[:, 0:SCALAR_MORE])
+                    nc.gpsimd.tensor_scalar(in_slot[:, SCALAR_MORE:], src[:, SCALAR_MORE:], 1.0, 0.0, MULT, ADD)
                 else:
                     nc.scalar.copy(in_slot, src)
             if i == SLOTS - 1:
@@ -194,12 +196,11 @@ def tile_list_passive_radar_doppler_kernel(
                     )
             if i in we_after_plane:
                 w = we_after_plane[i]
-                nc.scalar.copy(
-                    we_woven[:, SLOTS * H * w : SLOTS * H * (w + 1)].rearrange(
-                        "p (t g q j) -> p t g q j", t=SLOTS, g=16, q=8
-                    ),
-                    we_raw[w][:].rearrange("p j (g t q) -> p t g q j", t=SLOTS, q=8),
-                )
+                for u in range(2):
+                    nc.scalar.copy(
+                        we_woven[u][:, 2 * H * w : 2 * H * (w + 1)].rearrange("p (t g q j) -> p t g q j", t=2, g=16, q=8),
+                        we_raw[w][:].rearrange("p j (g t q) -> p t g q j", t=SLOTS, q=8)[:, 2 * u : 2 * u + 2],
+                    )
             if i == dop_round_after:
                 nc.scalar.copy(
                     dop_woven[:].rearrange("p (c m t) -> p c m t", c=N_SLICES, t=SLOTS),
@@ -247,10 +248,10 @@ def tile_list_passive_radar_doppler_kernel(
 
         def b_row(t, lo, hi):
             if t == LAST and lo == 0:
-                return cells[:, 1, HALF - UNIT : HALF]
+                return cells[:, 1, QUARTER:HALF]
             return b_rows[:, t, lo:hi]
 
-        last_cuts = ((0, UNIT), (UNIT, HALF))
+        last_cuts = PIECES[:FUSED_PIECES]
         first_banks = [bank_tile(HALF, t) for t in range(SLOTS)]
         for a in range(K_PASSES):
             for t in range(SLOTS):
@@ -259,9 +260,9 @@ def tile_list_passive_radar_doppler_kernel(
             for lo, hi in last_cuts if t == LAST else ((0, HALF),):
                 nc.scalar.copy(b_row(t, lo, hi), first_banks[t][:, lo:hi])
 
-        we_codes = kept([P, M_PASSES * H], U32, "we_codes")
-        we_sc = placed([P, M_PASSES * H], U8, "we_sc", WE_SC_AT)
-        nc.vector.quantize_mx(we_codes[:].bitcast(FP8X4), we_sc[:], we_woven[:])
+        we_codes = [kept([P, H], U32, "we_codes%d" % u) for u in range(2)]
+        we_sc = [placed([P, H], U8, "we_sc%d" % u, WE_SC_AT[u]) for u in range(2)]
+        nc.vector.quantize_mx(we_codes[0][:].bitcast(FP8X4), we_sc[0][:], we_woven[0][:])
         page_codes = [placed([P, T2], U32, "page_codes%d" % a, PAGE_CODES_AT[a]) for a in range(M_PASSES)]
         for half in range(2):
             cols = page_half(half)
@@ -269,6 +270,7 @@ def tile_list_passive_radar_doppler_kernel(
                 nc.vector.quantize_mx(
                     page_codes[a][:, cols].bitcast(FP8X4), page_sc[a][:, cols], page_woven[a][half][:]
                 )
+        nc.vector.quantize_mx(we_codes[1][:].bitcast(FP8X4), we_sc[1][:], we_woven[1][:])
         dop_codes = placed([P, N], U32, "dop_codes", DOP_CODES_AT)
         dop_sc = kept([P, N], U8, "dop_sc")
         for lo, hi in ((0, 2 * P), (2 * P, N)):
@@ -283,11 +285,11 @@ def tile_list_passive_radar_doppler_kernel(
             cols = slice(c * CHUNK, (c + 1) * CHUNK)
             bank = bank_tile(CHUNK, (SLOTS + turn) % BANKS)
             for a in range(M_PASSES):
-                we_cols = slice(H * a + P * t, H * a + P * (t + 1))
+                we_cols = slice(P * (2 * a + t % 2), P * (2 * a + t % 2 + 1))
                 nc.tensor.matmul_mx(
                     bank[:],
-                    lhsT=we_codes[:, we_cols].bitcast(FP8X4),
-                    lhsT_scale=we_sc[:, we_cols],
+                    lhsT=we_codes[t // 2][:, we_cols].bitcast(FP8X4),
+                    lhsT_scale=we_sc[t // 2][:, we_cols],
                     rhs=page_codes[a][:, cols].bitcast(FP8X4),
                     rhs_scale=page_sc[a][:, cols],
                     start=(a == 0),
@@ -306,7 +308,7 @@ def tile_list_passive_radar_doppler_kernel(
         def woven_piece(n):
             lo, hi = PIECES[n]
             row = 2 * CELL_STEP
-            held = {0: row + HALF, UNIT: row, QUARTER: row + QUARTER, HALF: H_START + HALF - UNIT}
+            held = {0: row - QUARTER, QUARTER: row + QUARTER, HALF: H_START + HALF - UNIT}
             if lo in held:
                 return work[:, held[lo] : held[lo] + 2 * (hi - lo)].bitcast(BF16)
             return placed([P, SLOTS * (hi - lo)], BF16, "h_woven%d" % n, H_WOVEN_AT + 2 * SLOTS * lo)[:]
@@ -327,13 +329,9 @@ def tile_list_passive_radar_doppler_kernel(
 
         def weave_h(n):
             lo, hi = PIECES[n]
-            nc.gpsimd.tensor_scalar(
-                h_woven[n].rearrange("p (j t) -> p j t", t=SLOTS),
-                h_rows[:, :, lo:hi].rearrange("p t j -> p j t"),
-                1.0,
-                0.0,
-                MULT,
-                ADD,
+            nc.scalar.copy(
+                h_woven[n].rearrange("p (c i t) -> p c t i", i=4, t=SLOTS),
+                h_rows[:, :, lo:hi].rearrange("p t (c i) -> p c t i", i=4),
             )
 
         def multiply(n, j):
@@ -389,15 +387,13 @@ def tile_list_passive_radar_doppler_kernel(
                 gather_cells(0, HALF, J)
         for lo, hi in last_cuts:
             gather_product(LAST, lo, hi)
-        weave_h(0)
-        weave_h(1)
+        for n in range(FUSED_PIECES):
+            weave_h(n)
         gather_cells(1, HALF, J)
         finish(0)
-        finish(1)
-        weave_h(2)
         gather_cells(LAST, *PIECES[piece_c])
         gather_cells(2, *PIECES[piece_c])
-        finish(2)
+        finish(1)
         multiply(piece_c, PIECES[piece_c][0])
         multiply(piece_c, PIECES[piece_c][0] + UNIT)
         gather_cells(LAST, *PIECES[piece_d])

@@ -105,10 +105,9 @@ def tile_list_passive_radar_doppler_kernel(
         nc.vector.memset(warm[:, 0:1], 1.0)
         nc.scalar.activation(warm[:, 1:2], warm[:, 0:1], ACT.Ln)
 
-        sc_rows = tab_scales.rearrange("a q t -> (a q) t").bitcast(I32)
         nc.sync.dma_start(idx[:], offs)
-        nc.sync.dma_start(tab_sc[SCALE_ROW0 : SCALE_ROW0 + SCALE_ROWS, :].bitcast(I32), sc_rows[0:SCALE_ROWS, :])
-        nc.sync.dma_start(tab_sc[SCALE_ROW0 + SCALE_ROWS : scale_end, :].bitcast(I32), sc_rows[SCALE_ROWS:, :])
+        for a in range(K_PASSES):
+            nc.sync.dma_start(tab_sc[SCALE_ROW0 + a : scale_end : K_PASSES, :].bitcast(I32), tab_scales[a].bitcast(I32))
         nc.vector.tensor_copy(v_sc_rows[:], tab_sc[:].indirect(idx[:]))
 
         base_planes = base.rearrange("(a p i) t -> a i p t", a=M_PASSES, i=SLOTS)
@@ -213,9 +212,10 @@ def tile_list_passive_radar_doppler_kernel(
             if i == SLOTS - 1:
                 for k in range(K_PASSES):
                     for q in range(4):
-                        row = SCALE_ROW0 + SCALE_ROWS * k + 4 * q
+                        row = SCALE_ROW0 + K_PASSES * 4 * q + k
                         nc.sync.dma_start(
-                            v_sc[k][32 * q : 32 * q + 4, :].bitcast(I32), v_sc_rows[row : row + 4, :].bitcast(I32)
+                            v_sc[k][32 * q : 32 * q + 4, :].bitcast(I32),
+                            v_sc_rows[row : row + K_PASSES * 4 : K_PASSES, :].bitcast(I32),
                         )
 
         v_words = []

@@ -37,7 +37,6 @@ SCALAR_MORE = 256
 HALF = J // 2
 QUARTER = J // 4
 PIECES = [(0, QUARTER), (QUARTER, HALF), (HALF, J - QUARTER), (J - QUARTER, J - UNIT), (J - UNIT, J)]
-FUSED_PIECES = 2
 
 KB = 1024
 PAGE_AT = [8 * KB * i for i in range(PLANES)]
@@ -51,16 +50,22 @@ TABLE_AT = [PAGE_AT[0], PAGE_AT[2], WE_RAW_AT[0]]
 PICKED_AT = [XS_AT[5], WOVEN_AT[1][1]]
 WE_SC_AT = [SCALE_ROWS_AT, WOVEN_AT[0][1]]
 PAGE_CODES_AT = [SCALE_ROWS_AT + KB // 2, WE_WOVEN_AT]
-DOP_CODES_AT = WOVEN_AT[1][0]
+DOP_CODES_AT = WOVEN_AT[1][0] + 6 * KB
 A_AT = [PAGE_AT[4], PAGE_AT[5], PAGE_AT[6], XS_AT[3]]
-B_AT = PAGE_AT[7]
-WORK_AT = 136 * KB
+B_AT = [PAGE_AT[7], XS_AT[0]]
+WORK_AT = WOVEN_AT[0][1] + KB // 2
 RESULT_AT = TABLE_AT[0]
 H_WOVEN_AT = TABLE_AT[1]
 
-CELL_STEP = HALF + QUARTER
-H_START = LAST * CELL_STEP
-WORK_COLUMNS = H_START + SLOTS * HALF
+FOURTH_AT, FOURTH_STEP = 0, HALF + QUARTER
+WOVEN1_AT = HALF
+B1_AT = 2 * FOURTH_STEP - QUARTER
+WOVEN2_AT = LAST * FOURTH_STEP
+FIRST_AT = WOVEN2_AT + QUARTER - 64
+THIRD_AT = FIRST_AT + SLOTS * HALF
+B2_AT = THIRD_AT + HALF
+WOVEN0_AT = THIRD_AT + LAST * HALF
+WORK_COLUMNS = THIRD_AT + SLOTS * HALF
 
 
 def tile_list_passive_radar_doppler_kernel(
@@ -97,9 +102,6 @@ def tile_list_passive_radar_doppler_kernel(
         nc.gpsimd.memset(wr_sc_raw[:].bitcast(I32), 0)
         for a in range(K_PASSES):
             nc.gpsimd.memset(v_sc[a][:].bitcast(I32), 0)
-
-        ones = kept([P, UNIT], F32, "ones")
-        nc.gpsimd.memset(ones[:], 1.0)
 
         warm = kept([P, 2], F32, "warm")
         nc.vector.memset(warm[:, 0:1], 1.0)
@@ -241,24 +243,30 @@ def tile_list_passive_radar_doppler_kernel(
                 )
 
         gather_table(0)
-        work = placed([P, WORK_COLUMNS], F32, "work", WORK_AT)
-        cells = work[:, 0 : SLOTS * CELL_STEP].rearrange("p (t j) -> p t j", t=SLOTS)
-        h_rows = work[:, H_START:WORK_COLUMNS].rearrange("p (t j) -> p t j", t=SLOTS)
-        b_rows = placed([P, SLOTS, HALF], F32, "b_rows", B_AT)
+        b_rows = [placed([P, SLOTS, HALF], F32, "b_rows%d" % part, B_AT[part]) for part in range(2)]
 
-        def b_row(t, lo, hi):
-            if t == LAST and lo == 0:
-                return cells[:, 1, QUARTER:HALF]
-            return b_rows[:, t, lo:hi]
+        def h_rows(lo, hi):
+            if lo < HALF:
+                at, step, first = FIRST_AT, HALF, 0
+            elif lo < J - QUARTER:
+                at, step, first = THIRD_AT, HALF, HALF
+            else:
+                at, step, first = FOURTH_AT, FOURTH_STEP, J - QUARTER
+            rows = work[:, at : at + SLOTS * step].rearrange("p (t j) -> p t j", t=SLOTS)
+            return rows[:, :, lo - first : hi - first]
 
-        last_cuts = PIECES[:FUSED_PIECES]
+        def b_row(t, part):
+            if part == 1 and t in (1, 2):
+                at = B1_AT if t == 1 else B2_AT
+                return work[:, at : at + HALF]
+            return b_rows[part][:, t, :]
+
         first_banks = [bank_tile(HALF, t) for t in range(SLOTS)]
         for a in range(K_PASSES):
             for t in range(SLOTS):
                 project_references(first_banks[t][:], t, 0, HALF, (a,))
         for t in range(SLOTS):
-            for lo, hi in last_cuts if t == LAST else ((0, HALF),):
-                nc.scalar.copy(b_row(t, lo, hi), first_banks[t][:, lo:hi])
+            nc.scalar.copy(b_row(t, 0), first_banks[t][:])
 
         we_codes = [kept([P, H], U32, "we_codes%d" % u) for u in range(2)]
         we_sc = [placed([P, H], U8, "we_sc%d" % u, WE_SC_AT[u]) for u in range(2)]
@@ -279,9 +287,11 @@ def tile_list_passive_radar_doppler_kernel(
             )
         gather_table(1)
 
+        work = placed([P, WORK_COLUMNS], F32, "work", WORK_AT)
         a_sb = [placed([P, T2], F32, "a%d" % t, A_AT[t]) for t in range(SLOTS)]
         by_halves = [(t, c) for half in range(2) for t in range(2) for c in range(2 * half, 2 * half + 2)]
-        for turn, (t, c) in enumerate(by_halves + [(t, c) for t in range(2, SLOTS) for c in range(CHUNKS)]):
+
+        def project_page(turn, t, c):
             cols = slice(c * CHUNK, (c + 1) * CHUNK)
             bank = bank_tile(CHUNK, (SLOTS + turn) % BANKS)
             for a in range(M_PASSES):
@@ -295,54 +305,44 @@ def tile_list_passive_radar_doppler_kernel(
                     start=(a == 0),
                     stop=(a == M_PASSES - 1),
                 )
-            nc.scalar.copy(a_sb[t][:, cols], bank[:])
+            return bank
 
-        b_banks = {}
-        for u in range(HALF // UNIT, J // UNIT):
-            b_banks[u] = bank_tile(SLOTS * UNIT, u)
-            for t in range(SLOTS):
-                project_references(b_banks[u][:, t * UNIT : (t + 1) * UNIT], t, u * UNIT, (u + 1) * UNIT)
+        def second_b(t):
+            bank = bank_tile(HALF, SLOTS + t)
+            project_references(bank[:], t, HALF, J)
+            nc.scalar.copy(b_row(t, 1), bank[:])
+
+        for turn, (t, c) in enumerate(by_halves + [(2, c) for c in range(CHUNKS)]):
+            nc.scalar.copy(a_sb[t][:, c * CHUNK : (c + 1) * CHUNK], project_page(turn, t, c)[:])
+        last_banks = [project_page(LAST * CHUNKS + c, LAST, c) for c in range(CHUNKS)]
+        for c in range(CHUNKS):
+            nc.scalar.copy(a_sb[LAST][:, c * CHUNK : (c + 1) * CHUNK], last_banks[c][:])
+            if c == 0:
+                second_b(0)
+        for t in (2, 1, LAST):
+            second_b(t)
 
         out_slices = out.rearrange("(p c) j -> p c j", c=N_SLICES)
 
         def woven_piece(n):
             lo, hi = PIECES[n]
-            row = 2 * CELL_STEP
-            held = {0: row - QUARTER, QUARTER: row + QUARTER, HALF: H_START + HALF - UNIT}
-            if lo in held:
-                return work[:, held[lo] : held[lo] + 2 * (hi - lo)].bitcast(BF16)
+            if n < 3:
+                at = (WOVEN0_AT, WOVEN1_AT, WOVEN2_AT)[n]
+                return work[:, at : at + HALF].bitcast(BF16)
             return placed([P, SLOTS * (hi - lo)], BF16, "h_woven%d" % n, H_WOVEN_AT + 2 * SLOTS * lo)[:]
 
         h_woven = [woven_piece(n) for n in range(len(PIECES))]
 
         def gather_product(t, lo, hi):
             window = a_sb[t][:].indirect(offsets(idx3, lo, hi))
-            nc.vector.tensor_tensor(h_rows[:, t, lo:hi], window, b_row(t, lo, hi), MULT)
+            b = b_row(t, lo // HALF)[:, lo % HALF : lo % HALF + hi - lo]
+            nc.vector.tensor_tensor(h_rows(lo, hi)[:, t, :], window, b, MULT)
 
-        def gather_cells(t, lo, hi):
-            dst = cells[:, t, lo - HALF : hi - HALF]
-            window = a_sb[t][:].indirect(offsets(idx3, lo, hi))
-            if hi - lo > UNIT:
-                nc.vector.tensor_copy(dst, window)
-            else:
-                nc.vector.tensor_tensor(dst, window, ones[:], MULT)
-
-        def weave_h(n):
+        def weave_h(n, copy):
             lo, hi = PIECES[n]
-            nc.scalar.copy(
+            copy(
                 h_woven[n].rearrange("p (c i t) -> p c t i", i=4, t=SLOTS),
-                h_rows[:, :, lo:hi].rearrange("p t (c i) -> p c t i", i=4),
-            )
-
-        def multiply(n, j):
-            lo = PIECES[n][0]
-            nc.vector.tensor_tensor(
-                h_woven[n][:, SLOTS * (j - lo) : SLOTS * (j - lo + UNIT)].rearrange(
-                    "p (c i t) -> p c t i", i=2, t=SLOTS
-                ),
-                cells[:, :, j - HALF : j - HALF + UNIT].rearrange("p t (c i) -> p c t i", i=2),
-                b_banks[j // UNIT][:].rearrange("p (t c i) -> p c t i", t=SLOTS, i=2),
-                MULT,
+                h_rows(lo, hi).rearrange("p t (c i) -> p c t i", i=4),
             )
 
         def finish(n):
@@ -380,27 +380,27 @@ def tile_list_passive_radar_doppler_kernel(
                 nc.sync.dma_start(out_slices[:, 0:2, lo:hi], result[:, 0:2, :])
                 nc.scalar.dma_start(out_slices[:, 2, lo:hi], result[:, 2, :])
 
-        piece_c, piece_d, piece_e = range(FUSED_PIECES, len(PIECES))
+        fourth = (J - QUARTER, J)
         for t in range(LAST):
             gather_product(t, 0, HALF)
-            if t == 0:
-                gather_cells(0, HALF, J)
-        for lo, hi in last_cuts:
-            gather_product(LAST, lo, hi)
-        for n in range(FUSED_PIECES):
-            weave_h(n)
-        gather_cells(1, HALF, J)
+        gather_product(0, *PIECES[2])
+        gather_product(0, *fourth)
+        gather_product(LAST, *PIECES[0])
+        gather_product(LAST, *PIECES[1])
+        weave_h(0, nc.vector.tensor_copy)
+        weave_h(1, nc.scalar.copy)
+        gather_product(2, *PIECES[2])
         finish(0)
-        gather_cells(LAST, *PIECES[piece_c])
-        gather_cells(2, *PIECES[piece_c])
+        gather_product(1, *PIECES[2])
+        gather_product(LAST, *PIECES[2])
         finish(1)
-        multiply(piece_c, PIECES[piece_c][0])
-        multiply(piece_c, PIECES[piece_c][0] + UNIT)
-        gather_cells(LAST, *PIECES[piece_d])
-        gather_cells(2, PIECES[piece_d][0], J)
-        finish(piece_c)
-        multiply(piece_d, PIECES[piece_d][0])
-        gather_cells(LAST, *PIECES[piece_e])
-        finish(piece_d)
-        multiply(piece_e, PIECES[piece_e][0])
-        finish(piece_e)
+        weave_h(2, nc.vector.tensor_copy)
+        gather_product(1, *fourth)
+        finish(2)
+        gather_product(2, *fourth)
+        gather_product(LAST, *PIECES[3])
+        gather_product(LAST, *PIECES[4])
+        weave_h(3, nc.vector.tensor_copy)
+        weave_h(4, nc.vector.tensor_copy)
+        finish(3)
+        finish(4)

@@ -47,25 +47,26 @@ WOVEN_AT = [[120 * KB, 128 * KB], [154 * KB, 162 * KB]]
 PAIRS_AT = [138 * KB, 146 * KB]
 SCALE_ROWS_AT = 171 * KB
 TABLE_AT = [PAGE_AT[0], PAGE_AT[2], WE_RAW_AT[0]]
+PASS_ORDER = (0, 2, 1)
 PICKED_AT = [XS_AT[5], WOVEN_AT[1][1]]
 WE_SC_AT = [SCALE_ROWS_AT, WOVEN_AT[0][1]]
 PAGE_CODES_AT = [SCALE_ROWS_AT + KB // 2, WE_WOVEN_AT]
 DOP_CODES_AT = WOVEN_AT[1][0] + 6 * KB
+V_SC_AT = XS_AT[0]
 A_AT = [PAGE_AT[4], PAGE_AT[5], PAGE_AT[6], XS_AT[3]]
-B_AT = [PAGE_AT[7], XS_AT[0]]
+B_AT = [PAGE_AT[7], XS_AT[1]]
 WORK_AT = WOVEN_AT[0][1] + KB // 2
 RESULT_AT = TABLE_AT[0]
 H_WOVEN_AT = TABLE_AT[1]
 
-FOURTH_AT, FOURTH_STEP = 0, HALF + QUARTER
-WOVEN1_AT = HALF
-B1_AT = 2 * FOURTH_STEP - QUARTER
-WOVEN2_AT = LAST * FOURTH_STEP
-FIRST_AT = WOVEN2_AT + QUARTER - 64
-THIRD_AT = FIRST_AT + SLOTS * HALF
-B2_AT = THIRD_AT + HALF
-WOVEN0_AT = THIRD_AT + LAST * HALF
-WORK_COLUMNS = THIRD_AT + SLOTS * HALF
+MIDDLE = QUARTER + UNIT
+OVERLAP = 64
+WOVEN2_AT = 0
+LAST_AT = WOVEN2_AT
+FIRST_AT = WOVEN2_AT + HALF - QUARTER - OVERLAP
+MIDDLE_AT = FIRST_AT + SLOTS * HALF
+WOVEN1_AT = MIDDLE_AT + LAST * MIDDLE + QUARTER
+WORK_COLUMNS = WOVEN1_AT + HALF
 
 
 def tile_list_passive_radar_doppler_kernel(
@@ -95,13 +96,10 @@ def tile_list_passive_radar_doppler_kernel(
         scale_end = SCALE_ROW0 + K_PASSES * SCALE_ROWS
         tab_sc = kept([P, T], U8, "tab_sc")
         wr_sc_raw = kept([P, K_PASSES * H], U8, "wr_sc_raw")
-        v_sc = [kept([P, J], U8, "v_sc%d" % a) for a in range(K_PASSES)]
         v_sc_rows = placed([P, J], U8, "v_sc_rows", SCALE_ROWS_AT)
         nc.vector.memset(tab_sc[0:SCALE_ROW0, :].bitcast(I32), 0)
         nc.vector.memset(tab_sc[scale_end:P, :].bitcast(I32), 0)
-        nc.gpsimd.memset(wr_sc_raw[:].bitcast(I32), 0)
-        for a in range(K_PASSES):
-            nc.gpsimd.memset(v_sc[a][:].bitcast(I32), 0)
+        nc.vector.memset(wr_sc_raw[:].bitcast(I32), 0)
 
         warm = kept([P, 2], F32, "warm")
         nc.vector.memset(warm[:, 0:1], 1.0)
@@ -195,6 +193,10 @@ def tile_list_passive_radar_doppler_kernel(
                         page_woven[0][half][:].bitcast(F32).rearrange("p (c u) -> p c u", u=2),
                         pairs[half][:].rearrange("p u c e -> p u (c e)").bitcast(F32).rearrange("p u c -> p c u"),
                     )
+            if i == 0:
+                v_sc = [placed([P, J], U8, "v_sc%d" % k, V_SC_AT + J * k) for k in range(K_PASSES)]
+                for k in range(K_PASSES):
+                    nc.gpsimd.memset(v_sc[k][:].bitcast(I32), 0)
             if i in we_after_plane:
                 w = we_after_plane[i]
                 for u in range(2):
@@ -225,11 +227,11 @@ def tile_list_passive_radar_doppler_kernel(
         def gather_table(part):
             words = placed([P, K_PASSES, HALF], U32, "v_words%d" % part, PICKED_AT[part])
             v_words.append(words)
-            for a in range(K_PASSES):
+            for a in PASS_ORDER:
                 window = table[a][:].bitcast(U32).indirect(offsets(idx, part * HALF, (part + 1) * HALF))
                 nc.vector.tensor_copy(words[:, a, :], window)
 
-        def project_references(bank, t, lo, hi, passes=range(K_PASSES)):
+        def project_references(bank, t, lo, hi, passes=PASS_ORDER):
             for a in passes:
                 col = H * a + P * t
                 nc.tensor.matmul_mx(
@@ -238,35 +240,18 @@ def tile_list_passive_radar_doppler_kernel(
                     lhsT_scale=wr_sc[:, col : col + P],
                     rhs=v_words[lo // HALF][:, a, lo % HALF : lo % HALF + hi - lo].bitcast(FP8X4),
                     rhs_scale=v_sc[a][:, lo:hi],
-                    start=(a == 0),
-                    stop=(a == K_PASSES - 1),
+                    start=(a == PASS_ORDER[0]),
+                    stop=(a == PASS_ORDER[-1]),
                 )
 
         gather_table(0)
         b_rows = [placed([P, SLOTS, HALF], F32, "b_rows%d" % part, B_AT[part]) for part in range(2)]
-
-        def h_rows(lo, hi):
-            if lo < HALF:
-                at, step, first = FIRST_AT, HALF, 0
-            elif lo < J - QUARTER:
-                at, step, first = THIRD_AT, HALF, HALF
-            else:
-                at, step, first = FOURTH_AT, FOURTH_STEP, J - QUARTER
-            rows = work[:, at : at + SLOTS * step].rearrange("p (t j) -> p t j", t=SLOTS)
-            return rows[:, :, lo - first : hi - first]
-
-        def b_row(t, part):
-            if part == 1 and t in (1, 2):
-                at = B1_AT if t == 1 else B2_AT
-                return work[:, at : at + HALF]
-            return b_rows[part][:, t, :]
-
         first_banks = [bank_tile(HALF, t) for t in range(SLOTS)]
-        for a in range(K_PASSES):
+        for a in PASS_ORDER:
             for t in range(SLOTS):
                 project_references(first_banks[t][:], t, 0, HALF, (a,))
         for t in range(SLOTS):
-            nc.scalar.copy(b_row(t, 0), first_banks[t][:])
+            nc.scalar.copy(b_rows[0][:, t, :], first_banks[t][:])
 
         we_codes = [kept([P, H], U32, "we_codes%d" % u) for u in range(2)]
         we_sc = [placed([P, H], U8, "we_sc%d" % u, WE_SC_AT[u]) for u in range(2)]
@@ -287,11 +272,9 @@ def tile_list_passive_radar_doppler_kernel(
             )
         gather_table(1)
 
-        work = placed([P, WORK_COLUMNS], F32, "work", WORK_AT)
         a_sb = [placed([P, T2], F32, "a%d" % t, A_AT[t]) for t in range(SLOTS)]
         by_halves = [(t, c) for half in range(2) for t in range(2) for c in range(2 * half, 2 * half + 2)]
-
-        def project_page(turn, t, c):
+        for turn, (t, c) in enumerate(by_halves + [(t, c) for t in range(2, SLOTS) for c in range(CHUNKS)]):
             cols = slice(c * CHUNK, (c + 1) * CHUNK)
             bank = bank_tile(CHUNK, (SLOTS + turn) % BANKS)
             for a in range(M_PASSES):
@@ -305,37 +288,38 @@ def tile_list_passive_radar_doppler_kernel(
                     start=(a == 0),
                     stop=(a == M_PASSES - 1),
                 )
-            return bank
+            nc.scalar.copy(a_sb[t][:, cols], bank[:])
 
-        def second_b(t):
+        for t in range(SLOTS):
             bank = bank_tile(HALF, SLOTS + t)
             project_references(bank[:], t, HALF, J)
-            nc.scalar.copy(b_row(t, 1), bank[:])
+            nc.scalar.copy(b_rows[1][:, t, :], bank[:])
 
-        for turn, (t, c) in enumerate(by_halves + [(2, c) for c in range(CHUNKS)]):
-            nc.scalar.copy(a_sb[t][:, c * CHUNK : (c + 1) * CHUNK], project_page(turn, t, c)[:])
-        last_banks = [project_page(LAST * CHUNKS + c, LAST, c) for c in range(CHUNKS)]
-        for c in range(CHUNKS):
-            nc.scalar.copy(a_sb[LAST][:, c * CHUNK : (c + 1) * CHUNK], last_banks[c][:])
-            if c == 0:
-                second_b(0)
-        for t in (2, 1, LAST):
-            second_b(t)
-
+        work = placed([P, WORK_COLUMNS], F32, "work", WORK_AT)
         out_slices = out.rearrange("(p c) j -> p c j", c=N_SLICES)
+
+        def h_rows(lo, hi):
+            if lo < HALF:
+                at, step, first = FIRST_AT, HALF, 0
+            elif lo < J - UNIT:
+                at, step, first = MIDDLE_AT, MIDDLE, HALF
+            else:
+                at, step, first = LAST_AT, UNIT, J - UNIT
+            rows = work[:, at : at + SLOTS * step].rearrange("p (t j) -> p t j", t=SLOTS)
+            return rows[:, :, lo - first : hi - first]
 
         def woven_piece(n):
             lo, hi = PIECES[n]
-            if n < 3:
-                at = (WOVEN0_AT, WOVEN1_AT, WOVEN2_AT)[n]
-                return work[:, at : at + HALF].bitcast(BF16)
+            in_work = {1: WOVEN1_AT, 2: WOVEN2_AT}
+            if n in in_work:
+                return work[:, in_work[n] : in_work[n] + SLOTS * (hi - lo) // 2].bitcast(BF16)
             return placed([P, SLOTS * (hi - lo)], BF16, "h_woven%d" % n, H_WOVEN_AT + 2 * SLOTS * lo)[:]
 
         h_woven = [woven_piece(n) for n in range(len(PIECES))]
 
         def gather_product(t, lo, hi):
             window = a_sb[t][:].indirect(offsets(idx3, lo, hi))
-            b = b_row(t, lo // HALF)[:, lo % HALF : lo % HALF + hi - lo]
+            b = b_rows[lo // HALF][:, t, lo % HALF : lo % HALF + hi - lo]
             nc.vector.tensor_tensor(h_rows(lo, hi)[:, t, :], window, b, MULT)
 
         def weave_h(n, copy):
@@ -380,27 +364,24 @@ def tile_list_passive_radar_doppler_kernel(
                 nc.sync.dma_start(out_slices[:, 0:2, lo:hi], result[:, 0:2, :])
                 nc.scalar.dma_start(out_slices[:, 2, lo:hi], result[:, 2, :])
 
-        fourth = (J - QUARTER, J)
         for t in range(LAST):
             gather_product(t, 0, HALF)
-        gather_product(0, *PIECES[2])
-        gather_product(0, *fourth)
         gather_product(LAST, *PIECES[0])
         gather_product(LAST, *PIECES[1])
         weave_h(0, nc.vector.tensor_copy)
         weave_h(1, nc.scalar.copy)
-        gather_product(2, *PIECES[2])
+        gather_product(0, HALF, J - UNIT)
         finish(0)
-        gather_product(1, *PIECES[2])
+        gather_product(1, HALF, J - UNIT)
+        gather_product(2, HALF, J - UNIT)
         gather_product(LAST, *PIECES[2])
         finish(1)
         weave_h(2, nc.vector.tensor_copy)
-        gather_product(1, *fourth)
-        finish(2)
-        gather_product(2, *fourth)
         gather_product(LAST, *PIECES[3])
-        gather_product(LAST, *PIECES[4])
+        finish(2)
         weave_h(3, nc.vector.tensor_copy)
-        weave_h(4, nc.vector.tensor_copy)
+        for t in range(SLOTS):
+            gather_product(t, *PIECES[4])
         finish(3)
+        weave_h(4, nc.vector.tensor_copy)
         finish(4)

@@ -266,29 +266,32 @@ def tile_list_passive_radar_doppler_kernel(
         nc.vector.quantize_mx(we_codes[1][:].bitcast(FP8X4), we_sc[1][:], we_woven[1][:])
         dop_codes = placed([P, N], U32, "dop_codes", DOP_CODES_AT)
         dop_sc = kept([P, N], U8, "dop_sc")
-        for lo, hi in ((0, 2 * P), (2 * P, N)):
-            nc.vector.quantize_mx(
-                dop_codes[:, lo:hi].bitcast(FP8X4), dop_sc[:, lo:hi], dop_woven[:, SLOTS * lo : SLOTS * hi]
-            )
+        nc.vector.quantize_mx(dop_codes[:].bitcast(FP8X4), dop_sc[:], dop_woven[:])
         gather_table(1)
 
         a_sb = [placed([P, T2], F32, "a%d" % t, A_AT[t]) for t in range(SLOTS)]
-        by_halves = [(t, c) for half in range(2) for t in range(2) for c in range(2 * half, 2 * half + 2)]
-        for turn, (t, c) in enumerate(by_halves + [(t, c) for t in range(2, SLOTS) for c in range(CHUNKS)]):
-            cols = slice(c * CHUNK, (c + 1) * CHUNK)
-            bank = bank_tile(CHUNK, (SLOTS + turn) % BANKS)
+        turns = [(t, c) for half in range(2) for t in range(2) for c in range(2 * half, 2 * half + 2)]
+        turns = turns + [(t, c) for t in range(2, SLOTS) for c in range(CHUNKS)]
+        runs = [range(0, 4), range(4, 8)] + [range(turn, turn + 1) for turn in range(8, len(turns))]
+        for run in runs:
+            banks = {turn: bank_tile(CHUNK, (SLOTS + turn) % BANKS) for turn in run}
             for a in range(M_PASSES):
-                we_cols = slice(P * (2 * a + t % 2), P * (2 * a + t % 2 + 1))
-                nc.tensor.matmul_mx(
-                    bank[:],
-                    lhsT=we_codes[t // 2][:, we_cols].bitcast(FP8X4),
-                    lhsT_scale=we_sc[t // 2][:, we_cols],
-                    rhs=page_codes[a][:, cols].bitcast(FP8X4),
-                    rhs_scale=page_sc[a][:, cols],
-                    start=(a == 0),
-                    stop=(a == M_PASSES - 1),
-                )
-            nc.scalar.copy(a_sb[t][:, cols], bank[:])
+                for turn in run:
+                    t, c = turns[turn]
+                    cols = slice(c * CHUNK, (c + 1) * CHUNK)
+                    we_cols = slice(P * (2 * a + t % 2), P * (2 * a + t % 2 + 1))
+                    nc.tensor.matmul_mx(
+                        banks[turn][:],
+                        lhsT=we_codes[t // 2][:, we_cols].bitcast(FP8X4),
+                        lhsT_scale=we_sc[t // 2][:, we_cols],
+                        rhs=page_codes[a][:, cols].bitcast(FP8X4),
+                        rhs_scale=page_sc[a][:, cols],
+                        start=(a == 0),
+                        stop=(a == M_PASSES - 1),
+                    )
+            for turn in run:
+                t, c = turns[turn]
+                nc.scalar.copy(a_sb[t][:, c * CHUNK : (c + 1) * CHUNK], banks[turn][:])
 
         for t in range(SLOTS):
             bank = bank_tile(HALF, SLOTS + t)
@@ -337,10 +340,7 @@ def tile_list_passive_radar_doppler_kernel(
             nc.vector.quantize_mx(h_codes[:].bitcast(FP8X4), h_sc[:], h_woven[n])
             squares = ring.tile([P, N_SLICES, width], F32, name="squares")
             result = placed([P, N_SLICES, width], F32, "result%d" % n, RESULT_AT + 4 * N_SLICES * lo)
-            if hi == J:
-                groups = ((0,), (1,), (2,))
-            else:
-                groups = ((0, 1), (2,)) if width > UNIT else ((0, 1, 2),)
+            groups = ((0, 1), (2,)) if width > UNIT or hi == J else ((0, 1, 2),)
             for g, group in enumerate(groups):
                 bank = bank_tile(len(group) * width, (lo // UNIT + g) % BANKS)
                 for k, c in enumerate(group):
@@ -368,7 +368,7 @@ def tile_list_passive_radar_doppler_kernel(
             gather_product(t, 0, HALF)
         gather_product(LAST, *PIECES[0])
         gather_product(LAST, *PIECES[1])
-        weave_h(0, nc.vector.tensor_copy)
+        weave_h(0, nc.scalar.copy)
         weave_h(1, nc.scalar.copy)
         gather_product(0, HALF, J - UNIT)
         finish(0)

@@ -49,13 +49,13 @@ SCALE_ROWS_AT = 171 * KB
 TABLE_AT = [PAGE_AT[0], PAGE_AT[2], WE_RAW_AT[0]]
 PASS_ORDER = (0, 2, 1)
 PICKED_AT = [XS_AT[5], WOVEN_AT[1][1]]
-WE_SC_AT = [SCALE_ROWS_AT, WOVEN_AT[0][1]]
+WE_SC_AT = [SCALE_ROWS_AT, WOVEN_AT[0][0]]
 PAGE_CODES_AT = [SCALE_ROWS_AT + KB // 2, WE_WOVEN_AT]
 DOP_CODES_AT = WOVEN_AT[1][0] + 6 * KB
 V_SC_AT = XS_AT[0]
 A_AT = [PAGE_AT[4], PAGE_AT[5], PAGE_AT[6], XS_AT[3]]
 B_AT = [PAGE_AT[7], XS_AT[1]]
-WORK_AT = WOVEN_AT[0][1] + KB // 2
+WORK_AT = WOVEN_AT[0][1]
 RESULT_AT = TABLE_AT[0]
 H_WOVEN_AT = TABLE_AT[1]
 
@@ -247,32 +247,41 @@ def tile_list_passive_radar_doppler_kernel(
         gather_table(0)
         b_rows = [placed([P, SLOTS, HALF], F32, "b_rows%d" % part, B_AT[part]) for part in range(2)]
         first_banks = [bank_tile(HALF, t) for t in range(SLOTS)]
-        for a in PASS_ORDER:
-            for t in range(SLOTS):
-                project_references(first_banks[t][:], t, 0, HALF, (a,))
         for t in range(SLOTS):
+            project_references(first_banks[t][:], t, 0, HALF, PASS_ORDER[:1])
+        for t in range(SLOTS):
+            project_references(first_banks[t][:], t, 0, HALF, PASS_ORDER[1:])
             nc.scalar.copy(b_rows[0][:, t, :], first_banks[t][:])
 
         we_codes = [kept([P, H], U32, "we_codes%d" % u) for u in range(2)]
         we_sc = [placed([P, H], U8, "we_sc%d" % u, WE_SC_AT[u]) for u in range(2)]
         nc.vector.quantize_mx(we_codes[0][:].bitcast(FP8X4), we_sc[0][:], we_woven[0][:])
         page_codes = [placed([P, T2], U32, "page_codes%d" % a, PAGE_CODES_AT[a]) for a in range(M_PASSES)]
-        for half in range(2):
-            cols = page_half(half)
-            for a in range(M_PASSES):
-                nc.vector.quantize_mx(
-                    page_codes[a][:, cols].bitcast(FP8X4), page_sc[a][:, cols], page_woven[a][half][:]
-                )
+
+        def quantise_page(a, first, chunks):
+            cols = slice(first * CHUNK, (first + chunks) * CHUNK)
+            at = SLOTS * CHUNK * (first % 2)
+            woven = page_woven[a][first // 2][:, at : at + SLOTS * CHUNK * chunks]
+            nc.vector.quantize_mx(page_codes[a][:, cols].bitcast(FP8X4), page_sc[a][:, cols], woven)
+
+        quantise_page(0, 0, 2)
+        quantise_page(1, 0, 1)
+        quantise_page(1, 1, 1)
         nc.vector.quantize_mx(we_codes[1][:].bitcast(FP8X4), we_sc[1][:], we_woven[1][:])
+        quantise_page(0, 2, 2)
+        quantise_page(1, 2, 2)
         dop_codes = placed([P, N], U32, "dop_codes", DOP_CODES_AT)
         dop_sc = kept([P, N], U8, "dop_sc")
         nc.vector.quantize_mx(dop_codes[:].bitcast(FP8X4), dop_sc[:], dop_woven[:])
         gather_table(1)
 
         a_sb = [placed([P, T2], F32, "a%d" % t, A_AT[t]) for t in range(SLOTS)]
-        turns = [(t, c) for half in range(2) for t in range(2) for c in range(2 * half, 2 * half + 2)]
-        turns = turns + [(t, c) for t in range(2, SLOTS) for c in range(CHUNKS)]
-        runs = [range(0, 4), range(4, 8)] + [range(turn, turn + 1) for turn in range(8, len(turns))]
+        turns = [(t, c) for c in range(2) for t in range(2)] + [(2, c) for c in range(2)]
+        second_half = len(turns)
+        turns = turns + [(t, c) for t in range(LAST) for c in range(2, CHUNKS)] + [(LAST, c) for c in range(CHUNKS)]
+        ahead = {0: 2, second_half: 4}
+        inside = [n + k for n, length in ahead.items() for k in range(1, length)]
+        runs = [range(n, n + ahead.get(n, 1)) for n in range(len(turns)) if n not in inside]
         for run in runs:
             banks = {turn: bank_tile(CHUNK, (SLOTS + turn) % BANKS) for turn in run}
             for a in range(M_PASSES):

@@ -349,7 +349,10 @@ def tile_list_passive_radar_doppler_kernel(
             nc.vector.quantize_mx(h_codes[:].bitcast(FP8X4), h_sc[:], h_woven[n])
             squares = ring.tile([P, N_SLICES, width], F32, name="squares")
             result = placed([P, N_SLICES, width], F32, "result%d" % n, RESULT_AT + 4 * N_SLICES * lo)
-            groups = ((0, 1), (2,)) if width > UNIT or hi == J else ((0, 1, 2),)
+            if hi == J:
+                groups = ((0,), (1,), (2,))
+            else:
+                groups = ((0, 1), (2,)) if width > UNIT else ((0, 1, 2),)
             for g, group in enumerate(groups):
                 bank = bank_tile(len(group) * width, (lo // UNIT + g) % BANKS)
                 for k, c in enumerate(group):

@@ -37,6 +37,7 @@ SCALAR_MORE = 256
 HALF = J // 2
 QUARTER = J // 4
 PIECES = [(0, QUARTER), (QUARTER, HALF), (HALF, J - QUARTER), (J - QUARTER, J - UNIT), (J - UNIT, J)]
+Y_BANKS = ((0, 1), (2, 3), (4, 5), (6, 2, 3), (7, 0, 1))
 
 KB = 1024
 PAGE_AT = [8 * KB * i for i in range(PLANES)]
@@ -349,12 +350,9 @@ def tile_list_passive_radar_doppler_kernel(
             nc.vector.quantize_mx(h_codes[:].bitcast(FP8X4), h_sc[:], h_woven[n])
             squares = ring.tile([P, N_SLICES, width], F32, name="squares")
             result = placed([P, N_SLICES, width], F32, "result%d" % n, RESULT_AT + 4 * N_SLICES * lo)
-            if hi == J:
-                groups = ((0,), (1,), (2,))
-            else:
-                groups = ((0, 1), (2,)) if width > UNIT else ((0, 1, 2),)
+            groups = ((0, 1), (2,)) if width > UNIT else ((0,), (1,), (2,))
             for g, group in enumerate(groups):
-                bank = bank_tile(len(group) * width, (lo // UNIT + g) % BANKS)
+                bank = bank_tile(len(group) * width, Y_BANKS[n][g])
                 for k, c in enumerate(group):
                     nc.tensor.matmul_mx(
                         bank[:, k * width : (k + 1) * width],

@@ -37,7 +37,9 @@ SCALAR_MORE = 256
 HALF = J // 2
 QUARTER = J // 4
 PIECES = [(0, QUARTER), (QUARTER, HALF), (HALF, J - QUARTER), (J - QUARTER, J - UNIT), (J - UNIT, J)]
-Y_BANKS = ((0, 1), (2, 3), (4, 5), (6, 2, 3), (7, 0, 1))
+Y_BANKS = ((0, 1), (2, 3), (4, 5), (0, 1, 2), (3, 4, 5))
+THIRD_BANKS = (4, 5)
+KEPT_BANKS = (6, 7)
 
 KB = 1024
 PAGE_AT = [8 * KB * i for i in range(PLANES)]
@@ -60,14 +62,14 @@ WORK_AT = WOVEN_AT[0][1]
 RESULT_AT = TABLE_AT[0]
 H_WOVEN_AT = TABLE_AT[1]
 
-MIDDLE = QUARTER + UNIT
-OVERLAP = 64
-WOVEN2_AT = 0
-LAST_AT = WOVEN2_AT
-FIRST_AT = WOVEN2_AT + HALF - QUARTER - OVERLAP
-MIDDLE_AT = FIRST_AT + SLOTS * HALF
-WOVEN1_AT = MIDDLE_AT + LAST * MIDDLE + QUARTER
-WORK_COLUMNS = WOVEN1_AT + HALF
+THIRD_AT = 0
+WOVEN3_AT = THIRD_AT
+WOVEN0_AT = THIRD_AT + 2 * HALF
+FIRST_AT = THIRD_AT + LAST * HALF
+CELLS_AT = FIRST_AT + QUARTER + UNIT
+CELLS_STEP = HALF
+WOVEN_12_AT = CELLS_AT + LAST * CELLS_STEP + UNIT
+WORK_COLUMNS = WOVEN_12_AT + HALF
 
 
 def tile_list_passive_radar_doppler_kernel(
@@ -246,13 +248,13 @@ def tile_list_passive_radar_doppler_kernel(
                 )
 
         gather_table(0)
-        b_rows = [placed([P, SLOTS, HALF], F32, "b_rows%d" % part, B_AT[part]) for part in range(2)]
+        b_first = placed([P, SLOTS, HALF], F32, "b_first", B_AT[0])
         first_banks = [bank_tile(HALF, t) for t in range(SLOTS)]
         for t in range(SLOTS):
             project_references(first_banks[t][:], t, 0, HALF, PASS_ORDER[:1])
         for t in range(SLOTS):
             project_references(first_banks[t][:], t, 0, HALF, PASS_ORDER[1:])
-            nc.scalar.copy(b_rows[0][:, t, :], first_banks[t][:])
+            nc.scalar.copy(b_first[:, t, :], first_banks[t][:])
 
         we_codes = [kept([P, H], U32, "we_codes%d" % u) for u in range(2)]
         we_sc = [placed([P, H], U8, "we_sc%d" % u, WE_SC_AT[u]) for u in range(2)]
@@ -303,56 +305,87 @@ def tile_list_passive_radar_doppler_kernel(
                 t, c = turns[turn]
                 nc.scalar.copy(a_sb[t][:, c * CHUNK : (c + 1) * CHUNK], banks[turn][:])
 
-        for t in range(SLOTS):
-            bank = bank_tile(HALF, SLOTS + t)
-            project_references(bank[:], t, HALF, J)
-            nc.scalar.copy(b_rows[1][:, t, :], bank[:])
-
         work = placed([P, WORK_COLUMNS], F32, "work", WORK_AT)
+        b_third = [placed([P, HALF], F32, "b_third%d" % g, B_AT[1] + 4 * HALF * g)[:] for g in range(2)]
+        third_banks = [bank_tile(HALF, THIRD_BANKS[g]) for g in range(2)]
+        b_kept = {}
+        for g in range(2):
+            for k in range(2):
+                project_references(third_banks[g][:, k * QUARTER : (k + 1) * QUARTER], 2 * g + k, *PIECES[2])
+            n = 3 + g
+            b_kept[n] = bank_tile(SLOTS * UNIT, KEPT_BANKS[g])
+            for t in range(SLOTS):
+                project_references(b_kept[n][:, t * UNIT : (t + 1) * UNIT], t, *PIECES[n])
+
+        def copy_third(g):
+            nc.scalar.copy(b_third[g], third_banks[g][:])
+
+        copy_third(0)
+
         out_slices = out.rearrange("(p c) j -> p c j", c=N_SLICES)
+        h_first = work[:, FIRST_AT : FIRST_AT + SLOTS * HALF].rearrange("p (t j) -> p t j", t=SLOTS)
+        h_third = work[:, THIRD_AT : THIRD_AT + SLOTS * HALF].rearrange("p (t j) -> p t j", t=SLOTS)[:, :, 0:QUARTER]
+        cells = work[:, CELLS_AT : CELLS_AT + SLOTS * CELLS_STEP].rearrange("p (t j) -> p t j", t=SLOTS)[:, :, 0:QUARTER]
+        h_woven = [
+            work[:, WOVEN0_AT : WOVEN0_AT + HALF].bitcast(BF16),
+            work[:, WOVEN_12_AT : WOVEN_12_AT + HALF].bitcast(BF16),
+            work[:, WOVEN_12_AT : WOVEN_12_AT + HALF].bitcast(BF16),
+            work[:, WOVEN3_AT : WOVEN3_AT + QUARTER].bitcast(BF16),
+            kept([P, SLOTS * UNIT], BF16, "woven4")[:],
+        ]
 
-        def h_rows(lo, hi):
-            if lo < HALF:
-                at, step, first = FIRST_AT, HALF, 0
-            elif lo < J - UNIT:
-                at, step, first = MIDDLE_AT, MIDDLE, HALF
-            else:
-                at, step, first = LAST_AT, UNIT, J - UNIT
-            rows = work[:, at : at + SLOTS * step].rearrange("p (t j) -> p t j", t=SLOTS)
-            return rows[:, :, lo - first : hi - first]
+        def window(t, lo, hi):
+            return a_sb[t][:].indirect(offsets(idx3, lo, hi))
 
-        def woven_piece(n):
+        def gather_first(t, lo, hi):
+            nc.vector.tensor_tensor(h_first[:, t, lo:hi], window(t, lo, hi), b_first[:, t, lo:hi], MULT)
+
+        def gather_third(t):
+            b = b_third[t // 2][:, t % 2 * QUARTER : (t % 2 + 1) * QUARTER]
+            nc.vector.tensor_tensor(h_third[:, t, :], window(t, *PIECES[2]), b, MULT)
+
+        def gather_cells(t, lo, hi):
+            first = PIECES[3][0]
+            nc.vector.tensor_copy(cells[:, t, lo - first : hi - first], window(t, lo, hi))
+
+        def weave_first(n):
             lo, hi = PIECES[n]
-            in_work = {1: WOVEN1_AT, 2: WOVEN2_AT}
-            if n in in_work:
-                return work[:, in_work[n] : in_work[n] + SLOTS * (hi - lo) // 2].bitcast(BF16)
-            return placed([P, SLOTS * (hi - lo)], BF16, "h_woven%d" % n, H_WOVEN_AT + 2 * SLOTS * lo)[:]
-
-        h_woven = [woven_piece(n) for n in range(len(PIECES))]
-
-        def gather_product(t, lo, hi):
-            window = a_sb[t][:].indirect(offsets(idx3, lo, hi))
-            b = b_rows[lo // HALF][:, t, lo % HALF : lo % HALF + hi - lo]
-            nc.vector.tensor_tensor(h_rows(lo, hi)[:, t, :], window, b, MULT)
-
-        def weave_h(n, copy):
-            lo, hi = PIECES[n]
-            copy(
+            nc.scalar.copy(
                 h_woven[n].rearrange("p (c i t) -> p c t i", i=4, t=SLOTS),
-                h_rows(lo, hi).rearrange("p t (c i) -> p c t i", i=4),
+                h_first[:, :, lo:hi].rearrange("p t (c i) -> p c t i", i=4),
             )
 
-        def finish(n):
+        def weave_third():
+            nc.gpsimd.tensor_scalar(
+                h_woven[2].rearrange("p (j t) -> p j t", t=SLOTS), h_third.rearrange("p t j -> p j t"), 1.0, 0.0, MULT, ADD
+            )
+
+        def multiply_kept(n):
+            lo, hi = PIECES[n]
+            first = PIECES[3][0]
+            nc.vector.tensor_tensor(
+                h_woven[n].rearrange("p (c i t) -> p c t i", i=2, t=SLOTS),
+                cells[:, :, lo - first : hi - first].rearrange("p t (c i) -> p c t i", i=2),
+                b_kept[n][:].rearrange("p (t c i) -> p c t i", t=SLOTS, i=2),
+                MULT,
+            )
+
+        def groups_of(n):
+            lo, hi = PIECES[n]
+            return ((0, 1), (2,)) if hi - lo > UNIT else ((0,), (1,), (2,))
+
+        y_banks = {}
+
+        def project(n):
             lo, hi = PIECES[n]
             width = hi - lo
             h_codes = kept([P, width], U32, "h_codes%d" % n)
             h_sc = kept([P, width], U8, "h_sc%d" % n)
             nc.vector.quantize_mx(h_codes[:].bitcast(FP8X4), h_sc[:], h_woven[n])
-            squares = ring.tile([P, N_SLICES, width], F32, name="squares")
-            result = placed([P, N_SLICES, width], F32, "result%d" % n, RESULT_AT + 4 * N_SLICES * lo)
-            groups = ((0, 1), (2,)) if width > UNIT else ((0,), (1,), (2,))
-            for g, group in enumerate(groups):
+            y_banks[n] = []
+            for g, group in enumerate(groups_of(n)):
                 bank = bank_tile(len(group) * width, Y_BANKS[n][g])
+                y_banks[n].append(bank)
                 for k, c in enumerate(group):
                     nc.tensor.matmul_mx(
                         bank[:, k * width : (k + 1) * width],
@@ -363,9 +396,17 @@ def tile_list_passive_radar_doppler_kernel(
                         start=True,
                         stop=True,
                     )
-                nc.scalar.activation(
-                    squares[:, group[0] : group[-1] + 1, :].rearrange("p c j -> p (c j)"), bank[:], ACT.Square
-                )
+
+        def display(n):
+            lo, hi = PIECES[n]
+            width = hi - lo
+            squares = ring.tile([P, N_SLICES, width], F32, name="squares")
+            result = placed([P, N_SLICES, width], F32, "result%d" % n, RESULT_AT + 4 * N_SLICES * lo)
+            groups = groups_of(n)
+            for g, group in enumerate(groups):
+                bank = y_banks[n][g]
+                square = squares[:, group[0] : group[-1] + 1, :].rearrange("p c j -> p (c j)")
+                nc.scalar.activation(square, bank[:], ACT.Square)
                 for c in (groups[g - 1] if g else ()) + (group if g == len(groups) - 1 else ()):
                     nc.scalar.activation(result[:, c, :], squares[:, c, :], ACT.Ln, bias=noise_sb[:, c : c + 1])
             if hi < J:
@@ -375,23 +416,30 @@ def tile_list_passive_radar_doppler_kernel(
                 nc.scalar.dma_start(out_slices[:, 2, lo:hi], result[:, 2, :])
 
         for t in range(LAST):
-            gather_product(t, 0, HALF)
-        gather_product(LAST, *PIECES[0])
-        gather_product(LAST, *PIECES[1])
-        weave_h(0, nc.scalar.copy)
-        weave_h(1, nc.scalar.copy)
-        gather_product(0, HALF, J - UNIT)
-        finish(0)
-        gather_product(1, HALF, J - UNIT)
-        gather_product(2, HALF, J - UNIT)
-        gather_product(LAST, *PIECES[2])
-        finish(1)
-        weave_h(2, nc.vector.tensor_copy)
-        gather_product(LAST, *PIECES[3])
-        finish(2)
-        weave_h(3, nc.vector.tensor_copy)
-        for t in range(SLOTS):
-            gather_product(t, *PIECES[4])
-        finish(3)
-        weave_h(4, nc.vector.tensor_copy)
-        finish(4)
+            gather_first(t, 0, HALF)
+        gather_first(LAST, *PIECES[0])
+        gather_first(LAST, *PIECES[1])
+        weave_first(0)
+        copy_third(1)
+        weave_first(1)
+        gather_third(0)
+        gather_third(1)
+        project(0)
+        display(0)
+        gather_third(3)
+        gather_third(2)
+        project(1)
+        weave_third()
+        display(1)
+        for t in range(LAST):
+            gather_cells(t, J - QUARTER, J)
+        gather_cells(LAST, *PIECES[3])
+        project(2)
+        display(2)
+        multiply_kept(3)
+        gather_cells(LAST, *PIECES[4])
+        project(3)
+        display(3)
+        multiply_kept(4)
+        project(4)
+        display(4)

@@ -36,7 +36,8 @@ LAST = SLOTS - 1
 SCALAR_MORE = 256
 HALF = J // 2
 QUARTER = J // 4
-PIECES = [(0, QUARTER), (QUARTER, HALF), (HALF, J - QUARTER), (J - QUARTER, J - UNIT), (J - UNIT, J)]
+PIECES = [(0, QUARTER), (QUARTER, HALF), (HALF, J - QUARTER), (J - UNIT, J), (J - QUARTER, J - UNIT)]
+FINAL = len(PIECES) - 1
 Y_BANKS = ((0, 1), (2, 3), (4, 5), (0, 1, 2), (3, 4, 5))
 THIRD_BANKS = (4, 5)
 KEPT_BANKS = (6, 7)
@@ -66,10 +67,11 @@ THIRD_AT = 0
 WOVEN3_AT = THIRD_AT
 WOVEN0_AT = THIRD_AT + 2 * HALF
 FIRST_AT = THIRD_AT + LAST * HALF
-CELLS_AT = FIRST_AT + QUARTER + UNIT
-CELLS_STEP = HALF
-WOVEN_12_AT = CELLS_AT + LAST * CELLS_STEP + UNIT
-WORK_COLUMNS = WOVEN_12_AT + HALF
+CELLS_AT = FIRST_AT + UNIT
+CELLS_STEP = 3 * QUARTER
+WOVEN2_AT = FIRST_AT + SLOTS * HALF
+WOVEN1_AT = CELLS_AT + LAST * CELLS_STEP
+WORK_COLUMNS = CELLS_AT + SLOTS * CELLS_STEP
 
 
 def tile_list_passive_radar_doppler_kernel(
@@ -328,8 +330,8 @@ def tile_list_passive_radar_doppler_kernel(
         cells = work[:, CELLS_AT : CELLS_AT + SLOTS * CELLS_STEP].rearrange("p (t j) -> p t j", t=SLOTS)[:, :, 0:QUARTER]
         h_woven = [
             work[:, WOVEN0_AT : WOVEN0_AT + HALF].bitcast(BF16),
-            work[:, WOVEN_12_AT : WOVEN_12_AT + HALF].bitcast(BF16),
-            work[:, WOVEN_12_AT : WOVEN_12_AT + HALF].bitcast(BF16),
+            work[:, WOVEN1_AT : WOVEN1_AT + HALF].bitcast(BF16),
+            work[:, WOVEN2_AT : WOVEN2_AT + HALF].bitcast(BF16),
             work[:, WOVEN3_AT : WOVEN3_AT + QUARTER].bitcast(BF16),
             kept([P, SLOTS * UNIT], BF16, "woven4")[:],
         ]
@@ -345,7 +347,7 @@ def tile_list_passive_radar_doppler_kernel(
             nc.vector.tensor_tensor(h_third[:, t, :], window(t, *PIECES[2]), b, MULT)
 
         def gather_cells(t, lo, hi):
-            first = PIECES[3][0]
+            first = J - QUARTER
             nc.vector.tensor_copy(cells[:, t, lo - first : hi - first], window(t, lo, hi))
 
         def weave_first(n):
@@ -360,13 +362,12 @@ def tile_list_passive_radar_doppler_kernel(
                 h_woven[2].rearrange("p (j t) -> p j t", t=SLOTS), h_third.rearrange("p t j -> p j t"), 1.0, 0.0, MULT, ADD
             )
 
-        def multiply_kept(n):
-            lo, hi = PIECES[n]
-            first = PIECES[3][0]
+        def multiply_kept(n, lo, hi):
+            first = PIECES[n][0] - (J - QUARTER)
             nc.vector.tensor_tensor(
-                h_woven[n].rearrange("p (c i t) -> p c t i", i=2, t=SLOTS),
-                cells[:, :, lo - first : hi - first].rearrange("p t (c i) -> p c t i", i=2),
-                b_kept[n][:].rearrange("p (t c i) -> p c t i", t=SLOTS, i=2),
+                h_woven[n][:, SLOTS * lo : SLOTS * hi].rearrange("p (c i t) -> p c t i", i=2, t=SLOTS),
+                cells[:, :, first + lo : first + hi].rearrange("p t (c i) -> p c t i", i=2),
+                b_kept[n][:].rearrange("p (t j) -> p t j", t=SLOTS)[:, :, lo:hi].rearrange("p t (c i) -> p c t i", i=2),
                 MULT,
             )
 
@@ -381,7 +382,10 @@ def tile_list_passive_radar_doppler_kernel(
             width = hi - lo
             h_codes = kept([P, width], U32, "h_codes%d" % n)
             h_sc = kept([P, width], U8, "h_sc%d" % n)
-            nc.vector.quantize_mx(h_codes[:].bitcast(FP8X4), h_sc[:], h_woven[n])
+            step = width // 2 if n == FINAL else width
+            for at in range(0, width, step):
+                woven = h_woven[n][:, SLOTS * at : SLOTS * (at + step)]
+                nc.vector.quantize_mx(h_codes[:, at : at + step].bitcast(FP8X4), h_sc[:, at : at + step], woven)
             y_banks[n] = []
             for g, group in enumerate(groups_of(n)):
                 bank = bank_tile(len(group) * width, Y_BANKS[n][g])
@@ -409,7 +413,7 @@ def tile_list_passive_radar_doppler_kernel(
                 nc.scalar.activation(square, bank[:], ACT.Square)
                 for c in (groups[g - 1] if g else ()) + (group if g == len(groups) - 1 else ()):
                     nc.scalar.activation(result[:, c, :], squares[:, c, :], ACT.Ln, bias=noise_sb[:, c : c + 1])
-            if hi < J:
+            if n < FINAL:
                 nc.sync.dma_start(out_slices[:, :, lo:hi], result[:])
             else:
                 nc.sync.dma_start(out_slices[:, 0:2, lo:hi], result[:, 0:2, :])
@@ -431,15 +435,18 @@ def tile_list_passive_radar_doppler_kernel(
         project(1)
         weave_third()
         display(1)
-        for t in range(LAST):
+        for t in (1, 2):
             gather_cells(t, J - QUARTER, J)
-        gather_cells(LAST, *PIECES[3])
+        for t in (0, LAST):
+            gather_cells(t, *PIECES[3])
         project(2)
         display(2)
-        multiply_kept(3)
-        gather_cells(LAST, *PIECES[4])
+        multiply_kept(3, 0, UNIT)
+        for t in (0, LAST):
+            gather_cells(t, *PIECES[4])
         project(3)
         display(3)
-        multiply_kept(4)
+        multiply_kept(4, 0, UNIT // 2)
+        multiply_kept(4, UNIT // 2, UNIT)
         project(4)
         display(4)

@@ -38,7 +38,7 @@ HALF = J // 2
 QUARTER = J // 4
 PIECES = [(0, QUARTER), (QUARTER, HALF), (HALF, J - QUARTER), (J - UNIT, J), (J - QUARTER, J - UNIT)]
 FINAL = len(PIECES) - 1
-Y_BANKS = ((0, 1), (2, 3), (4, 5), (0, 1, 2), (3, 4, 5))
+Y_BANKS = ((0, 1), (2, 3), (4, 5, 0), (1, 2, 3), (4, 5, 0))
 THIRD_BANKS = (4, 5)
 KEPT_BANKS = (6, 7)
 
@@ -314,15 +314,11 @@ def tile_list_passive_radar_doppler_kernel(
         for g in range(2):
             for k in range(2):
                 project_references(third_banks[g][:, k * QUARTER : (k + 1) * QUARTER], 2 * g + k, *PIECES[2])
-            n = 3 + g
-            b_kept[n] = bank_tile(SLOTS * UNIT, KEPT_BANKS[g])
+            nc.scalar.copy(b_third[g], third_banks[g][:])
+        for n in (3, 4):
+            b_kept[n] = bank_tile(SLOTS * UNIT, KEPT_BANKS[n - 3])
             for t in range(SLOTS):
                 project_references(b_kept[n][:, t * UNIT : (t + 1) * UNIT], t, *PIECES[n])
-
-        def copy_third(g):
-            nc.scalar.copy(b_third[g], third_banks[g][:])
-
-        copy_third(0)
 
         out_slices = out.rearrange("(p c) j -> p c j", c=N_SLICES)
         h_first = work[:, FIRST_AT : FIRST_AT + SLOTS * HALF].rearrange("p (t j) -> p t j", t=SLOTS)
@@ -373,7 +369,7 @@ def tile_list_passive_radar_doppler_kernel(
 
         def groups_of(n):
             lo, hi = PIECES[n]
-            return ((0, 1), (2,)) if hi - lo > UNIT else ((0,), (1,), (2,))
+            return ((0, 1), (2,)) if hi <= HALF else ((0,), (1,), (2,))
 
         y_banks = {}
 
@@ -416,7 +412,8 @@ def tile_list_passive_radar_doppler_kernel(
             if n < FINAL:
                 nc.sync.dma_start(out_slices[:, :, lo:hi], result[:])
             else:
-                nc.sync.dma_start(out_slices[:, 0:2, lo:hi], result[:, 0:2, :])
+                for c in range(2):
+                    nc.sync.dma_start(out_slices[:, c, lo:hi], result[:, c, :])
                 nc.scalar.dma_start(out_slices[:, 2, lo:hi], result[:, 2, :])
 
         for t in range(LAST):
@@ -424,7 +421,6 @@ def tile_list_passive_radar_doppler_kernel(
         gather_first(LAST, *PIECES[0])
         gather_first(LAST, *PIECES[1])
         weave_first(0)
-        copy_third(1)
         weave_first(1)
         gather_third(0)
         gather_third(1)

@@ -412,8 +412,7 @@ def tile_list_passive_radar_doppler_kernel(
             if n < FINAL:
                 nc.sync.dma_start(out_slices[:, :, lo:hi], result[:])
             else:
-                for c in range(2):
-                    nc.sync.dma_start(out_slices[:, c, lo:hi], result[:, c, :])
+                nc.sync.dma_start(out_slices[:, 0:2, lo:hi], result[:, 0:2, :])
                 nc.scalar.dma_start(out_slices[:, 2, lo:hi], result[:, 2, :])
 
         for t in range(LAST):

@@ -397,11 +397,13 @@ def tile_list_passive_radar_doppler_kernel(
                         stop=True,
                     )
 
+        results = [placed([P, N_SLICES, QUARTER], F32, "result%d" % q, RESULT_AT + 4 * N_SLICES * QUARTER * q) for q in range(4)]
+
         def display(n):
             lo, hi = PIECES[n]
             width = hi - lo
             squares = ring.tile([P, N_SLICES, width], F32, name="squares")
-            result = placed([P, N_SLICES, width], F32, "result%d" % n, RESULT_AT + 4 * N_SLICES * lo)
+            result = results[lo // QUARTER][:, :, lo % QUARTER : lo % QUARTER + width]
             groups = groups_of(n)
             for g, group in enumerate(groups):
                 bank = y_banks[n][g]
@@ -409,11 +411,12 @@ def tile_list_passive_radar_doppler_kernel(
                 nc.scalar.activation(square, bank[:], ACT.Square)
                 for c in (groups[g - 1] if g else ()) + (group if g == len(groups) - 1 else ()):
                     nc.scalar.activation(result[:, c, :], squares[:, c, :], ACT.Ln, bias=noise_sb[:, c : c + 1])
-            if n < FINAL:
-                nc.sync.dma_start(out_slices[:, :, lo:hi], result[:])
+            if width > UNIT:
+                nc.sync.dma_start(out_slices[:, :, lo:hi], result)
             else:
                 nc.sync.dma_start(out_slices[:, 0:2, lo:hi], result[:, 0:2, :])
-                nc.scalar.dma_start(out_slices[:, 2, lo:hi], result[:, 2, :])
+            if n == FINAL:
+                nc.scalar.dma_start(out_slices[:, 2, J - QUARTER : J], results[-1][:, 2, :])
 
         for t in range(LAST):
             gather_first(t, 0, HALF)

from contextlib import ExitStack

import concourse.mybir as mybir

K, T, K2, T2, S, J, H, N = 1536, 4096, 1024, 2048, 1024, 1024, 512, 384
FLOPS = 2 * (K2 * H * T2 + K * H * J + H * N * J)

F32 = mybir.dt.float32
BF16 = mybir.dt.bfloat16
I32 = mybir.dt.int32
U32 = mybir.dt.uint32
U16 = mybir.dt.uint16
U8 = mybir.dt.uint8
FP8X4 = mybir.dt.float8_e4m3fn_x4
FP4X4 = mybir.dt.float4_e2m1fn_x4
ACT = mybir.ActivationFunctionType
MULT = mybir.AluOpType.mult
ADD = mybir.AluOpType.add

P = 128
SLOTS = 4
PASS = P * SLOTS
M_PASSES = K2 // PASS
K_PASSES = K // PASS
PLANES = M_PASSES * SLOTS
N_SLICES = N // P
BANKS = 8
CHUNK = 512
CHUNKS = T2 // CHUNK
UNIT = 128
PER_COLUMN = 16
SCALE_ROWS = 16
SCALE_ROW0 = 48
LAST = SLOTS - 1

SCALAR_MORE = 256
HALF = J // 2
QUARTER = J // 4
PIECES = [(0, QUARTER), (QUARTER, HALF), (HALF, J - QUARTER), (J - UNIT, J), (J - QUARTER, J - UNIT)]
FINAL = len(PIECES) - 1
Y_BANKS = ((0, 1), (2, 3), (4, 5, 0), (1, 2, 3), (4, 5, 0))
THIRD_BANKS = (4, 5)
KEPT_BANKS = (6, 7)

KB = 1024
PAGE_AT = [8 * KB * i for i in range(PLANES)]
XS_AT = [64 * KB + 4 * KB * i for i in range(PLANES)]
WE_RAW_AT = [96 * KB, 104 * KB]
WE_WOVEN_AT = 112 * KB
WOVEN_AT = [[120 * KB, 128 * KB], [154 * KB, 162 * KB]]
PAIRS_AT = [138 * KB, 146 * KB]
SCALE_ROWS_AT = 171 * KB
TABLE_AT = [PAGE_AT[0], PAGE_AT[2], WE_RAW_AT[0]]
PASS_ORDER = (0, 2, 1)
PICKED_AT = [XS_AT[5], WOVEN_AT[1][1]]
WE_SC_AT = [SCALE_ROWS_AT, WOVEN_AT[0][0]]
PAGE_CODES_AT = [SCALE_ROWS_AT + KB // 2, WE_WOVEN_AT]
DOP_CODES_AT = WOVEN_AT[1][0] + 6 * KB
V_SC_AT = XS_AT[0]
A_AT = [PAGE_AT[4], PAGE_AT[5], PAGE_AT[6], XS_AT[3]]
B_AT = [PAGE_AT[7], XS_AT[1]]
WORK_AT = WOVEN_AT[0][1]
RESULT_AT = TABLE_AT[0]
H_WOVEN_AT = TABLE_AT[1]

THIRD_AT = 0
WOVEN3_AT = THIRD_AT
WOVEN0_AT = THIRD_AT + 2 * HALF
FIRST_AT = THIRD_AT + LAST * HALF
CELLS_AT = FIRST_AT + UNIT
CELLS_STEP = 3 * QUARTER
WOVEN2_AT = FIRST_AT + SLOTS * HALF
WOVEN1_AT = CELLS_AT + LAST * CELLS_STEP
WORK_COLUMNS = CELLS_AT + SLOTS * CELLS_STEP


def tile_list_passive_radar_doppler_kernel(
    tc, tab_words, tab_scales, offs, xs, base, offs2, offs3, we, wr_words, wr_scales, dop, noise, out
):
    nc = tc.nc
    with ExitStack() as ctx:
        lists = ctx.enter_context(tc.tile_pool(name="lists", bufs=1))
        arena = ctx.enter_context(tc.tile_pool(name="arena", bufs=1))
        keep = ctx.enter_context(tc.tile_pool(name="keep", bufs=1))
        ring = ctx.enter_context(tc.tile_pool(name="ring", bufs=2))
        psum = ctx.enter_context(tc.psum_pool(name="psum", bufs=1))

        def placed(shape, dtype, name, at):
            return arena.tile(shape, dtype, name=name, offset=at, align_bytes=64)

        def kept(shape, dtype, name):
            return keep.tile(shape, dtype, name=name, align_bytes=64)

        def bank_tile(columns, bank):
            return psum.tile([P, columns], F32, name="bank%d" % bank)

        idx = lists.tile([P, J // PER_COLUMN], U16, name="idx")
        idx2 = lists.tile([P, S // PER_COLUMN], U16, name="idx2")
        idx3 = lists.tile([P, J // PER_COLUMN], U16, name="idx3")

        scale_end = SCALE_ROW0 + K_PASSES * SCALE_ROWS
        tab_sc = kept([P, T], U8, "tab_sc")
        wr_sc_raw = kept([P, K_PASSES * H], U8, "wr_sc_raw")
        v_sc_rows = placed([P, J], U8, "v_sc_rows", SCALE_ROWS_AT)
        nc.vector.memset(tab_sc[0:SCALE_ROW0, :].bitcast(I32), 0)
        nc.vector.memset(tab_sc[scale_end:P, :].bitcast(I32), 0)
        nc.vector.memset(wr_sc_raw[:].bitcast(I32), 0)

        warm = kept([P, 2], F32, "warm")
        nc.vector.memset(warm[:, 0:1], 1.0)
        nc.scalar.activation(warm[:, 1:2], warm[:, 0:1], ACT.Ln)

        nc.sync.dma_start(idx[:], offs)
        for a in range(K_PASSES):
            nc.sync.dma_start(tab_sc[SCALE_ROW0 + a : scale_end : K_PASSES, :].bitcast(I32), tab_scales[a].bitcast(I32))
        nc.vector.tensor_copy(v_sc_rows[:], tab_sc[:].indirect(idx[:]))

        base_planes = base.rearrange("(a p i) t -> a i p t", a=M_PASSES, i=SLOTS)
        xs_planes = xs.rearrange("(a p i) t -> a i p t", a=M_PASSES, i=SLOTS)
        dop_slots = dop.rearrange("(g t q) n -> t g q n", t=SLOTS, q=8)
        page = [placed([P, T2], F32, "page%d" % i, PAGE_AT[i]) for i in range(PLANES)]
        xs_sb = [placed([P, S], F32, "xs%d" % i, XS_AT[i]) for i in range(PLANES)]
        we_raw = [placed([P, SLOTS, H], F32, "we_raw%d" % a, WE_RAW_AT[a]) for a in range(M_PASSES)]
        dop_raw = kept([P, SLOTS, N], F32, "dop_raw")
        noise_sb = kept([P, N_SLICES], F32, "noise_sb")
        wr_raw = kept([P, K_PASSES * 2 * H], U8, "wr_raw")
        parts = [[(0, S // 4), (S // 4, S)] if i == 0 else [(0, S)] for i in range(PLANES)]
        we_after_plane = {1: 0, 2: 1}
        dop_load_after, dop_round_after, wr_load_after = 3, 4, 4
        for i in range(PLANES):
            nc.sync.dma_start(page[i][:], base_planes[i // SLOTS, i % SLOTS])
            if i == 0:
                nc.sync.dma_start(idx2[:], offs2)
            for lo, hi in parts[i]:
                nc.sync.dma_start(xs_sb[i][:, lo:hi], xs_planes[i // SLOTS, i % SLOTS][:, lo:hi])
            if i in we_after_plane:
                a = we_after_plane[i]
                rows = we[PASS * a : PASS * (a + 1), :]
                nc.sync.dma_start(we_raw[a][:], rows.rearrange("(p j) c -> p j c", j=SLOTS))
            if i == dop_load_after:
                for t in range(SLOTS):
                    nc.sync.dma_start(dop_raw[:, t, :], dop_slots[t])
            if i == wr_load_after:
                nc.sync.dma_start(
                    wr_raw[:].bitcast(I32).rearrange("p (a n) -> p a n", a=K_PASSES),
                    wr_words.bitcast(I32).rearrange("a p n -> p a n"),
                )
                for q in range(4):
                    nc.sync.dma_start(
                        wr_sc_raw[32 * q : 32 * q + 4, :].bitcast(I32).rearrange("p (a n) -> p a n", a=K_PASSES),
                        wr_scales[:, 4 * q : 4 * q + 4, :].bitcast(I32).rearrange("a r n -> r a n"),
                    )
        nc.sync.dma_start(idx3[:], offs3)
        nc.sync.dma_start(noise_sb[:], noise.rearrange("(p c) -> p c", c=N_SLICES))

        we_woven = [placed([P, SLOTS * H], BF16, "we_woven0", WE_WOVEN_AT), kept([P, SLOTS * H], BF16, "we_woven1")]
        dop_woven = kept([P, SLOTS * N], BF16, "dop_woven")
        page_sc = [kept([P, T2], U8, "page_sc%d" % a) for a in range(M_PASSES)]
        table = {}

        def offsets(tile, lo, hi):
            return tile[:, lo // PER_COLUMN : hi // PER_COLUMN]

        def page_half(half):
            return slice(half * T2 // 2, (half + 1) * T2 // 2)

        wr_w = kept([P, K_PASSES * 2 * H], U8, "wr_w")
        wr_sc = kept([P, K_PASSES * H], U8, "wr_sc")
        for dst, src in ((wr_w, wr_raw), (wr_sc, wr_sc_raw)):
            nc.gpsimd.tensor_copy(
                dst[:].bitcast(I32).rearrange("p (a t g w) -> p a t g w", a=K_PASSES, t=SLOTS, g=16),
                src[:].bitcast(I32).rearrange("p (a g t w) -> p a t g w", a=K_PASSES, t=SLOTS, g=16),
            )

        table_after_plane = {1: 0, 2: 2, 3: 1}
        pairs = [placed([P, 2, T2 // 2, 2], BF16, "pairs%d" % half, PAIRS_AT[half]) for half in range(2)]
        page_woven = [
            [placed([P, SLOTS * T2 // 2], BF16, "woven%d_%d" % (a, half), WOVEN_AT[a][half]) for half in range(2)]
            for a in range(M_PASSES)
        ]
        for i in range(PLANES):
            a, slot = divmod(i, SLOTS)
            for lo, hi in parts[i]:
                nc.vector.tensor_copy(page[i][:].indirect(offsets(idx2, lo, hi)), xs_sb[i][:, lo:hi])
            for half in range(2):
                src = page[i][:, page_half(half)]
                in_slot = page_woven[a][half][:].rearrange("p (c t) -> p c t", t=SLOTS)[:, :, slot]
                if a == 0:
                    nc.scalar.copy(pairs[half][:, slot // 2, :, slot % 2], src)
                elif half == 1:
                    nc.scalar.copy(in_slot[:, 0:SCALAR_MORE], src[:, 0:SCALAR_MORE])
                    nc.gpsimd.tensor_scalar(in_slot[:, SCALAR_MORE:], src[:, SCALAR_MORE:], 1.0, 0.0, MULT, ADD)
                else:
                    nc.scalar.copy(in_slot, src)
            if i == SLOTS - 1:
                for half in range(2):
                    nc.scalar.copy(
                        page_woven[0][half][:].bitcast(F32).rearrange("p (c u) -> p c u", u=2),
                        pairs[half][:].rearrange("p u c e -> p u (c e)").bitcast(F32).rearrange("p u c -> p c u"),
                    )
            if i == 0:
                v_sc = [placed([P, J], U8, "v_sc%d" % k, V_SC_AT + J * k) for k in range(K_PASSES)]
                for k in range(K_PASSES):
                    nc.gpsimd.memset(v_sc[k][:].bitcast(I32), 0)
            if i in we_after_plane:
                w = we_after_plane[i]
                for u in range(2):
                    nc.scalar.copy(
                        we_woven[u][:, 2 * H * w : 2 * H * (w + 1)].rearrange("p (t g q j) -> p t g q j", t=2, g=16, q=8),
                        we_raw[w][:].rearrange("p j (g t q) -> p t g q j", t=SLOTS, q=8)[:, 2 * u : 2 * u + 2],
                    )
            if i == dop_round_after:
                nc.scalar.copy(
                    dop_woven[:].rearrange("p (c m t) -> p c m t", c=N_SLICES, t=SLOTS),
                    dop_raw[:].rearrange("p t (m c) -> p c m t", c=N_SLICES),
                )
            if i in table_after_plane:
                k = table_after_plane[i]
                table[k] = placed([P, T], I32, "table%d" % k, TABLE_AT[k])
                nc.sync.dma_start(table[k][:], tab_words[k].rearrange("p t i -> p (t i)").bitcast(I32))
            if i == SLOTS - 1:
                for k in range(K_PASSES):
                    for q in range(4):
                        row = SCALE_ROW0 + K_PASSES * 4 * q + k
                        nc.sync.dma_start(
                            v_sc[k][32 * q : 32 * q + 4, :].bitcast(I32),
                            v_sc_rows[row : row + K_PASSES * 4 : K_PASSES, :].bitcast(I32),
                        )

        v_words = []

        def gather_table(part):
            words = placed([P, K_PASSES, HALF], U32, "v_words%d" % part, PICKED_AT[part])
            v_words.append(words)
            for a in PASS_ORDER:
                window = table[a][:].bitcast(U32).indirect(offsets(idx, part * HALF, (part + 1) * HALF))
                nc.vector.tensor_copy(words[:, a, :], window)

        def project_references(bank, t, lo, hi, passes=PASS_ORDER):
            for a in passes:
                col = H * a + P * t
                nc.tensor.matmul_mx(
                    bank,
                    lhsT=wr_w[:, 2 * col : 2 * (col + P)].bitcast(FP4X4),
                    lhsT_scale=wr_sc[:, col : col + P],
                    rhs=v_words[lo // HALF][:, a, lo % HALF : lo % HALF + hi - lo].bitcast(FP8X4),
                    rhs_scale=v_sc[a][:, lo:hi],
                    start=(a == PASS_ORDER[0]),
                    stop=(a == PASS_ORDER[-1]),
                )

        gather_table(0)
        b_first = placed([P, SLOTS, HALF], F32, "b_first", B_AT[0])
        first_banks = [bank_tile(HALF, t) for t in range(SLOTS)]
        for t in range(SLOTS):
            project_references(first_banks[t][:], t, 0, HALF, PASS_ORDER[:1])
        for t in range(SLOTS):
            project_references(first_banks[t][:], t, 0, HALF, PASS_ORDER[1:])
            nc.scalar.copy(b_first[:, t, :], first_banks[t][:])

        we_codes = [kept([P, H], U32, "we_codes%d" % u) for u in range(2)]
        we_sc = [placed([P, H], U8, "we_sc%d" % u, WE_SC_AT[u]) for u in range(2)]
        nc.vector.quantize_mx(we_codes[0][:].bitcast(FP8X4), we_sc[0][:], we_woven[0][:])
        page_codes = [placed([P, T2], U32, "page_codes%d" % a, PAGE_CODES_AT[a]) for a in range(M_PASSES)]

        def quantise_page(a, first, chunks):
            cols = slice(first * CHUNK, (first + chunks) * CHUNK)
            at = SLOTS * CHUNK * (first % 2)
            woven = page_woven[a][first // 2][:, at : at + SLOTS * CHUNK * chunks]
            nc.vector.quantize_mx(page_codes[a][:, cols].bitcast(FP8X4), page_sc[a][:, cols], woven)

        quantise_page(0, 0, 2)
        quantise_page(1, 0, 1)
        quantise_page(1, 1, 1)
        nc.vector.quantize_mx(we_codes[1][:].bitcast(FP8X4), we_sc[1][:], we_woven[1][:])
        quantise_page(0, 2, 2)
        quantise_page(1, 2, 2)
        dop_codes = placed([P, N], U32, "dop_codes", DOP_CODES_AT)
        dop_sc = kept([P, N], U8, "dop_sc")
        nc.vector.quantize_mx(dop_codes[:].bitcast(FP8X4), dop_sc[:], dop_woven[:])
        gather_table(1)

        a_sb = [placed([P, T2], F32, "a%d" % t, A_AT[t]) for t in range(SLOTS)]
        turns = [(t, c) for c in range(2) for t in range(2)] + [(2, c) for c in range(2)]
        second_half = len(turns)
        turns = turns + [(t, c) for t in range(LAST) for c in range(2, CHUNKS)] + [(LAST, c) for c in range(CHUNKS)]
        ahead = {0: 2, second_half: 4}
        inside = [n + k for n, length in ahead.items() for k in range(1, length)]
        runs = [range(n, n + ahead.get(n, 1)) for n in range(len(turns)) if n not in inside]
        for run in runs:
            banks = {turn: bank_tile(CHUNK, (SLOTS + turn) % BANKS) for turn in run}
            for a in range(M_PASSES):
                for turn in run:
                    t, c = turns[turn]
                    cols = slice(c * CHUNK, (c + 1) * CHUNK)
                    we_cols = slice(P * (2 * a + t % 2), P * (2 * a + t % 2 + 1))
                    nc.tensor.matmul_mx(
                        banks[turn][:],
                        lhsT=we_codes[t // 2][:, we_cols].bitcast(FP8X4),
                        lhsT_scale=we_sc[t // 2][:, we_cols],
                        rhs=page_codes[a][:, cols].bitcast(FP8X4),
                        rhs_scale=page_sc[a][:, cols],
                        start=(a == 0),
                        stop=(a == M_PASSES - 1),
                    )
            for turn in run:
                t, c = turns[turn]
                nc.scalar.copy(a_sb[t][:, c * CHUNK : (c + 1) * CHUNK], banks[turn][:])

        work = placed([P, WORK_COLUMNS], F32, "work", WORK_AT)
        b_third = [placed([P, HALF], F32, "b_third%d" % g, B_AT[1] + 4 * HALF * g)[:] for g in range(2)]
        third_banks = [bank_tile(HALF, THIRD_BANKS[g]) for g in range(2)]
        b_kept = {}
        for g in range(2):
            for k in range(2):
                project_references(third_banks[g][:, k * QUARTER : (k + 1) * QUARTER], 2 * g + k, *PIECES[2])
            nc.scalar.copy(b_third[g], third_banks[g][:])
        for n in (3, 4):
            b_kept[n] = bank_tile(SLOTS * UNIT, KEPT_BANKS[n - 3])
            for t in range(SLOTS):
                project_references(b_kept[n][:, t * UNIT : (t + 1) * UNIT], t, *PIECES[n])

        out_slices = out.rearrange("(p c) j -> p c j", c=N_SLICES)
        h_first = work[:, FIRST_AT : FIRST_AT + SLOTS * HALF].rearrange("p (t j) -> p t j", t=SLOTS)
        h_third = work[:, THIRD_AT : THIRD_AT + SLOTS * HALF].rearrange("p (t j) -> p t j", t=SLOTS)[:, :, 0:QUARTER]
        cells = work[:, CELLS_AT : CELLS_AT + SLOTS * CELLS_STEP].rearrange("p (t j) -> p t j", t=SLOTS)[:, :, 0:QUARTER]
        h_woven = [
            work[:, WOVEN0_AT : WOVEN0_AT + HALF].bitcast(BF16),
            work[:, WOVEN1_AT : WOVEN1_AT + HALF].bitcast(BF16),
            work[:, WOVEN2_AT : WOVEN2_AT + HALF].bitcast(BF16),
            work[:, WOVEN3_AT : WOVEN3_AT + QUARTER].bitcast(BF16),
            kept([P, SLOTS * UNIT], BF16, "woven4")[:],
        ]

        def window(t, lo, hi):
            return a_sb[t][:].indirect(offsets(idx3, lo, hi))

        def gather_first(t, lo, hi):
            nc.vector.tensor_tensor(h_first[:, t, lo:hi], window(t, lo, hi), b_first[:, t, lo:hi], MULT)

        def gather_third(t):
            b = b_third[t // 2][:, t % 2 * QUARTER : (t % 2 + 1) * QUARTER]
            nc.vector.tensor_tensor(h_third[:, t, :], window(t, *PIECES[2]), b, MULT)

        def gather_cells(t, lo, hi):
            first = J - QUARTER
            nc.vector.tensor_copy(cells[:, t, lo - first : hi - first], window(t, lo, hi))

        def weave_first(n):
            lo, hi = PIECES[n]
            nc.scalar.copy(
                h_woven[n].rearrange("p (c i t) -> p c t i", i=4, t=SLOTS),
                h_first[:, :, lo:hi].rearrange("p t (c i) -> p c t i", i=4),
            )

        def weave_third():
            nc.gpsimd.tensor_scalar(
                h_woven[2].rearrange("p (j t) -> p j t", t=SLOTS), h_third.rearrange("p t j -> p j t"), 1.0, 0.0, MULT, ADD
            )

        def multiply_kept(n, lo, hi):
            first = PIECES[n][0] - (J - QUARTER)
            nc.vector.tensor_tensor(
                h_woven[n][:, SLOTS * lo : SLOTS * hi].rearrange("p (c i t) -> p c t i", i=2, t=SLOTS),
                cells[:, :, first + lo : first + hi].rearrange("p t (c i) -> p c t i", i=2),
                b_kept[n][:].rearrange("p (t j) -> p t j", t=SLOTS)[:, :, lo:hi].rearrange("p t (c i) -> p c t i", i=2),
                MULT,
            )

        def groups_of(n):
            lo, hi = PIECES[n]
            return ((0, 1), (2,)) if hi <= HALF else ((0,), (1,), (2,))

        y_banks = {}

        def project(n):
            lo, hi = PIECES[n]
            width = hi - lo
            h_codes = kept([P, width], U32, "h_codes%d" % n)
            h_sc = kept([P, width], U8, "h_sc%d" % n)
            step = width // 2 if n == FINAL else width
            for at in range(0, width, step):
                woven = h_woven[n][:, SLOTS * at : SLOTS * (at + step)]
                nc.vector.quantize_mx(h_codes[:, at : at + step].bitcast(FP8X4), h_sc[:, at : at + step], woven)
            y_banks[n] = []
            for g, group in enumerate(groups_of(n)):
                bank = bank_tile(len(group) * width, Y_BANKS[n][g])
                y_banks[n].append(bank)
                for k, c in enumerate(group):
                    nc.tensor.matmul_mx(
                        bank[:, k * width : (k + 1) * width],
                        lhsT=dop_codes[:, c * P : (c + 1) * P].bitcast(FP8X4),
                        lhsT_scale=dop_sc[:, c * P : (c + 1) * P],
                        rhs=h_codes[:].bitcast(FP8X4),
                        rhs_scale=h_sc[:],
                        start=True,
                        stop=True,
                    )

        results = [placed([P, N_SLICES, QUARTER], F32, "result%d" % q, RESULT_AT + 4 * N_SLICES * QUARTER * q) for q in range(4)]

        def display(n):
            lo, hi = PIECES[n]
            width = hi - lo
            squares = ring.tile([P, N_SLICES, width], F32, name="squares")
            result = results[lo // QUARTER][:, :, lo % QUARTER : lo % QUARTER + width]
            groups = groups_of(n)
            for g, group in enumerate(groups):
                bank = y_banks[n][g]
                square = squares[:, group[0] : group[-1] + 1, :].rearrange("p c j -> p (c j)")
                nc.scalar.activation(square, bank[:], ACT.Square)
                for c in (groups[g - 1] if g else ()) + (group if g == len(groups) - 1 else ()):
                    nc.scalar.activation(result[:, c, :], squares[:, c, :], ACT.Ln, bias=noise_sb[:, c : c + 1])
            if width > UNIT:
                nc.sync.dma_start(out_slices[:, :, lo:hi], result)
            else:
                nc.sync.dma_start(out_slices[:, 0:2, lo:hi], result[:, 0:2, :])
            if n == FINAL:
                nc.scalar.dma_start(out_slices[:, 2, J - QUARTER : J], results[-1][:, 2, :])

        for t in range(LAST):
            gather_first(t, 0, HALF)
        gather_first(LAST, *PIECES[0])
        gather_first(LAST, *PIECES[1])
        weave_first(0)
        weave_first(1)
        gather_third(0)
        gather_third(1)
        project(0)
        display(0)
        gather_third(3)
        gather_third(2)
        project(1)
        weave_third()
        display(1)
        for t in (1, 2):
            gather_cells(t, J - QUARTER, J)
        for t in (0, LAST):
            gather_cells(t, *PIECES[3])
        project(2)
        display(2)
        multiply_kept(3, 0, UNIT)
        for t in (0, LAST):
            gather_cells(t, *PIECES[4])
        project(3)
        display(3)
        multiply_kept(4, 0, UNIT // 2)
        multiply_kept(4, UNIT // 2, UNIT)
        project(4)
        display(4)
